import numpy as np
import ml_dtypes


def mxq(x, axis, fmt="e4m3"):
    dtype, down = {"e4m3": (ml_dtypes.float8_e4m3fn, 7), "e5m2": (ml_dtypes.float8_e5m2, 14)}[fmt]
    v = np.moveaxis(np.asarray(x, np.float32).astype(ml_dtypes.bfloat16).astype(np.float64), axis, -1)
    blocks = v.reshape(v.shape[:-1] + (-1, 32))
    amax = np.abs(blocks).max(-1, keepdims=True)
    byte = np.maximum(np.where(amax > 0, np.frexp(amax)[1] - 1 + 127, 0) - down, 1)
    scale = np.exp2(byte - 127.0)
    codes = (blocks / scale).astype(np.float32).astype(dtype).astype(np.float64)
    return np.moveaxis((codes * scale).reshape(v.shape), -1, axis)


WIDE = False


def mx_kscale(k):
    if not WIDE:
        return np.ones(k)
    levels = np.array([24, -24, 12, -12, 0])
    if k % 512:
        return np.exp2(np.random.permutation(np.resize(levels, k // 32))).repeat(32)
    a = np.empty((k // 512, 16))
    for p in range(k // 512):
        a[p, :8] = np.random.permutation(np.resize(levels, 8))
        for g in range(8):
            far = levels[np.abs(levels - a[p, g]) >= 10]
            a[p, g + 8] = far[np.random.randint(len(far))]
    return np.exp2(a.ravel()).repeat(32)


def f64(x):
    return np.asarray(x).astype(np.float64)


def striped(idx):
    return np.tile(idx.reshape(-1, 16).T, (8, 1)).astype(np.uint16)


def unstriped(offs):
    return offs[:16].T.reshape(-1).astype(np.int64)


E2M1 = np.array([0.0, 0.5, 1.0, 1.5, 2.0, 3.0, 4.0, 6.0, -0.0, -0.5, -1.0, -1.5, -2.0, -3.0, -4.0, -6.0])


def pack_weight(w, fmt):
    k, n = w.shape
    w = f64(np.asarray(w, np.float32).astype(ml_dtypes.bfloat16)).reshape(k // 32, 32, n)
    amax = np.abs(w).max(1)
    if fmt == "e4m3":
        byte = np.frexp(amax)[1] - 1 + 127 - 7
    else:
        mant, ex = np.frexp(amax / 6.0)
        byte = np.where(mant > 0.5, ex, ex - 1) + 127
    byte = np.clip(np.where(amax > 0, byte, 1), 1, 254)
    scaled = (w * np.exp2(127.0 - byte)[:, None, :]).reshape(k, n).astype(np.float32)
    by_word = np.ascontiguousarray(scaled.reshape(k // 512, 128, 4, n).transpose(0, 1, 3, 2))
    if fmt == "e4m3":
        words = by_word.astype(ml_dtypes.float8_e4m3fn).view(np.uint8)
    else:
        c = by_word.astype(ml_dtypes.float4_e2m1fn).view(np.uint8) & 0xF
        words = (c[..., 0::2] | (c[..., 1::2] << 4)).reshape(k // 512, 128, 2 * n)
    return np.ascontiguousarray(words), np.ascontiguousarray(byte.astype(np.uint8).reshape(k // 512, 16, n))


def unpack_weight(words, scales, fmt):
    g, _, n = scales.shape
    words = np.ascontiguousarray(words).reshape(g, 128, n, -1)
    if fmt == "e4m3":
        vals = words.view(ml_dtypes.float8_e4m3fn).astype(np.float64)
    else:
        nib = np.empty((g, 128, n, 4), np.uint8)
        nib[..., 0::2] = words & 0xF
        nib[..., 1::2] = words >> 4
        vals = E2M1[nib]
    vals = vals * np.repeat(np.exp2(scales.astype(np.float64) - 127.0), 8, axis=1)[..., None]
    return vals.transpose(0, 1, 3, 2).reshape(g * 512, n)


def pack_table4(v):
    words, scales = pack_weight(v, "e2m1")
    g, t = words.shape[0] // 2, v.shape[1]
    return np.ascontiguousarray(words.reshape(g, 2, 128, t, 2).transpose(0, 2, 3, 1, 4).reshape(g, 128, t, 4)), scales


def unpack_table4(words, scales):
    g, _, t, _ = words.shape
    return unpack_weight(words.reshape(g, 128, t, 2, 2).transpose(0, 3, 1, 2, 4).reshape(2 * g, 128, 2 * t), scales, "e2m1")


def planes(y):
    n, m = y.shape
    v = y.astype(np.float32).astype(ml_dtypes.bfloat16).astype(np.float64).reshape(n // 32, 32, m)
    top = np.abs(v).max(1)
    byte = np.clip(np.where(top > 0, np.frexp(top)[1] - 1 + 127 - 7, 1), 1, 254)
    codes = (v * np.exp2(127.0 - byte)[:, None, :]).reshape(n, m).astype(np.float32).astype(ml_dtypes.float8_e4m3fn).view(np.uint8)
    words = codes.reshape(n // 512, 128, 4, m).transpose(0, 1, 3, 2)
    return np.ascontiguousarray(words), np.ascontiguousarray(byte.astype(np.uint8).reshape(n // 512, 16, m))


K, R, N, T, J = 1024, 512, 512, 2048, 1024


def setup_inputs():
    n = np.random.standard_normal
    s = mx_kscale(K)[:, None]
    u = mx_kscale(R)[:, None]
    wd = n((R, N)) / np.sqrt(R) / u
    wd4 = pack_weight(wd, "e2m1")
    wdrest = wd - unpack_weight(*wd4, "e2m1")
    p_tab = pack_table4(n((K, T)) * s)
    p_ws = pack_weight(n((K, R)) / np.sqrt(2 * K) / s, "e2m1")
    p_wt = pack_weight(n((K, R)) / np.sqrt(2 * K) / s, "e2m1")
    p_wd8 = pack_weight(wdrest, "e4m3")
    return {
        "tab_words": p_tab[0],
        "tab_scales": p_tab[1],
        "ws_words": p_ws[0],
        "ws_scales": p_ws[1],
        "wt_words": p_wt[0],
        "wt_scales": p_wt[1],
        "sm": (np.random.uniform(0.5, 2.0, R) * u[:, 0]).astype(np.float32),
        "wd4_words": wd4[0],
        "wd4_scales": wd4[1],
        "wd8_words": p_wd8[0],
        "wd8_scales": p_wd8[1],
        "gT": (n((N, T))).astype(np.float32),
        "wgo": np.tile(np.random.uniform(0.5, 2.0, J), (128, 1)).astype(np.float32),
        "offs": striped(np.random.permutation(T)[:J]),
        "offs2": striped(np.random.permutation(T)[:J]),
    }


def reference(tab_words, tab_scales, ws_words, ws_scales, wt_words, wt_scales, sm, wd4_words, wd4_scales, wd8_words, wd8_scales, gT, wgo, offs, offs2):
    idx = unstriped(offs)
    idx2 = unstriped(offs2)
    tab_ = unpack_table4(tab_words, tab_scales)[:, idx]
    tabb_ = unpack_table4(tab_words, tab_scales)[:, idx2]
    ws_ = unpack_weight(ws_words, ws_scales, "e2m1")
    wt_ = unpack_weight(wt_words, wt_scales, "e2m1")
    a = ws_.T @ tab_ + wt_.T @ tabb_
    h = f64(sm)[:, None] * np.tanh(a)
    h_ = mxq(h, 0, "e4m3")
    wd4_ = unpack_weight(wd4_words, wd4_scales, "e2m1")
    wd8_ = unpack_weight(wd8_words, wd8_scales, "e4m3")
    y = wd4_.T @ h_ + wd8_.T @ h_
    out = np.zeros((N, T))
    out[:, idx2] = f64(wgo)[0] * (y * f64(gT)[:, idx])
    return (out,) + planes(out)

@@ -1,0 +1,239 @@
+from contextlib import ExitStack
+
+import concourse.mybir as mybir
+from concourse.masks import make_identity
+
+K, R, N, T, J = 1024, 512, 512, 2048, 1024
+FLOPS = 2 * (2 * K * R * J + 2 * R * N * J)
+
+F32 = mybir.dt.float32
+BF16 = mybir.dt.bfloat16
+I32 = mybir.dt.int32
+U32 = mybir.dt.uint32
+U16 = mybir.dt.uint16
+U8 = mybir.dt.uint8
+FP8X4 = mybir.dt.float8_e4m3fn_x4
+FP4X4 = mybir.dt.float4_e2m1fn_x4
+COPY = mybir.ActivationFunctionType.Copy
+TANH = mybir.ActivationFunctionType.Tanh
+MULT = mybir.AluOpType.mult
+
+P = 128
+HALF = J // 2
+QUARTER = J // 4
+CHUNK = 512
+
+
+def tile_list_msg_tanh_res_gateP_kernel(
+    tc, tab_words, tab_scales, ws_words, ws_scales, wt_words, wt_scales, sm,
+    wd4_words, wd4_scales, wd8_words, wd8_scales, gT, wgo, offs, offs2,
+    out_0, out_1, out_2,
+):
+    nc = tc.nc
+    with ExitStack() as ctx:
+        keep = ctx.enter_context(tc.tile_pool(name="keep", bufs=1))
+        ring = ctx.enter_context(tc.tile_pool(name="ring", bufs=3))
+        psum = ctx.enter_context(tc.psum_pool(name="psum", bufs=2))
+
+        lists = [keep.tile([P, J // 16], U16, name=f"list{l}") for l in range(2)]
+        tab_w = keep.tile([P, T], I32, name="tab_w", tag="slot2")
+        tab_s = keep.tile([P, T], U8, name="tab_s", tag="slot1")
+        w_s = keep.tile([P, 6 * R], U8, name="w_s", align_bytes=64)
+        shifted = [keep.tile([P, 2 * HALF], U8, name=f"shifted{h}", align_bytes=64) for h in range(2)]
+
+        nc.gpsimd.memset(tab_s[:].bitcast(I32), 0)
+        nc.vector.memset(w_s[:].bitcast(I32), 0)
+        for h in range(2):
+            nc.vector.memset(shifted[h][:].bitcast(I32), 0)
+
+        nc.sync.dma_start(lists[0][:], offs)
+        tab_s_rows = tab_scales.bitcast(I32).rearrange("a (q r) t -> r q a t", r=4)
+        for r in range(4):
+            nc.sync.dma_start(tab_s[:].bitcast(I32)[r:P:16, :], tab_s_rows[r])
+        nc.sync.dma_start(tab_w[:], tab_words[0].rearrange("p t b -> p (t b)").bitcast(I32))
+        nc.sync.dma_start(lists[1][:], offs2)
+        w_s32 = w_s[:].bitcast(I32)
+        col = 0
+        for sc in (ws_scales, wt_scales, wd4_scales, wd8_scales):
+            n_pass = sc.shape[0]
+            width = n_pass * R // 4
+            nc.sync.dma_start(
+                w_s32[0:16, col : col + width].rearrange("q (a n) -> q a n", a=n_pass),
+                sc.bitcast(I32).rearrange("a q n -> q a n"),
+            )
+            col = col + width
+        w1 = [keep.tile([P, 2 * 2 * R], U8, name=f"w1_{l}", align_bytes=64) for l in range(2)]
+        for l, words in enumerate((ws_words, wt_words)):
+            nc.sync.dma_start(
+                w1[l][:].bitcast(I32).rearrange("p (a n) -> p a n", a=2),
+                words.bitcast(I32).rearrange("a p n -> p a n"),
+            )
+        for q in range(1, 4):
+            nc.sync.dma_start(w_s32[32 * q : 32 * q + 4, :], w_s32[4 * q : 4 * q + 4, :])
+        sm_t = keep.tile([P, 4], F32, name="sm_t")
+        nc.sync.dma_start(sm_t[:], sm.rearrange("(p t) -> p t", t=4))
+        wgo_rows = keep.tile([P, P], F32, name="wgo_rows")
+        nc.gpsimd.memset(wgo_rows[:], 0.0)
+        nc.sync.dma_start(wgo_rows[0 : J // P, :], wgo[0:1, :].rearrange("o (b p) -> (o b) p", p=P))
+        ident = keep.tile([P, P], F32, name="ident")
+        make_identity(nc, ident[:])
+        pages = [keep.tile([P, T], F32, name=f"page{t}") for t in range(4)]
+        for t in range(4):
+            for c in range(T // CHUNK):
+                nc.gpsimd.memset(pages[t][:, c * CHUNK : (c + 1) * CHUNK], 0.0)
+        wd4 = keep.tile([P, 2 * N], U8, name="wd4", align_bytes=64)
+        nc.sync.dma_start(wd4[:].bitcast(I32), wd4_words[0].bitcast(I32))
+        wd8 = keep.tile([P, N], I32, name="wd8", align_bytes=64)
+        nc.sync.dma_start(wd8[:], wd8_words[0].rearrange("p n i -> p (n i)").bitcast(I32))
+
+        wgo_bank = psum.tile([P, 4, P], F32, name="y_turned", tag="y_turned")
+        nc.tensor.transpose(wgo_bank[:, 0, :], wgo_rows[:], ident[:])
+        wgo_cols = keep.tile([P, J // P], F32, name="wgo_cols")
+        nc.scalar.copy(wgo_cols[:], wgo_bank[:, 0, 0 : J // P])
+
+        def half_of(l, h):
+            return lists[l][:, h * (HALF // 16) : (h + 1) * (HALF // 16)]
+
+        picked_s, parted = [], []
+        for h in range(2):
+            ps = keep.tile([P, 2 * HALF], U8, name=f"picked_s{h}", align_bytes=64)
+            for l in range(2):
+                nc.vector.tensor_copy(ps[:, l * HALF : (l + 1) * HALF], tab_s[:].indirect(half_of(l, h)))
+            nc.sync.dma_start(shifted[h][:].bitcast(I32)[0 : P - 16, :], ps[:].bitcast(I32)[16:P, :])
+            pw = keep.tile([P, 2 * HALF], U32, name=f"picked_w{h}", tag=f"slot{3 * h}")
+            for l in range(2):
+                nc.vector.tensor_copy(pw[:, l * HALF : (l + 1) * HALF], tab_w[:].bitcast(U32).indirect(half_of(l, h)))
+            pt = keep.tile([P, 2 * 2 * 2 * HALF], U8, name=f"parted{h}", align_bytes=64)
+            for l in range(2):
+                nc.vector.tensor_copy(
+                    pt[:].bitcast(U16)[:, 2 * l * HALF : 2 * (l + 1) * HALF].rearrange("p (a j) -> p a j", a=2),
+                    pw[:, l * HALF : (l + 1) * HALF].bitcast(U16).rearrange("p (j a) -> p a j", a=2),
+                )
+            picked_s.append(ps)
+            parted.append(pt)
+
+        gates = [keep.tile([P, T], F32, name=f"gates{t}", tag=f"slot{t}") for t in range(4)]
+        gT_rows = gT.rearrange("(p t) c -> t p c", t=4)
+        for t in range(4):
+            nc.sync.dma_start(gates[t][:], gT_rows[t])
+
+        y = [keep.tile([P, 4, HALF], F32, name=f"y{h}") for h in range(2)]
+
+        def first_stage(b, h_rows):
+            h, j0 = divmod(b * P, HALF)
+            a_bank = psum.tile([P, R], F32, name="a_bank")
+            steps = [(l, a) for a in range(2) for l in range(2)]
+            for i, (l, a) in enumerate(steps):
+                c0 = (2 * l + a) * HALF + j0
+                scales = (picked_s, shifted)[a][h]
+                nc.tensor.matmul_mx(
+                    a_bank[:],
+                    lhsT=parted[h][:, 2 * c0 : 2 * (c0 + P)].bitcast(FP4X4),
+                    lhsT_scale=scales[:, l * HALF + j0 : l * HALF + j0 + P],
+                    rhs=w1[l][:, 2 * a * R : 2 * (a + 1) * R].bitcast(FP4X4),
+                    rhs_scale=w_s[:, (2 * l + a) * R : (2 * l + a + 1) * R],
+                    start=(i == 0),
+                    stop=(i == len(steps) - 1),
+                )
+            th = ring.tile([P, 4, P], F32, name="th")
+            nc.scalar.activation(th[:], a_bank[:].rearrange("p (m t) -> p t m", t=4), TANH)
+            h_bank = psum.tile([P, 4, P], F32, name="h_bank")
+            for t in range(4):
+                nc.tensor.transpose(h_bank[:, t, :], th[:, t, :], ident[:])
+            c = (b % 2) * P
+            for t in range(4):
+                nc.scalar.activation(h_rows[:, t, c : c + P], h_bank[:, t, :], COPY, scale=sm_t[:, t : t + 1])
+
+        def second_stage(b, h_codes, h_scales):
+            h, j0 = divmod(b * P, HALF)
+            c = (b % 2) * P
+            y_bank = psum.tile([P, N], F32, name="y_bank")
+            for i, (w, fmt) in enumerate(((wd4, FP4X4), (wd8, FP8X4))):
+                nc.tensor.matmul_mx(
+                    y_bank[:],
+                    lhsT=h_codes[:, c : c + P].bitcast(FP8X4),
+                    lhsT_scale=h_scales[:, c : c + P],
+                    rhs=w[:].bitcast(fmt),
+                    rhs_scale=w_s[:, (4 + i) * N : (5 + i) * N],
+                    start=(i == 0),
+                    stop=(i == 1),
+                )
+            yw = ring.tile([P, 4, P], F32, name="yw")
+            nc.scalar.activation(
+                yw[:], y_bank[:].rearrange("p (m t) -> p t m", t=4), COPY, scale=wgo_cols[:, b : b + 1]
+            )
+            y_turned = psum.tile([P, 4, P], F32, name="y_turned", tag="y_turned")
+            for t in range(4):
+                nc.tensor.transpose(y_turned[:, t, :], yw[:, t, :], ident[:])
+            nc.scalar.copy(y[h][:, :, j0 : j0 + P], y_turned[:])
+
+        h_codes, h_scales = [], []
+
+        def hidden(q):
+            h_rows = ring.tile([P, 4, QUARTER], BF16, name="h_rows")
+            for b in (2 * q, 2 * q + 1):
+                first_stage(b, h_rows)
+            h_woven = keep.tile([P, 4 * QUARTER], BF16, name=f"h_woven{q}", align_bytes=64)
+            nc.scalar.copy(
+                h_woven[:].rearrange("p (c i t) -> p c t i", i=4, t=4),
+                h_rows[:].rearrange("p t (c i) -> p c t i", i=4),
+            )
+            h_codes.append(keep.tile([P, QUARTER], U32, name=f"h_codes{q}", align_bytes=64))
+            h_scales.append(keep.tile([P, QUARTER], U8, name=f"h_scales{q}", align_bytes=64))
+            nc.vector.quantize_mx(h_codes[q][:].bitcast(FP8X4), h_scales[q][:], h_woven[:])
+
+        def message(q):
+            for b in (2 * q, 2 * q + 1):
+                second_stage(b, h_codes[q], h_scales[q])
+
+        hidden(0)
+        hidden(1)
+        message(0)
+        hidden(2)
+        hidden(3)
+        for q in (1, 2, 3):
+            message(q)
+
+        def piece_of(l, j0, n):
+            return lists[l][:, j0 // 16 : (j0 + n) // 16]
+
+        groups = [
+            (0, QUARTER, (0, 1, 2, 3), "g_first"),
+            (QUARTER, QUARTER, (0, 1, 2, 3), "g_second"),
+            (HALF, HALF, (0, 1, 2, 3), "g_last"),
+        ]
+        g = []
+        for i, (j0, n, rows, tag) in enumerate(groups):
+            picked = keep.tile([P, len(rows), n], F32, name=f"g{i}", tag=tag, align_bytes=64)
+            for k, t in enumerate(rows):
+                nc.vector.tensor_copy(picked[:, k, :], gates[t][:].indirect(piece_of(0, j0, n)))
+            g.append(picked)
+
+        out_rows = out_0.rearrange("(p t) c -> t p c", t=4)
+        pairs = [keep.tile([P, 2, CHUNK, 2], BF16, name=f"pairs{c}") for c in range(T // CHUNK)]
+        for i, (j0, n, rows, tag) in enumerate(groups):
+            h, c0 = divmod(j0, HALF)
+            for k, t in enumerate(rows):
+                nc.vector.tensor_tensor(
+                    pages[t][:].indirect(piece_of(1, j0, n)), y[h][:, t, c0 : c0 + n], g[i][:, k, :], MULT
+                )
+                if h == 1:
+                    nc.sync.dma_start(out_rows[t], pages[t][:])
+                    for c in range(T // CHUNK):
+                        nc.scalar.copy(pairs[c][:, t // 2, :, t % 2], pages[t][:, c * CHUNK : (c + 1) * CHUNK])
+
+        o_scales = keep.tile([P, T], U8, name="o_scales", align_bytes=64)
+        out_words = out_1[0].rearrange("p t i -> p (t i)").bitcast(I32)
+        woven = [keep.tile([P, 4 * CHUNK], BF16, name=f"woven{c}", align_bytes=64) for c in range(T // CHUNK)]
+        for c in range(T // CHUNK):
+            nc.vector.tensor_copy(
+                woven[c][:].bitcast(I32).rearrange("p (j u) -> p j u", u=2),
+                pairs[c][:].rearrange("p u j e -> p u (j e)").bitcast(I32).rearrange("p u j -> p j u"),
+            )
+            o_codes = keep.tile([P, CHUNK], I32, name=f"o_codes{c}", align_bytes=64)
+            nc.vector.quantize_mx(o_codes[:].bitcast(FP8X4), o_scales[:, c * CHUNK : (c + 1) * CHUNK], woven[c][:])
+            nc.sync.dma_start(out_words[:, c * CHUNK : (c + 1) * CHUNK], o_codes[:])
+        out_scales = out_2[0].bitcast(I32)
+        for q in range(4):
+            queue = (nc.sync, nc.scalar)[q % 2]
+            queue.dma_start(out_scales[4 * q : 4 * q + 4, :], o_scales[:].bitcast(I32)[32 * q : 32 * q + 4, :])

@@ -22,6 +22,8 @@ P = 128
 HALF = J // 2
 QUARTER = J // 4
 CHUNK = 512
+PIECE = 256
+VECTOR_PIECES = 5
 
 
 def tile_list_msg_tanh_res_gateP_kernel(
@@ -33,60 +35,67 @@ def tile_list_msg_tanh_res_gateP_kernel(
     with ExitStack() as ctx:
         keep = ctx.enter_context(tc.tile_pool(name="keep", bufs=1))
         ring = ctx.enter_context(tc.tile_pool(name="ring", bufs=3))
-        psum = ctx.enter_context(tc.psum_pool(name="psum", bufs=2))
+        psum = ctx.enter_context(tc.psum_pool(name="psum", bufs=1))
 
         lists = [keep.tile([P, J // 16], U16, name=f"list{l}") for l in range(2)]
-        tab_w = keep.tile([P, T], I32, name="tab_w", tag="slot2")
-        tab_s = keep.tile([P, T], U8, name="tab_s", tag="slot1")
-        w_s = keep.tile([P, 6 * R], U8, name="w_s", align_bytes=64)
+        tab_w = keep.tile([P, T], I32, name="tab_w", tag="slot2", align_bytes=64)
+        tab_s = keep.tile([P, T], U8, name="tab_s", tag="slot1", align_bytes=64)
+        w_s = [keep.tile([P, n * R], U8, name=f"w_s{i}", align_bytes=64) for i, n in enumerate((4, 2))]
         shifted = [keep.tile([P, 2 * HALF], U8, name=f"shifted{h}", align_bytes=64) for h in range(2)]
+        wgo_rows = keep.tile([P, P], F32, name="wgo_rows")
 
         nc.gpsimd.memset(tab_s[:].bitcast(I32), 0)
-        nc.vector.memset(w_s[:].bitcast(I32), 0)
+        nc.gpsimd.memset(w_s[0][:].bitcast(I32), 0)
+        nc.vector.memset(w_s[1][:].bitcast(I32), 0)
+        nc.vector.memset(wgo_rows[:], 0.0)
         for h in range(2):
             nc.vector.memset(shifted[h][:].bitcast(I32), 0)
+
+        def load_scales(queue, plane, sources):
+            rows = plane[:].bitcast(I32)
+            col = 0
+            for sc in sources:
+                n_pass = sc.shape[0]
+                width = n_pass * R // 4
+                queue.dma_start(
+                    rows[0:16, col : col + width].rearrange("q (a n) -> q a n", a=n_pass),
+                    sc.bitcast(I32).rearrange("a q n -> q a n"),
+                )
+                col = col + width
+
+        def spread_scales(queue, plane):
+            rows = plane[:].bitcast(I32)
+            for q in range(1, 4):
+                queue.dma_start(rows[32 * q : 32 * q + 4, :], rows[4 * q : 4 * q + 4, :])
 
         nc.sync.dma_start(lists[0][:], offs)
         tab_s_rows = tab_scales.bitcast(I32).rearrange("a (q r) t -> r q a t", r=4)
         for r in range(4):
             nc.sync.dma_start(tab_s[:].bitcast(I32)[r:P:16, :], tab_s_rows[r])
-        nc.sync.dma_start(tab_w[:], tab_words[0].rearrange("p t b -> p (t b)").bitcast(I32))
         nc.sync.dma_start(lists[1][:], offs2)
-        w_s32 = w_s[:].bitcast(I32)
-        col = 0
-        for sc in (ws_scales, wt_scales, wd4_scales, wd8_scales):
-            n_pass = sc.shape[0]
-            width = n_pass * R // 4
-            nc.sync.dma_start(
-                w_s32[0:16, col : col + width].rearrange("q (a n) -> q a n", a=n_pass),
-                sc.bitcast(I32).rearrange("a q n -> q a n"),
-            )
-            col = col + width
+        nc.sync.dma_start(tab_w[:], tab_words[0].rearrange("p t b -> p (t b)").bitcast(I32))
+        load_scales(nc.gpsimd, w_s[0], (ws_scales, wt_scales))
         w1 = [keep.tile([P, 2 * 2 * R], U8, name=f"w1_{l}", align_bytes=64) for l in range(2)]
         for l, words in enumerate((ws_words, wt_words)):
             nc.sync.dma_start(
                 w1[l][:].bitcast(I32).rearrange("p (a n) -> p a n", a=2),
                 words.bitcast(I32).rearrange("a p n -> p a n"),
             )
-        for q in range(1, 4):
-            nc.sync.dma_start(w_s32[32 * q : 32 * q + 4, :], w_s32[4 * q : 4 * q + 4, :])
+        spread_scales(nc.scalar, w_s[0])
         sm_t = keep.tile([P, 4], F32, name="sm_t")
         nc.sync.dma_start(sm_t[:], sm.rearrange("(p t) -> p t", t=4))
-        wgo_rows = keep.tile([P, P], F32, name="wgo_rows")
-        nc.gpsimd.memset(wgo_rows[:], 0.0)
-        nc.sync.dma_start(wgo_rows[0 : J // P, :], wgo[0:1, :].rearrange("o (b p) -> (o b) p", p=P))
+
         ident = keep.tile([P, P], F32, name="ident")
         make_identity(nc, ident[:])
-        pages = [keep.tile([P, T], F32, name=f"page{t}") for t in range(4)]
-        for t in range(4):
-            for c in range(T // CHUNK):
-                nc.gpsimd.memset(pages[t][:, c * CHUNK : (c + 1) * CHUNK], 0.0)
+        load_scales(nc.gpsimd, w_s[1], (wd4_scales, wd8_scales))
+        nc.gpsimd.dma_start(wgo_rows[0 : J // P, :], wgo[0:1, :].rearrange("o (b p) -> (o b) p", p=P))
         wd4 = keep.tile([P, 2 * N], U8, name="wd4", align_bytes=64)
-        nc.sync.dma_start(wd4[:].bitcast(I32), wd4_words[0].bitcast(I32))
+        nc.gpsimd.dma_start(wd4[:].bitcast(I32), wd4_words[0].bitcast(I32))
         wd8 = keep.tile([P, N], I32, name="wd8", align_bytes=64)
-        nc.sync.dma_start(wd8[:], wd8_words[0].rearrange("p n i -> p (n i)").bitcast(I32))
+        nc.gpsimd.dma_start(wd8[:], wd8_words[0].rearrange("p n i -> p (n i)").bitcast(I32))
+        spread_scales(nc.gpsimd, w_s[1])
 
-        wgo_bank = psum.tile([P, 4, P], F32, name="y_turned", tag="y_turned")
+        wgo_bank = psum.tile([P, 4, P], F32, name="wgo_bank", tag="turned0")
         nc.tensor.transpose(wgo_bank[:, 0, :], wgo_rows[:], ident[:])
         wgo_cols = keep.tile([P, J // P], F32, name="wgo_cols")
         nc.scalar.copy(wgo_cols[:], wgo_bank[:, 0, 0 : J // P])
@@ -96,32 +105,34 @@ def tile_list_msg_tanh_res_gateP_kernel(
 
         picked_s, parted = [], []
         for h in range(2):
-            ps = keep.tile([P, 2 * HALF], U8, name=f"picked_s{h}", align_bytes=64)
+            ps = keep.tile([P, 2 * HALF], U8, name=f"picked_s{h}", tag=("picked_s0", "words0_0")[h], align_bytes=64)
             for l in range(2):
                 nc.vector.tensor_copy(ps[:, l * HALF : (l + 1) * HALF], tab_s[:].indirect(half_of(l, h)))
             nc.sync.dma_start(shifted[h][:].bitcast(I32)[0 : P - 16, :], ps[:].bitcast(I32)[16:P, :])
-            pw = keep.tile([P, 2 * HALF], U32, name=f"picked_w{h}", tag=f"slot{3 * h}")
+            tags = (("words0_0", "slot0"), ("words1_0", "slot3"))[h]
+            pw = [keep.tile([P, HALF], U32, name=f"picked_w{h}_{l}", tag=tags[l], align_bytes=64) for l in range(2)]
             for l in range(2):
-                nc.vector.tensor_copy(pw[:, l * HALF : (l + 1) * HALF], tab_w[:].bitcast(U32).indirect(half_of(l, h)))
+                nc.vector.tensor_copy(pw[l][:], tab_w[:].bitcast(U32).indirect(half_of(l, h)))
             pt = keep.tile([P, 2 * 2 * 2 * HALF], U8, name=f"parted{h}", align_bytes=64)
             for l in range(2):
                 nc.vector.tensor_copy(
                     pt[:].bitcast(U16)[:, 2 * l * HALF : 2 * (l + 1) * HALF].rearrange("p (a j) -> p a j", a=2),
-                    pw[:, l * HALF : (l + 1) * HALF].bitcast(U16).rearrange("p (j a) -> p a j", a=2),
+                    pw[l][:].bitcast(U16).rearrange("p (j a) -> p a j", a=2),
                 )
             picked_s.append(ps)
             parted.append(pt)
 
-        gates = [keep.tile([P, T], F32, name=f"gates{t}", tag=f"slot{t}") for t in range(4)]
+        gates = [keep.tile([P, T], F32, name=f"gates{t}", tag=f"slot{t}", align_bytes=64) for t in range(4)]
         gT_rows = gT.rearrange("(p t) c -> t p c", t=4)
         for t in range(4):
             nc.sync.dma_start(gates[t][:], gT_rows[t])
 
-        y = [keep.tile([P, 4, HALF], F32, name=f"y{h}") for h in range(2)]
+        spans = ((0, QUARTER), (QUARTER, QUARTER), (HALF, HALF))
+        y = {j0: keep.tile([P, 4, n], F32, name=f"y{j0}") for j0, n in spans}
 
-        def first_stage(b, h_rows):
+        def first_stage(b, h_banks):
             h, j0 = divmod(b * P, HALF)
-            a_bank = psum.tile([P, R], F32, name="a_bank")
+            a_bank = psum.tile([P, R], F32, name="a_bank", tag=f"bank{b % 2}")
             steps = [(l, a) for a in range(2) for l in range(2)]
             for i, (l, a) in enumerate(steps):
                 c0 = (2 * l + a) * HALF + j0
@@ -131,49 +142,49 @@ def tile_list_msg_tanh_res_gateP_kernel(
                     lhsT=parted[h][:, 2 * c0 : 2 * (c0 + P)].bitcast(FP4X4),
                     lhsT_scale=scales[:, l * HALF + j0 : l * HALF + j0 + P],
                     rhs=w1[l][:, 2 * a * R : 2 * (a + 1) * R].bitcast(FP4X4),
-                    rhs_scale=w_s[:, (2 * l + a) * R : (2 * l + a + 1) * R],
+                    rhs_scale=w_s[0][:, (2 * l + a) * R : (2 * l + a + 1) * R],
                     start=(i == 0),
                     stop=(i == len(steps) - 1),
                 )
             th = ring.tile([P, 4, P], F32, name="th")
-            nc.scalar.activation(th[:], a_bank[:].rearrange("p (m t) -> p t m", t=4), TANH)
-            h_bank = psum.tile([P, 4, P], F32, name="h_bank")
-            for t in range(4):
-                nc.tensor.transpose(h_bank[:, t, :], th[:, t, :], ident[:])
+            nc.scalar.activation(th[:].rearrange("p t m -> p m t"), a_bank[:].rearrange("p (m t) -> p m t", t=4), TANH)
             c = (b % 2) * P
             for t in range(4):
-                nc.scalar.activation(h_rows[:, t, c : c + P], h_bank[:, t, :], COPY, scale=sm_t[:, t : t + 1])
+                nc.tensor.transpose(h_banks[:, t, c : c + P], th[:, t, :], ident[:])
 
-        def second_stage(b, h_codes, h_scales):
-            h, j0 = divmod(b * P, HALF)
+        def second_stage(b, h_codes, h_scales, y_bank):
+            span = max(j0 for j0 in y if j0 <= b * P)
+            j0 = b * P - span
             c = (b % 2) * P
-            y_bank = psum.tile([P, N], F32, name="y_bank")
             for i, (w, fmt) in enumerate(((wd4, FP4X4), (wd8, FP8X4))):
                 nc.tensor.matmul_mx(
-                    y_bank[:],
+                    y_bank,
                     lhsT=h_codes[:, c : c + P].bitcast(FP8X4),
                     lhsT_scale=h_scales[:, c : c + P],
                     rhs=w[:].bitcast(fmt),
-                    rhs_scale=w_s[:, (4 + i) * N : (5 + i) * N],
+                    rhs_scale=w_s[1][:, i * N : (i + 1) * N],
                     start=(i == 0),
                     stop=(i == 1),
                 )
             yw = ring.tile([P, 4, P], F32, name="yw")
             nc.scalar.activation(
-                yw[:], y_bank[:].rearrange("p (m t) -> p t m", t=4), COPY, scale=wgo_cols[:, b : b + 1]
+                yw[:].rearrange("p t m -> p m t"), y_bank.rearrange("p (m t) -> p m t", t=4), COPY, scale=wgo_cols[:, b : b + 1]
             )
-            y_turned = psum.tile([P, 4, P], F32, name="y_turned", tag="y_turned")
+            y_turned = psum.tile([P, 4, P], F32, name="y_turned", tag=f"turned{b % 2}")
             for t in range(4):
                 nc.tensor.transpose(y_turned[:, t, :], yw[:, t, :], ident[:])
-            nc.scalar.copy(y[h][:, :, j0 : j0 + P], y_turned[:])
+            nc.scalar.copy(y[span][:, :, j0 : j0 + P], y_turned[:])
 
         h_codes, h_scales = [], []
 
         def hidden(q):
-            h_rows = ring.tile([P, 4, QUARTER], BF16, name="h_rows")
+            h_banks = psum.tile([P, 4, QUARTER], F32, name="h_banks", tag=f"pair{q % 2}")
             for b in (2 * q, 2 * q + 1):
-                first_stage(b, h_rows)
-            h_woven = keep.tile([P, 4 * QUARTER], BF16, name=f"h_woven{q}", align_bytes=64)
+                first_stage(b, h_banks)
+            h_rows = ring.tile([P, 4, QUARTER], BF16, name="h_rows")
+            for t in range(4):
+                nc.scalar.activation(h_rows[:, t, :], h_banks[:, t, :], COPY, scale=sm_t[:, t : t + 1])
+            h_woven = keep.tile([P, 4 * QUARTER], BF16, name=f"h_woven{q}", tag=f"h_woven{q}", align_bytes=64)
             nc.scalar.copy(
                 h_woven[:].rearrange("p (c i t) -> p c t i", i=4, t=4),
                 h_rows[:].rearrange("p t (c i) -> p c t i", i=4),
@@ -183,25 +194,25 @@ def tile_list_msg_tanh_res_gateP_kernel(
             nc.vector.quantize_mx(h_codes[q][:].bitcast(FP8X4), h_scales[q][:], h_woven[:])
 
         def message(q):
+            y_banks = psum.tile([P, 2, N], F32, name="y_banks", tag=f"pair{(q + 1) % 2}")
             for b in (2 * q, 2 * q + 1):
-                second_stage(b, h_codes[q], h_scales[q])
+                second_stage(b, h_codes[q], h_scales[q], y_banks[:, b % 2, :])
 
         hidden(0)
-        hidden(1)
-        message(0)
-        hidden(2)
-        hidden(3)
-        for q in (1, 2, 3):
-            message(q)
+        for q in range(1, 4):
+            hidden(q)
+            message(q - 1)
+        message(3)
+
+        pages = [keep.tile([P, T], F32, name=f"page{t}") for t in range(4)]
+        for t in range(4):
+            for c in range(T // CHUNK):
+                nc.gpsimd.memset(pages[t][:, c * CHUNK : (c + 1) * CHUNK], 0.0)
 
         def piece_of(l, j0, n):
             return lists[l][:, j0 // 16 : (j0 + n) // 16]
 
-        groups = [
-            (0, QUARTER, (0, 1, 2, 3), "g_first"),
-            (QUARTER, QUARTER, (0, 1, 2, 3), "g_second"),
-            (HALF, HALF, (0, 1, 2, 3), "g_last"),
-        ]
+        groups = [(0, QUARTER, (0, 1, 2, 3), "ga")] + [(QUARTER, QUARTER, (0,1), "gb"), (QUARTER, QUARTER, (2, 3), "h_woven3")] + [(HALF, HALF, (0, 1, 2, 3), "h_woven0")]
         g = []
         for i, (j0, n, rows, tag) in enumerate(groups):
             picked = keep.tile([P, len(rows), n], F32, name=f"g{i}", tag=tag, align_bytes=64)
@@ -210,29 +221,41 @@ def tile_list_msg_tanh_res_gateP_kernel(
             g.append(picked)
 
         out_rows = out_0.rearrange("(p t) c -> t p c", t=4)
-        pairs = [keep.tile([P, 2, CHUNK, 2], BF16, name=f"pairs{c}") for c in range(T // CHUNK)]
+        n_pieces = T // PIECE
+        rounded = [keep.tile([P, 4, PIECE], BF16, name=f"rounded{c}") for c in range(n_pieces)]
         for i, (j0, n, rows, tag) in enumerate(groups):
-            h, c0 = divmod(j0, HALF)
             for k, t in enumerate(rows):
-                nc.vector.tensor_tensor(
-                    pages[t][:].indirect(piece_of(1, j0, n)), y[h][:, t, c0 : c0 + n], g[i][:, k, :], MULT
-                )
-                if h == 1:
+                nc.vector.tensor_tensor(pages[t][:].indirect(piece_of(1, j0, n)), y[j0][:, t, :], g[i][:, k, :], MULT)
+                if j0 + n == J:
                     nc.sync.dma_start(out_rows[t], pages[t][:])
-                    for c in range(T // CHUNK):
-                        nc.scalar.copy(pairs[c][:, t // 2, :, t % 2], pages[t][:, c * CHUNK : (c + 1) * CHUNK])
+                    for c in range(n_pieces):
+                        nc.scalar.copy(rounded[c][:, t, :], pages[t][:, c * PIECE : (c + 1) * PIECE])
 
         o_scales = keep.tile([P, T], U8, name="o_scales", align_bytes=64)
         out_words = out_1[0].rearrange("p t i -> p (t i)").bitcast(I32)
-        woven = [keep.tile([P, 4 * CHUNK], BF16, name=f"woven{c}", align_bytes=64) for c in range(T // CHUNK)]
-        for c in range(T // CHUNK):
-            nc.vector.tensor_copy(
-                woven[c][:].bitcast(I32).rearrange("p (j u) -> p j u", u=2),
-                pairs[c][:].rearrange("p u j e -> p u (j e)").bitcast(I32).rearrange("p u j -> p j u"),
+        o_codes = [keep.tile([P, CHUNK], I32, name=f"o_codes{c}", align_bytes=64) for c in range(T // CHUNK)]
+        woven = [keep.tile([P, 4 * PIECE], BF16, name=f"woven{c}", align_bytes=64) for c in range(n_pieces)]
+
+        def weave(c):
+            copy = nc.vector.tensor_copy if c < VECTOR_PIECES else nc.scalar.copy
+            copy(
+                woven[c][:].rearrange("p (c i t) -> p c t i", i=4, t=4),
+                rounded[c][:].rearrange("p t (c i) -> p c t i", i=4),
             )
-            o_codes = keep.tile([P, CHUNK], I32, name=f"o_codes{c}", align_bytes=64)
-            nc.vector.quantize_mx(o_codes[:].bitcast(FP8X4), o_scales[:, c * CHUNK : (c + 1) * CHUNK], woven[c][:])
-            nc.sync.dma_start(out_words[:, c * CHUNK : (c + 1) * CHUNK], o_codes[:])
+
+        def quantise(c):
+            k, c0 = divmod(c * PIECE, CHUNK)
+            nc.vector.quantize_mx(
+                o_codes[k][:, c0 : c0 + PIECE].bitcast(FP8X4), o_scales[:, c * PIECE : (c + 1) * PIECE], woven[c][:]
+            )
+            if c0 + PIECE == CHUNK:
+                nc.sync.dma_start(out_words[:, k * CHUNK : (k + 1) * CHUNK], o_codes[k][:])
+
+        weave(0)
+        for c in range(1, n_pieces):
+            weave(c)
+            quantise(c - 1)
+        quantise(n_pieces - 1)
         out_scales = out_2[0].bitcast(I32)
         for q in range(4):
             queue = (nc.sync, nc.scalar)[q % 2]

@@ -45,11 +45,14 @@ def tile_list_msg_tanh_res_gateP_kernel(
         wgo_rows = keep.tile([P, P], F32, name="wgo_rows")
 
         nc.gpsimd.memset(tab_s[:].bitcast(I32), 0)
-        nc.gpsimd.memset(w_s[0][:].bitcast(I32), 0)
+        nc.vector.memset(w_s[0][:].bitcast(I32), 0)
+        nc.vector.memset(shifted[0][:].bitcast(I32), 0)
+        pages = [keep.tile([P, T], F32, name=f"page{t}") for t in range(4)]
+        for t in range(2):
+            nc.vector.memset(pages[t][:], 0.0)
+        nc.vector.memset(shifted[1][:].bitcast(I32), 0)
         nc.vector.memset(w_s[1][:].bitcast(I32), 0)
         nc.vector.memset(wgo_rows[:], 0.0)
-        for h in range(2):
-            nc.vector.memset(shifted[h][:].bitcast(I32), 0)
 
         def load_scales(queue, plane, sources):
             rows = plane[:].bitcast(I32)
@@ -74,7 +77,7 @@ def tile_list_msg_tanh_res_gateP_kernel(
             nc.sync.dma_start(tab_s[:].bitcast(I32)[r:P:16, :], tab_s_rows[r])
         nc.sync.dma_start(lists[1][:], offs2)
         nc.sync.dma_start(tab_w[:], tab_words[0].rearrange("p t b -> p (t b)").bitcast(I32))
-        load_scales(nc.gpsimd, w_s[0], (ws_scales, wt_scales))
+        load_scales(nc.sync, w_s[0], (ws_scales, wt_scales))
         w1 = [keep.tile([P, 2 * 2 * R], U8, name=f"w1_{l}", align_bytes=64) for l in range(2)]
         for l, words in enumerate((ws_words, wt_words)):
             nc.sync.dma_start(
@@ -87,13 +90,13 @@ def tile_list_msg_tanh_res_gateP_kernel(
 
         ident = keep.tile([P, P], F32, name="ident")
         make_identity(nc, ident[:])
-        load_scales(nc.gpsimd, w_s[1], (wd4_scales, wd8_scales))
-        nc.gpsimd.dma_start(wgo_rows[0 : J // P, :], wgo[0:1, :].rearrange("o (b p) -> (o b) p", p=P))
+        load_scales(nc.sync, w_s[1], (wd4_scales, wd8_scales))
+        nc.sync.dma_start(wgo_rows[0 : J // P, :], wgo[0:1, :].rearrange("o (b p) -> (o b) p", p=P))
         wd4 = keep.tile([P, 2 * N], U8, name="wd4", align_bytes=64)
-        nc.gpsimd.dma_start(wd4[:].bitcast(I32), wd4_words[0].bitcast(I32))
+        nc.sync.dma_start(wd4[:].bitcast(I32), wd4_words[0].bitcast(I32))
         wd8 = keep.tile([P, N], I32, name="wd8", align_bytes=64)
-        nc.gpsimd.dma_start(wd8[:], wd8_words[0].rearrange("p n i -> p (n i)").bitcast(I32))
-        spread_scales(nc.gpsimd, w_s[1])
+        nc.sync.dma_start(wd8[:], wd8_words[0].rearrange("p n i -> p (n i)").bitcast(I32))
+        spread_scales(nc.sync, w_s[1])
 
         wgo_bank = psum.tile([P, 4, P], F32, name="wgo_bank", tag="turned0")
         nc.tensor.transpose(wgo_bank[:, 0, :], wgo_rows[:], ident[:])
@@ -108,7 +111,7 @@ def tile_list_msg_tanh_res_gateP_kernel(
             ps = keep.tile([P, 2 * HALF], U8, name=f"picked_s{h}", tag=("picked_s0", "words0_0")[h], align_bytes=64)
             for l in range(2):
                 nc.vector.tensor_copy(ps[:, l * HALF : (l + 1) * HALF], tab_s[:].indirect(half_of(l, h)))
-            nc.sync.dma_start(shifted[h][:].bitcast(I32)[0 : P - 16, :], ps[:].bitcast(I32)[16:P, :])
+            (nc.scalar, nc.sync)[h].dma_start(shifted[h][:].bitcast(I32)[0 : P - 16, :], ps[:].bitcast(I32)[16:P, :])
             tags = (("words0_0", "slot0"), ("words1_0", "slot3"))[h]
             pw = [keep.tile([P, HALF], U32, name=f"picked_w{h}_{l}", tag=tags[l], align_bytes=64) for l in range(2)]
             for l in range(2):
@@ -122,13 +125,14 @@ def tile_list_msg_tanh_res_gateP_kernel(
             picked_s.append(ps)
             parted.append(pt)
 
+        for t in range(2, 4):
+            nc.vector.memset(pages[t][:], 0.0)
         gates = [keep.tile([P, T], F32, name=f"gates{t}", tag=f"slot{t}", align_bytes=64) for t in range(4)]
         gT_rows = gT.rearrange("(p t) c -> t p c", t=4)
         for t in range(4):
             nc.sync.dma_start(gates[t][:], gT_rows[t])
 
-        spans = ((0, QUARTER), (QUARTER, QUARTER), (HALF, HALF))
-        y = {j0: keep.tile([P, 4, n], F32, name=f"y{j0}") for j0, n in spans}
+        y = [keep.tile([P, 4, QUARTER], F32, name=f"y{q}") for q in range(4)]
 
         def first_stage(b, h_banks):
             h, j0 = divmod(b * P, HALF)
@@ -153,8 +157,6 @@ def tile_list_msg_tanh_res_gateP_kernel(
                 nc.tensor.transpose(h_banks[:, t, c : c + P], th[:, t, :], ident[:])
 
         def second_stage(b, h_codes, h_scales, y_bank):
-            span = max(j0 for j0 in y if j0 <= b * P)
-            j0 = b * P - span
             c = (b % 2) * P
             for i, (w, fmt) in enumerate(((wd4, FP4X4), (wd8, FP8X4))):
                 nc.tensor.matmul_mx(
@@ -173,7 +175,7 @@ def tile_list_msg_tanh_res_gateP_kernel(
             y_turned = psum.tile([P, 4, P], F32, name="y_turned", tag=f"turned{b % 2}")
             for t in range(4):
                 nc.tensor.transpose(y_turned[:, t, :], yw[:, t, :], ident[:])
-            nc.scalar.copy(y[span][:, :, j0 : j0 + P], y_turned[:])
+            nc.scalar.copy(y[b // 2][:, :, c : c + P], y_turned[:])
 
         h_codes, h_scales = [], []
 
@@ -204,32 +206,43 @@ def tile_list_msg_tanh_res_gateP_kernel(
             message(q - 1)
         message(3)
 
-        pages = [keep.tile([P, T], F32, name=f"page{t}") for t in range(4)]
-        for t in range(4):
-            for c in range(T // CHUNK):
-                nc.gpsimd.memset(pages[t][:, c * CHUNK : (c + 1) * CHUNK], 0.0)
-
         def piece_of(l, j0, n):
             return lists[l][:, j0 // 16 : (j0 + n) // 16]
 
-        groups = [(0, QUARTER, (0, 1, 2, 3), "ga")] + [(QUARTER, QUARTER, (0,1), "gb"), (QUARTER, QUARTER, (2, 3), "h_woven3")] + [(HALF, HALF, (0, 1, 2, 3), "h_woven0")]
-        g = []
-        for i, (j0, n, rows, tag) in enumerate(groups):
-            picked = keep.tile([P, len(rows), n], F32, name=f"g{i}", tag=tag, align_bytes=64)
+        g = {}
+
+        def pick_gates(j0, n, rows, tag):
+            picked = keep.tile([P, len(rows), n], F32, name=f"g{j0}_{rows[0]}", tag=tag, align_bytes=64)
             for k, t in enumerate(rows):
                 nc.vector.tensor_copy(picked[:, k, :], gates[t][:].indirect(piece_of(0, j0, n)))
-            g.append(picked)
+                for c0 in range(0, n, QUARTER):
+                    g[(j0 + c0) // QUARTER, t] = picked[:, k, c0 : c0 + QUARTER]
 
         out_rows = out_0.rearrange("(p t) c -> t p c", t=4)
         n_pieces = T // PIECE
         rounded = [keep.tile([P, 4, PIECE], BF16, name=f"rounded{c}") for c in range(n_pieces)]
-        for i, (j0, n, rows, tag) in enumerate(groups):
-            for k, t in enumerate(rows):
-                nc.vector.tensor_tensor(pages[t][:].indirect(piece_of(1, j0, n)), y[j0][:, t, :], g[i][:, k, :], MULT)
-                if j0 + n == J:
-                    nc.sync.dma_start(out_rows[t], pages[t][:])
-                    for c in range(n_pieces):
-                        nc.scalar.copy(rounded[c][:, t, :], pages[t][:, c * PIECE : (c + 1) * PIECE])
+
+        def place(q, t):
+            nc.vector.tensor_tensor(pages[t][:].indirect(piece_of(1, q * QUARTER, QUARTER)), y[q][:, t, :], g[q, t], MULT)
+            if q == 3:
+                nc.sync.dma_start(out_rows[t], pages[t][:])
+                for c in range(n_pieces):
+                    nc.scalar.copy(rounded[c][:, t, :], pages[t][:, c * PIECE : (c + 1) * PIECE])
+
+        pick_gates(0, HALF, (0, 1), "ga")
+        pick_gates(0, QUARTER, (2, 3), "gb")
+        pick_gates(QUARTER, QUARTER, (2, 3), "h_woven3")
+        pick_gates(HALF, HALF, (0, 1), "gc")
+        pick_gates(HALF, HALF, (2,), "gd")
+        for q in range(2):
+            for t in range(4):
+                place(q, t)
+        for q in (2, 3):
+            for t in range(3):
+                place(q, t)
+        pick_gates(HALF, HALF, (3,), "gc")
+        for q in (2, 3):
+            place(q, 3)
 
         o_scales = keep.tile([P, T], U8, name="o_scales", align_bytes=64)
         out_words = out_1[0].rearrange("p t i -> p (t i)").bitcast(I32)

@@ -21,9 +21,11 @@ MULT = mybir.AluOpType.mult
 P = 128
 HALF = J // 2
 QUARTER = J // 4
-CHUNK = 512
+SCALE_ROWS = 16
+HEAD_PAGES = 3
+STORE_COLS = 512
 PIECE = 256
-VECTOR_PIECES = 5
+VECTOR_PIECES = 6
 
 
 def tile_list_msg_tanh_res_gateP_kernel(
@@ -38,155 +40,169 @@ def tile_list_msg_tanh_res_gateP_kernel(
         psum = ctx.enter_context(tc.psum_pool(name="psum", bufs=1))
 
         lists = [keep.tile([P, J // 16], U16, name=f"list{l}") for l in range(2)]
-        tab_w = keep.tile([P, T], I32, name="tab_w", tag="slot2", align_bytes=64)
-        tab_s = keep.tile([P, T], U8, name="tab_s", tag="slot1", align_bytes=64)
-        w_s = [keep.tile([P, n * R], U8, name=f"w_s{i}", align_bytes=64) for i, n in enumerate((4, 2))]
-        shifted = [keep.tile([P, 2 * HALF], U8, name=f"shifted{h}", align_bytes=64) for h in range(2)]
+        tab_w = keep.tile([P, T], I32, name="tab_w", tag="gates2", align_bytes=64)
+        tab_s = keep.tile([P, T], U8, name="tab_s", tag="gates1", align_bytes=64)
+        w_planes = [keep.tile([P, n * R], U8, name=f"w_planes{i}", align_bytes=64) for i, n in enumerate((4, 2))]
+        pass1_planes = [keep.tile([P, 2 * HALF], U8, name=f"pass1_planes{h}", align_bytes=64) for h in range(2)]
         wgo_rows = keep.tile([P, P], F32, name="wgo_rows")
 
         nc.gpsimd.memset(tab_s[:].bitcast(I32), 0)
-        nc.vector.memset(w_s[0][:].bitcast(I32), 0)
-        nc.vector.memset(shifted[0][:].bitcast(I32), 0)
-        pages = [keep.tile([P, T], F32, name=f"page{t}") for t in range(4)]
-        for t in range(2):
-            nc.vector.memset(pages[t][:], 0.0)
-        nc.vector.memset(shifted[1][:].bitcast(I32), 0)
-        nc.vector.memset(w_s[1][:].bitcast(I32), 0)
-        nc.vector.memset(wgo_rows[:], 0.0)
+        nc.vector.memset(w_planes[0][:].bitcast(I32), 0)
+        nc.vector.memset(pass1_planes[0][:].bitcast(I32), 0)
+        pages = [keep.tile([P, T], F32, name=f"page{t}") for t in range(HEAD_PAGES)]
+        for t in range(HEAD_PAGES):
+            nc.vector.memset(pages[t][:].bitcast(I32), 0)
+        nc.vector.memset(pass1_planes[1][:].bitcast(I32), 0)
+        nc.vector.memset(w_planes[1][:].bitcast(I32), 0)
 
-        def load_scales(queue, plane, sources):
-            rows = plane[:].bitcast(I32)
+        def stage_scales(queue, staged, sources):
+            words = staged.bitcast(I32)
             col = 0
-            for sc in sources:
-                n_pass = sc.shape[0]
-                width = n_pass * R // 4
+            for scales in sources:
+                passes = scales.shape[0]
+                width = passes * R // 4
                 queue.dma_start(
-                    rows[0:16, col : col + width].rearrange("q (a n) -> q a n", a=n_pass),
-                    sc.bitcast(I32).rearrange("a q n -> q a n"),
+                    words[0:SCALE_ROWS, col : col + width].rearrange("q (a n) -> q a n", a=passes),
+                    scales.bitcast(I32).rearrange("a q n -> q a n"),
                 )
                 col = col + width
 
-        def spread_scales(queue, plane):
-            rows = plane[:].bitcast(I32)
-            for q in range(1, 4):
-                queue.dma_start(rows[32 * q : 32 * q + 4, :], rows[4 * q : 4 * q + 4, :])
+        def spread_scales(queue, planes, staged):
+            for quad in range(4):
+                queue.dma_start(
+                    planes[:].bitcast(I32)[32 * quad : 32 * quad + 4, :],
+                    staged.bitcast(I32)[4 * quad : 4 * quad + 4, :],
+                )
 
+        w_staged = keep.tile([SCALE_ROWS, 4 * R], U8, name="w_staged", tag="staged", align_bytes=64)
+        stage_scales(nc.gpsimd, w_staged[:], (ws_scales, wt_scales))
         nc.sync.dma_start(lists[0][:], offs)
         tab_s_rows = tab_scales.bitcast(I32).rearrange("a (q r) t -> r q a t", r=4)
         for r in range(4):
             nc.sync.dma_start(tab_s[:].bitcast(I32)[r:P:16, :], tab_s_rows[r])
         nc.sync.dma_start(lists[1][:], offs2)
         nc.sync.dma_start(tab_w[:], tab_words[0].rearrange("p t b -> p (t b)").bitcast(I32))
-        load_scales(nc.sync, w_s[0], (ws_scales, wt_scales))
-        w1 = [keep.tile([P, 2 * 2 * R], U8, name=f"w1_{l}", align_bytes=64) for l in range(2)]
+        w_words = [keep.tile([P, 2 * 2 * R], U8, name=f"w_words{l}", align_bytes=64) for l in range(2)]
         for l, words in enumerate((ws_words, wt_words)):
             nc.sync.dma_start(
-                w1[l][:].bitcast(I32).rearrange("p (a n) -> p a n", a=2),
+                w_words[l][:].bitcast(I32).rearrange("p (a n) -> p a n", a=2),
                 words.bitcast(I32).rearrange("a p n -> p a n"),
             )
-        spread_scales(nc.scalar, w_s[0])
-        sm_t = keep.tile([P, 4], F32, name="sm_t")
-        nc.sync.dma_start(sm_t[:], sm.rearrange("(p t) -> p t", t=4))
+        spread_scales(nc.scalar, w_planes[0], w_staged[:])
+        sm_rows = keep.tile([P, 4], F32, name="sm_rows")
+        nc.sync.dma_start(sm_rows[:], sm.rearrange("(p t) -> p t", t=4))
 
         ident = keep.tile([P, P], F32, name="ident")
         make_identity(nc, ident[:])
-        load_scales(nc.sync, w_s[1], (wd4_scales, wd8_scales))
-        nc.sync.dma_start(wgo_rows[0 : J // P, :], wgo[0:1, :].rearrange("o (b p) -> (o b) p", p=P))
-        wd4 = keep.tile([P, 2 * N], U8, name="wd4", align_bytes=64)
-        nc.sync.dma_start(wd4[:].bitcast(I32), wd4_words[0].bitcast(I32))
-        wd8 = keep.tile([P, N], I32, name="wd8", align_bytes=64)
-        nc.sync.dma_start(wd8[:], wd8_words[0].rearrange("p n i -> p (n i)").bitcast(I32))
-        spread_scales(nc.sync, w_s[1])
+        nc.gpsimd.memset(wgo_rows[:], 0.0)
+        nc.gpsimd.dma_start(wgo_rows[0 : J // P, :], wgo[0:1, :].rearrange("o (b p) -> (o b) p", p=P))
+        wd = keep.tile([P, 8 * N], U8, name="wd", tag="staged", align_bytes=64)
+        wd4, wd8, wd_staged = wd[:, 0 : 2 * N], wd[:, 2 * N : 6 * N], wd[:, 6 * N : 8 * N]
+        stage_scales(nc.sync, wd_staged, (wd4_scales, wd8_scales))
+        nc.sync.dma_start(wd4.bitcast(I32), wd4_words[0].bitcast(I32))
+        nc.sync.dma_start(wd8.bitcast(I32), wd8_words[0].rearrange("p n i -> p (n i)").bitcast(I32))
+        spread_scales(nc.sync, w_planes[1], wd_staged)
 
         wgo_bank = psum.tile([P, 4, P], F32, name="wgo_bank", tag="turned0")
         nc.tensor.transpose(wgo_bank[:, 0, :], wgo_rows[:], ident[:])
         wgo_cols = keep.tile([P, J // P], F32, name="wgo_cols")
         nc.scalar.copy(wgo_cols[:], wgo_bank[:, 0, 0 : J // P])
 
-        def half_of(l, h):
-            return lists[l][:, h * (HALF // 16) : (h + 1) * (HALF // 16)]
+        def offsets(l, j0, n):
+            return lists[l][:, j0 // 16 : (j0 + n) // 16]
 
-        picked_s, parted = [], []
+        plane_tags = ("pass0_planes0", "first_words")
+        word_tags = (("first_words", "gates0"), ("last_page", "gates3"))
+        pass0_planes, parted = [], []
         for h in range(2):
-            ps = keep.tile([P, 2 * HALF], U8, name=f"picked_s{h}", tag=("picked_s0", "words0_0")[h], align_bytes=64)
-            for l in range(2):
-                nc.vector.tensor_copy(ps[:, l * HALF : (l + 1) * HALF], tab_s[:].indirect(half_of(l, h)))
-            (nc.scalar, nc.sync)[h].dma_start(shifted[h][:].bitcast(I32)[0 : P - 16, :], ps[:].bitcast(I32)[16:P, :])
-            tags = (("words0_0", "slot0"), ("words1_0", "slot3"))[h]
-            pw = [keep.tile([P, HALF], U32, name=f"picked_w{h}_{l}", tag=tags[l], align_bytes=64) for l in range(2)]
-            for l in range(2):
-                nc.vector.tensor_copy(pw[l][:], tab_w[:].bitcast(U32).indirect(half_of(l, h)))
-            pt = keep.tile([P, 2 * 2 * 2 * HALF], U8, name=f"parted{h}", align_bytes=64)
+            planes = keep.tile([P, 2 * HALF], U8, name=f"pass0_planes{h}", tag=plane_tags[h], align_bytes=64)
             for l in range(2):
                 nc.vector.tensor_copy(
-                    pt[:].bitcast(U16)[:, 2 * l * HALF : 2 * (l + 1) * HALF].rearrange("p (a j) -> p a j", a=2),
-                    pw[l][:].bitcast(U16).rearrange("p (j a) -> p a j", a=2),
+                    planes[:, l * HALF : (l + 1) * HALF], tab_s[:].indirect(offsets(l, h * HALF, HALF))
                 )
-            picked_s.append(ps)
-            parted.append(pt)
+            (nc.scalar, nc.sync)[h].dma_start(
+                pass1_planes[h][:].bitcast(I32)[0 : P - 16, :], planes[:].bitcast(I32)[16:P, :]
+            )
+            picked = [
+                keep.tile([P, HALF], U32, name=f"picked{h}_{l}", tag=word_tags[h][l], align_bytes=64) for l in range(2)
+            ]
+            for l in range(2):
+                nc.vector.tensor_copy(picked[l][:], tab_w[:].bitcast(U32).indirect(offsets(l, h * HALF, HALF)))
+            words = keep.tile([P, 2 * 2 * 2 * HALF], U8, name=f"parted{h}", align_bytes=64)
+            for l in range(2):
+                nc.vector.tensor_copy(
+                    words[:].bitcast(U16)[:, 2 * l * HALF : 2 * (l + 1) * HALF].rearrange("p (a j) -> p a j", a=2),
+                    picked[l][:].bitcast(U16).rearrange("p (j a) -> p a j", a=2),
+                )
+            pass0_planes.append(planes)
+            parted.append(words)
 
-        for t in range(2, 4):
-            nc.vector.memset(pages[t][:], 0.0)
-        gates = [keep.tile([P, T], F32, name=f"gates{t}", tag=f"slot{t}", align_bytes=64) for t in range(4)]
+        gates = [keep.tile([P, T], F32, name=f"gates{t}", tag=f"gates{t}", align_bytes=64) for t in range(4)]
         gT_rows = gT.rearrange("(p t) c -> t p c", t=4)
         for t in range(4):
             nc.sync.dma_start(gates[t][:], gT_rows[t])
 
-        y = [keep.tile([P, 4, QUARTER], F32, name=f"y{q}") for q in range(4)]
+        wy = [keep.tile([P, 4, HALF], F32, name=f"wy{h}") for h in range(2)]
 
-        def first_stage(b, h_banks):
+        def first_product(b, tanh_banks):
             h, j0 = divmod(b * P, HALF)
-            a_bank = psum.tile([P, R], F32, name="a_bank", tag=f"bank{b % 2}")
+            a_bank = psum.tile([P, R], F32, name="a_bank", tag=f"sum{b % 2}")
             steps = [(l, a) for a in range(2) for l in range(2)]
             for i, (l, a) in enumerate(steps):
                 c0 = (2 * l + a) * HALF + j0
-                scales = (picked_s, shifted)[a][h]
+                planes = (pass0_planes, pass1_planes)[a][h]
                 nc.tensor.matmul_mx(
                     a_bank[:],
                     lhsT=parted[h][:, 2 * c0 : 2 * (c0 + P)].bitcast(FP4X4),
-                    lhsT_scale=scales[:, l * HALF + j0 : l * HALF + j0 + P],
-                    rhs=w1[l][:, 2 * a * R : 2 * (a + 1) * R].bitcast(FP4X4),
-                    rhs_scale=w_s[0][:, (2 * l + a) * R : (2 * l + a + 1) * R],
+                    lhsT_scale=planes[:, l * HALF + j0 : l * HALF + j0 + P],
+                    rhs=w_words[l][:, 2 * a * R : 2 * (a + 1) * R].bitcast(FP4X4),
+                    rhs_scale=w_planes[0][:, (2 * l + a) * R : (2 * l + a + 1) * R],
                     start=(i == 0),
                     stop=(i == len(steps) - 1),
                 )
-            th = ring.tile([P, 4, P], F32, name="th")
-            nc.scalar.activation(th[:].rearrange("p t m -> p m t"), a_bank[:].rearrange("p (m t) -> p m t", t=4), TANH)
-            c = (b % 2) * P
+            tanh_a = ring.tile([P, 4, P], F32, name="tanh_a")
+            nc.scalar.activation(
+                tanh_a[:].rearrange("p t m -> p m t"), a_bank[:].rearrange("p (m t) -> p m t", t=4), TANH
+            )
+            c0 = b * P % QUARTER
             for t in range(4):
-                nc.tensor.transpose(h_banks[:, t, c : c + P], th[:, t, :], ident[:])
+                nc.tensor.transpose(tanh_banks[:, t, c0 : c0 + P], tanh_a[:, t, :], ident[:])
 
-        def second_stage(b, h_codes, h_scales, y_bank):
-            c = (b % 2) * P
+        def second_product(b, y_bank, turned_tag):
+            q, c0 = divmod(b * P, QUARTER)
             for i, (w, fmt) in enumerate(((wd4, FP4X4), (wd8, FP8X4))):
                 nc.tensor.matmul_mx(
                     y_bank,
-                    lhsT=h_codes[:, c : c + P].bitcast(FP8X4),
-                    lhsT_scale=h_scales[:, c : c + P],
-                    rhs=w[:].bitcast(fmt),
-                    rhs_scale=w_s[1][:, i * N : (i + 1) * N],
+                    lhsT=h_codes[q][:, c0 : c0 + P].bitcast(FP8X4),
+                    lhsT_scale=h_scales[q][:, c0 : c0 + P],
+                    rhs=w.bitcast(fmt),
+                    rhs_scale=w_planes[1][:, i * N : (i + 1) * N],
                     start=(i == 0),
                     stop=(i == 1),
                 )
-            yw = ring.tile([P, 4, P], F32, name="yw")
+            wy_edges = ring.tile([P, 4, P], F32, name="wy_edges")
             nc.scalar.activation(
-                yw[:].rearrange("p t m -> p m t"), y_bank.rearrange("p (m t) -> p m t", t=4), COPY, scale=wgo_cols[:, b : b + 1]
+                wy_edges[:].rearrange("p t m -> p m t"),
+                y_bank.rearrange("p (m t) -> p m t", t=4),
+                COPY,
+                scale=wgo_cols[:, b : b + 1],
             )
-            y_turned = psum.tile([P, 4, P], F32, name="y_turned", tag=f"turned{b % 2}")
+            wy_bank = psum.tile([P, 4, P], F32, name="wy_bank", tag=turned_tag)
             for t in range(4):
-                nc.tensor.transpose(y_turned[:, t, :], yw[:, t, :], ident[:])
-            nc.scalar.copy(y[b // 2][:, :, c : c + P], y_turned[:])
+                nc.tensor.transpose(wy_bank[:, t, :], wy_edges[:, t, :], ident[:])
+            h, j0 = divmod(b * P, HALF)
+            nc.scalar.copy(wy[h][:, :, j0 : j0 + P], wy_bank[:])
 
         h_codes, h_scales = [], []
 
         def hidden(q):
-            h_banks = psum.tile([P, 4, QUARTER], F32, name="h_banks", tag=f"pair{q % 2}")
+            h_woven = keep.tile([P, 4 * QUARTER], BF16, name=f"h_woven{q}", tag=f"h_woven{q}", align_bytes=64)
+            tanh_banks = psum.tile([P, 4, QUARTER], F32, name="tanh_banks", tag=f"pair{q % 2}")
             for b in (2 * q, 2 * q + 1):
-                first_stage(b, h_banks)
+                first_product(b, tanh_banks)
             h_rows = ring.tile([P, 4, QUARTER], BF16, name="h_rows")
             for t in range(4):
-                nc.scalar.activation(h_rows[:, t, :], h_banks[:, t, :], COPY, scale=sm_t[:, t : t + 1])
-            h_woven = keep.tile([P, 4 * QUARTER], BF16, name=f"h_woven{q}", tag=f"h_woven{q}", align_bytes=64)
+                nc.scalar.activation(h_rows[:, t, :], tanh_banks[:, t, :], COPY, scale=sm_rows[:, t : t + 1])
             nc.scalar.copy(
                 h_woven[:].rearrange("p (c i t) -> p c t i", i=4, t=4),
                 h_rows[:].rearrange("p t (c i) -> p c t i", i=4),
@@ -196,9 +212,15 @@ def tile_list_msg_tanh_res_gateP_kernel(
             nc.vector.quantize_mx(h_codes[q][:].bitcast(FP8X4), h_scales[q][:], h_woven[:])
 
         def message(q):
-            y_banks = psum.tile([P, 2, N], F32, name="y_banks", tag=f"pair{(q + 1) % 2}")
-            for b in (2 * q, 2 * q + 1):
-                second_stage(b, h_codes[q], h_scales[q], y_banks[:, b % 2, :])
+            if q < 3:
+                pair = psum.tile([P, 2, N], F32, name="y_banks", tag=f"pair{(q + 1) % 2}")
+                y_banks = [pair[:, i, :] for i in range(2)]
+                turned_tags = ("turned0", "turned1")
+            else:
+                y_banks = [psum.tile([P, N], F32, name="y_bank", tag=f"turned{i}")[:] for i in range(2)]
+                turned_tags = ("sum0", "sum1")
+            for i in range(2):
+                second_product(2 * q + i, y_banks[i], turned_tags[i])
 
         hidden(0)
         for q in range(1, 4):
@@ -206,63 +228,65 @@ def tile_list_msg_tanh_res_gateP_kernel(
             message(q - 1)
         message(3)
 
-        def piece_of(l, j0, n):
-            return lists[l][:, j0 // 16 : (j0 + n) // 16]
+        pages.append(keep.tile([P, T], F32, name="page3", tag="last_page", align_bytes=64))
+        nc.vector.memset(pages[HEAD_PAGES][:].bitcast(I32), 0)
 
-        g = {}
+        picked_gates = {}
 
         def pick_gates(j0, n, rows, tag):
             picked = keep.tile([P, len(rows), n], F32, name=f"g{j0}_{rows[0]}", tag=tag, align_bytes=64)
             for k, t in enumerate(rows):
-                nc.vector.tensor_copy(picked[:, k, :], gates[t][:].indirect(piece_of(0, j0, n)))
+                nc.vector.tensor_copy(picked[:, k, :], gates[t][:].indirect(offsets(0, j0, n)))
                 for c0 in range(0, n, QUARTER):
-                    g[(j0 + c0) // QUARTER, t] = picked[:, k, c0 : c0 + QUARTER]
+                    picked_gates[j0 + c0, t] = picked[:, k, c0:n]
 
         out_rows = out_0.rearrange("(p t) c -> t p c", t=4)
         n_pieces = T // PIECE
-        rounded = [keep.tile([P, 4, PIECE], BF16, name=f"rounded{c}") for c in range(n_pieces)]
+        rounded = [keep.tile([P, 2, PIECE, 2], BF16, name=f"rounded{c}") for c in range(n_pieces)]
 
-        def place(q, t):
-            nc.vector.tensor_tensor(pages[t][:].indirect(piece_of(1, q * QUARTER, QUARTER)), y[q][:, t, :], g[q, t], MULT)
-            if q == 3:
+        def place(j0, n, t):
+            h, c0 = divmod(j0, HALF)
+            nc.vector.tensor_tensor(
+                pages[t][:].indirect(offsets(1, j0, n)), wy[h][:, t, c0 : c0 + n], picked_gates[j0, t][:, 0:n], MULT
+            )
+            if j0 + n == J:
                 nc.sync.dma_start(out_rows[t], pages[t][:])
                 for c in range(n_pieces):
-                    nc.scalar.copy(rounded[c][:, t, :], pages[t][:, c * PIECE : (c + 1) * PIECE])
+                    nc.scalar.copy(rounded[c][:, t // 2, :, t % 2], pages[t][:, c * PIECE : (c + 1) * PIECE])
 
-        pick_gates(0, HALF, (0, 1), "ga")
-        pick_gates(0, QUARTER, (2, 3), "gb")
+        pick_gates(0, HALF, (0, 1), "g_low_rows")
+        pick_gates(0, QUARTER, (2, 3), "g_high_rows")
         pick_gates(QUARTER, QUARTER, (2, 3), "h_woven3")
-        pick_gates(HALF, HALF, (0, 1), "gc")
-        pick_gates(HALF, HALF, (2,), "gd")
+        pick_gates(HALF, HALF, (0, 1, 2, 3), "g_second_half")
         for q in range(2):
             for t in range(4):
-                place(q, t)
+                place(q * QUARTER, QUARTER, t)
         for q in (2, 3):
-            for t in range(3):
-                place(q, t)
-        pick_gates(HALF, HALF, (3,), "gc")
-        for q in (2, 3):
-            place(q, 3)
+            place(q * QUARTER, QUARTER, 0)
+        for t in range(1, 4):
+            place(HALF, HALF, t)
 
-        o_scales = keep.tile([P, T], U8, name="o_scales", align_bytes=64)
+        out_plane = keep.tile([P, T], U8, name="out_plane", align_bytes=64)
         out_words = out_1[0].rearrange("p t i -> p (t i)").bitcast(I32)
-        o_codes = [keep.tile([P, CHUNK], I32, name=f"o_codes{c}", align_bytes=64) for c in range(T // CHUNK)]
+        out_codes = [
+            keep.tile([P, STORE_COLS], I32, name=f"out_codes{s}", align_bytes=64) for s in range(T // STORE_COLS)
+        ]
         woven = [keep.tile([P, 4 * PIECE], BF16, name=f"woven{c}", align_bytes=64) for c in range(n_pieces)]
 
         def weave(c):
-            copy = nc.vector.tensor_copy if c < VECTOR_PIECES else nc.scalar.copy
+            copy, word = (nc.vector.tensor_copy, I32) if c < VECTOR_PIECES else (nc.scalar.copy, U32)
             copy(
-                woven[c][:].rearrange("p (c i t) -> p c t i", i=4, t=4),
-                rounded[c][:].rearrange("p t (c i) -> p c t i", i=4),
+                woven[c][:].bitcast(word).rearrange("p (j u) -> p j u", u=2),
+                rounded[c][:].rearrange("p u j e -> p u (j e)").bitcast(word).rearrange("p u j -> p j u"),
             )
 
         def quantise(c):
-            k, c0 = divmod(c * PIECE, CHUNK)
+            s, c0 = divmod(c * PIECE, STORE_COLS)
             nc.vector.quantize_mx(
-                o_codes[k][:, c0 : c0 + PIECE].bitcast(FP8X4), o_scales[:, c * PIECE : (c + 1) * PIECE], woven[c][:]
+                out_codes[s][:, c0 : c0 + PIECE].bitcast(FP8X4), out_plane[:, c * PIECE : (c + 1) * PIECE], woven[c][:]
             )
-            if c0 + PIECE == CHUNK:
-                nc.sync.dma_start(out_words[:, k * CHUNK : (k + 1) * CHUNK], o_codes[k][:])
+            if c0 + PIECE == STORE_COLS:
+                nc.sync.dma_start(out_words[:, s * STORE_COLS : (s + 1) * STORE_COLS], out_codes[s][:])
 
         weave(0)
         for c in range(1, n_pieces):
@@ -270,6 +294,7 @@ def tile_list_msg_tanh_res_gateP_kernel(
             quantise(c - 1)
         quantise(n_pieces - 1)
         out_scales = out_2[0].bitcast(I32)
-        for q in range(4):
-            queue = (nc.sync, nc.scalar)[q % 2]
-            queue.dma_start(out_scales[4 * q : 4 * q + 4, :], o_scales[:].bitcast(I32)[32 * q : 32 * q + 4, :])
+        for quad in range(4):
+            (nc.sync, nc.scalar)[quad % 2].dma_start(
+                out_scales[4 * quad : 4 * quad + 4, :], out_plane[:].bitcast(I32)[32 * quad : 32 * quad + 4, :]
+            )

@@ -22,7 +22,6 @@ P = 128
 HALF = J // 2
 QUARTER = J // 4
 SCALE_ROWS = 16
-HEAD_PAGES = 3
 STORE_COLS = 512
 PIECE = 256
 VECTOR_PIECES = 6
@@ -36,21 +35,21 @@ def tile_list_msg_tanh_res_gateP_kernel(
     nc = tc.nc
     with ExitStack() as ctx:
         keep = ctx.enter_context(tc.tile_pool(name="keep", bufs=1))
-        ring = ctx.enter_context(tc.tile_pool(name="ring", bufs=3))
+        placed = ctx.enter_context(tc.tile_pool(name="placed", bufs=1))
+        ring = ctx.enter_context(tc.tile_pool(name="ring", bufs=4))
         psum = ctx.enter_context(tc.psum_pool(name="psum", bufs=1))
 
         lists = [keep.tile([P, J // 16], U16, name=f"list{l}") for l in range(2)]
-        tab_w = keep.tile([P, T], I32, name="tab_w", tag="gates2", align_bytes=64)
-        tab_s = keep.tile([P, T], U8, name="tab_s", tag="gates1", align_bytes=64)
+        tab_w = keep.tile([P, T], I32, name="tab_w", tag="gates3", align_bytes=64)
+        tab_s = keep.tile([P, T], U8, name="tab_s", tag="gates2", align_bytes=64)
         w_planes = [keep.tile([P, n * R], U8, name=f"w_planes{i}", align_bytes=64) for i, n in enumerate((4, 2))]
         pass1_planes = [keep.tile([P, 2 * HALF], U8, name=f"pass1_planes{h}", align_bytes=64) for h in range(2)]
-        wgo_rows = keep.tile([P, P], F32, name="wgo_rows")
 
-        nc.gpsimd.memset(tab_s[:].bitcast(I32), 0)
+        nc.vector.memset(tab_s[:].bitcast(I32), 0)
         nc.vector.memset(w_planes[0][:].bitcast(I32), 0)
         nc.vector.memset(pass1_planes[0][:].bitcast(I32), 0)
-        pages = [keep.tile([P, T], F32, name=f"page{t}") for t in range(HEAD_PAGES)]
-        for t in range(HEAD_PAGES):
+        pages = [keep.tile([P, T], F32, name=f"page{t}") for t in range(3)]
+        for t in range(3):
             nc.vector.memset(pages[t][:].bitcast(I32), 0)
         nc.vector.memset(pass1_planes[1][:].bitcast(I32), 0)
         nc.vector.memset(w_planes[1][:].bitcast(I32), 0)
@@ -74,197 +73,235 @@ def tile_list_msg_tanh_res_gateP_kernel(
                     staged.bitcast(I32)[4 * quad : 4 * quad + 4, :],
                 )
 
-        w_staged = keep.tile([SCALE_ROWS, 4 * R], U8, name="w_staged", tag="staged", align_bytes=64)
-        stage_scales(nc.gpsimd, w_staged[:], (ws_scales, wt_scales))
+        w_staged = keep.tile([SCALE_ROWS, 4 * R], U8, name="w_staged", align_bytes=64)[:]
+        ident = keep.tile([P, P], F32, name="ident")
+        make_identity(nc, ident[:])
         nc.sync.dma_start(lists[0][:], offs)
         tab_s_rows = tab_scales.bitcast(I32).rearrange("a (q r) t -> r q a t", r=4)
         for r in range(4):
             nc.sync.dma_start(tab_s[:].bitcast(I32)[r:P:16, :], tab_s_rows[r])
         nc.sync.dma_start(lists[1][:], offs2)
         nc.sync.dma_start(tab_w[:], tab_words[0].rearrange("p t b -> p (t b)").bitcast(I32))
-        w_words = [keep.tile([P, 2 * 2 * R], U8, name=f"w_words{l}", align_bytes=64) for l in range(2)]
+        stage_scales(nc.sync, w_staged, (ws_scales, wt_scales))
+        w_words = keep.tile([P, 8 * R], U8, name="w_words", align_bytes=64)
         for l, words in enumerate((ws_words, wt_words)):
             nc.sync.dma_start(
-                w_words[l][:].bitcast(I32).rearrange("p (a n) -> p a n", a=2),
+                w_words[:, 4 * l * R : 4 * (l + 1) * R].bitcast(I32).rearrange("p (a n) -> p a n", a=2),
                 words.bitcast(I32).rearrange("a p n -> p a n"),
             )
-        spread_scales(nc.scalar, w_planes[0], w_staged[:])
         sm_rows = keep.tile([P, 4], F32, name="sm_rows")
         nc.sync.dma_start(sm_rows[:], sm.rearrange("(p t) -> p t", t=4))
-
-        ident = keep.tile([P, P], F32, name="ident")
-        make_identity(nc, ident[:])
-        nc.gpsimd.memset(wgo_rows[:], 0.0)
-        nc.gpsimd.dma_start(wgo_rows[0 : J // P, :], wgo[0:1, :].rearrange("o (b p) -> (o b) p", p=P))
-        wd = keep.tile([P, 8 * N], U8, name="wd", tag="staged", align_bytes=64)
-        wd4, wd8, wd_staged = wd[:, 0 : 2 * N], wd[:, 2 * N : 6 * N], wd[:, 6 * N : 8 * N]
-        stage_scales(nc.sync, wd_staged, (wd4_scales, wd8_scales))
-        nc.sync.dma_start(wd4.bitcast(I32), wd4_words[0].bitcast(I32))
-        nc.sync.dma_start(wd8.bitcast(I32), wd8_words[0].rearrange("p n i -> p (n i)").bitcast(I32))
-        spread_scales(nc.sync, w_planes[1], wd_staged)
-
-        wgo_bank = psum.tile([P, 4, P], F32, name="wgo_bank", tag="turned0")
-        nc.tensor.transpose(wgo_bank[:, 0, :], wgo_rows[:], ident[:])
-        wgo_cols = keep.tile([P, J // P], F32, name="wgo_cols")
-        nc.scalar.copy(wgo_cols[:], wgo_bank[:, 0, 0 : J // P])
+        spread_scales(nc.scalar, w_planes[0], w_staged)
 
         def offsets(l, j0, n):
             return lists[l][:, j0 // 16 : (j0 + n) // 16]
 
-        plane_tags = ("pass0_planes0", "first_words")
-        word_tags = (("first_words", "gates0"), ("last_page", "gates3"))
-        pass0_planes, parted = [], []
-        for h in range(2):
-            planes = keep.tile([P, 2 * HALF], U8, name=f"pass0_planes{h}", tag=plane_tags[h], align_bytes=64)
-            for l in range(2):
-                nc.vector.tensor_copy(
-                    planes[:, l * HALF : (l + 1) * HALF], tab_s[:].indirect(offsets(l, h * HALF, HALF))
-                )
-            (nc.scalar, nc.sync)[h].dma_start(
-                pass1_planes[h][:].bitcast(I32)[0 : P - 16, :], planes[:].bitcast(I32)[16:P, :]
-            )
-            picked = [
-                keep.tile([P, HALF], U32, name=f"picked{h}_{l}", tag=word_tags[h][l], align_bytes=64) for l in range(2)
-            ]
-            for l in range(2):
-                nc.vector.tensor_copy(picked[l][:], tab_w[:].bitcast(U32).indirect(offsets(l, h * HALF, HALF)))
-            words = keep.tile([P, 2 * 2 * 2 * HALF], U8, name=f"parted{h}", align_bytes=64)
-            for l in range(2):
-                nc.vector.tensor_copy(
-                    words[:].bitcast(U16)[:, 2 * l * HALF : 2 * (l + 1) * HALF].rearrange("p (a j) -> p a j", a=2),
-                    picked[l][:].bitcast(U16).rearrange("p (j a) -> p a j", a=2),
-                )
-            pass0_planes.append(planes)
-            parted.append(words)
+        pass0_planes = [keep.tile([P, 2 * HALF], U8, name="pass0_planes0", align_bytes=64)]
+        parted = {}
 
-        gates = [keep.tile([P, T], F32, name=f"gates{t}", tag=f"gates{t}", align_bytes=64) for t in range(4)]
+        def pick_scales(h, queue):
+            for l in range(2):
+                nc.vector.tensor_copy(
+                    pass0_planes[h][:, l * HALF : (l + 1) * HALF], tab_s[:].indirect(offsets(l, h * HALF, HALF))
+                )
+            queue.dma_start(
+                pass1_planes[h][:].bitcast(I32)[0 : P - 16, :], pass0_planes[h][:].bitcast(I32)[16:P, :]
+            )
+
+        def pick_words(j0, n, picked):
+            for l in range(2):
+                nc.vector.tensor_copy(picked[l], tab_w[:].bitcast(U32).indirect(offsets(l, j0, n)))
+            words = keep.tile([P, 2 * 2 * 2 * n], U8, name=f"parted{j0}", align_bytes=64)
+            for l in range(2):
+                nc.vector.tensor_copy(
+                    words[:].bitcast(U16)[:, 2 * l * n : 2 * (l + 1) * n].rearrange("p (a j) -> p a j", a=2),
+                    picked[l].bitcast(U16).rearrange("p (j a) -> p a j", a=2),
+                )
+            for c0 in range(0, n, QUARTER):
+                parted[(j0 + c0) // QUARTER] = (words, n, c0)
+
+        pick_scales(0, nc.sync)
+        def place_tile(shape, dtype, name, offset):
+            return placed.tile(shape, dtype, name=name, offset=offset, align_bytes=64)
+
+        for q, starts in enumerate(((1024, 11200), (64, 10240))):
+            pick_words(q * QUARTER, QUARTER, [place_tile([P, QUARTER], U32, f"picked{q}_{l}", starts[l])[:] for l in range(2)])
+
+        wd = place_tile([P, 8 * N], U8, "wd", 1984)
+        wd4, wd8, wd_staged = wd[:, 0 : 2 * N], wd[:, 2 * N : 6 * N], wd[:, 6 * N : 8 * N]
+        stage_scales(nc.sync, wd_staged, (wd4_scales, wd8_scales))
+        nc.sync.dma_start(wd4.bitcast(I32), wd4_words[0].bitcast(I32))
+        nc.sync.dma_start(wd8.bitcast(I32), wd8_words[0].rearrange("p n i -> p (n i)").bitcast(I32))
+        wgo_rows = place_tile([P, P], F32, "wgo_rows", 1088)
+        nc.sync.dma_start(wgo_rows[:], wgo[0 : P * P // J, :].rearrange("r (b p) -> (r b) p", p=P))
         gT_rows = gT.rearrange("(p t) c -> t p c", t=4)
-        for t in range(4):
-            nc.sync.dma_start(gates[t][:], gT_rows[t])
+        gates01 = place_tile([P, 2, T], F32, "gates01", 10752)
+        gates = [gates01[:, 0, :], gates01[:, 1, :]]
+        for t in range(2):
+            nc.sync.dma_start(gates[t], gT_rows[t])
+        spread_scales(nc.sync, w_planes[1], wd_staged)
 
-        wy = [keep.tile([P, 4, HALF], F32, name=f"wy{h}") for h in range(2)]
+        pass0_planes.append(place_tile([P, 2 * HALF], U8, "pass0_planes1", 0))
+        pick_scales(1, nc.sync)
+        picked_half = place_tile([P, 2 * HALF], U32, "picked_half", 6208)
+        pick_words(HALF, HALF, [picked_half[:, l * HALF : (l + 1) * HALF] for l in range(2)])
+        for t in (2, 3):
+            gates.append(keep.tile([P, T], F32, name=f"gates{t}", tag=f"gates{t}", align_bytes=64)[:])
+            nc.sync.dma_start(gates[t], gT_rows[t])
 
-        def first_product(b, tanh_banks):
-            h, j0 = divmod(b * P, HALF)
-            a_bank = psum.tile([P, R], F32, name="a_bank", tag=f"sum{b % 2}")
+        wy = keep.tile([P, 4, J], F32, name="wy")
+        h_codes, h_scales, h_woven = {}, {}, {}
+        a_banks, tanh_a, tanh_banks, h_rows = {}, {}, {}, {}
+        y_banks, wy_edges, wy_banks = {}, {}, {}
+
+        def first_product(q):
+            words, n, c0 = parted[q]
+            h, j0 = divmod(q * QUARTER, HALF)
+            a_banks[q] = psum.tile([P, 2, R], F32, name="a_banks", tag=f"first{q % 2}")
             steps = [(l, a) for a in range(2) for l in range(2)]
-            for i, (l, a) in enumerate(steps):
-                c0 = (2 * l + a) * HALF + j0
-                planes = (pass0_planes, pass1_planes)[a][h]
-                nc.tensor.matmul_mx(
-                    a_bank[:],
-                    lhsT=parted[h][:, 2 * c0 : 2 * (c0 + P)].bitcast(FP4X4),
-                    lhsT_scale=planes[:, l * HALF + j0 : l * HALF + j0 + P],
-                    rhs=w_words[l][:, 2 * a * R : 2 * (a + 1) * R].bitcast(FP4X4),
-                    rhs_scale=w_planes[0][:, (2 * l + a) * R : (2 * l + a + 1) * R],
-                    start=(i == 0),
-                    stop=(i == len(steps) - 1),
+            for b in range(2):
+                for i, (l, a) in enumerate(steps):
+                    col = (2 * l + a) * n + c0 + b * P
+                    planes = (pass0_planes, pass1_planes)[a][h]
+                    pcol = l * HALF + j0 + b * P
+                    nc.tensor.matmul_mx(
+                        a_banks[q][:, b, :],
+                        lhsT=words[:, 2 * col : 2 * (col + P)].bitcast(FP4X4),
+                        lhsT_scale=planes[:, pcol : pcol + P],
+                        rhs=w_words[:, 2 * (2 * l + a) * R : 2 * (2 * l + a + 1) * R].bitcast(FP4X4),
+                        rhs_scale=w_planes[0][:, (2 * l + a) * R : (2 * l + a + 1) * R],
+                        start=(i == 0),
+                        stop=(i == len(steps) - 1),
+                    )
+
+        def tanh_rows(q):
+            for b in range(2):
+                tanh_a[q, b] = ring.tile([P, 4, P], F32, name="tanh_a")
+                nc.scalar.activation(
+                    tanh_a[q, b][:].rearrange("p t m -> p m t"),
+                    a_banks[q][:, b, :].rearrange("p (m t) -> p m t", t=4),
+                    TANH,
                 )
-            tanh_a = ring.tile([P, 4, P], F32, name="tanh_a")
-            nc.scalar.activation(
-                tanh_a[:].rearrange("p t m -> p m t"), a_bank[:].rearrange("p (m t) -> p m t", t=4), TANH
-            )
-            c0 = b * P % QUARTER
-            for t in range(4):
-                nc.tensor.transpose(tanh_banks[:, t, c0 : c0 + P], tanh_a[:, t, :], ident[:])
 
-        def second_product(b, y_bank, turned_tag):
-            q, c0 = divmod(b * P, QUARTER)
-            for i, (w, fmt) in enumerate(((wd4, FP4X4), (wd8, FP8X4))):
-                nc.tensor.matmul_mx(
-                    y_bank,
-                    lhsT=h_codes[q][:, c0 : c0 + P].bitcast(FP8X4),
-                    lhsT_scale=h_scales[q][:, c0 : c0 + P],
-                    rhs=w.bitcast(fmt),
-                    rhs_scale=w_planes[1][:, i * N : (i + 1) * N],
-                    start=(i == 0),
-                    stop=(i == 1),
-                )
-            wy_edges = ring.tile([P, 4, P], F32, name="wy_edges")
-            nc.scalar.activation(
-                wy_edges[:].rearrange("p t m -> p m t"),
-                y_bank.rearrange("p (m t) -> p m t", t=4),
-                COPY,
-                scale=wgo_cols[:, b : b + 1],
-            )
-            wy_bank = psum.tile([P, 4, P], F32, name="wy_bank", tag=turned_tag)
+        def turn_tanh(q):
+            tanh_banks[q] = psum.tile([P, 4, QUARTER], F32, name="tanh_banks", tag=f"first{q % 2}")
             for t in range(4):
-                nc.tensor.transpose(wy_bank[:, t, :], wy_edges[:, t, :], ident[:])
-            h, j0 = divmod(b * P, HALF)
-            nc.scalar.copy(wy[h][:, :, j0 : j0 + P], wy_bank[:])
+                for b in range(2):
+                    nc.tensor.transpose(tanh_banks[q][:, t, b * P : (b + 1) * P], tanh_a[q, b][:, t, :], ident[:])
 
-        h_codes, h_scales = [], []
-
-        def hidden(q):
-            h_woven = keep.tile([P, 4 * QUARTER], BF16, name=f"h_woven{q}", tag=f"h_woven{q}", align_bytes=64)
-            tanh_banks = psum.tile([P, 4, QUARTER], F32, name="tanh_banks", tag=f"pair{q % 2}")
-            for b in (2 * q, 2 * q + 1):
-                first_product(b, tanh_banks)
-            h_rows = ring.tile([P, 4, QUARTER], BF16, name="h_rows")
+        def scale_rows(q):
+            h_rows[q] = ring.tile([P, 4, QUARTER], BF16, name="h_rows")
             for t in range(4):
-                nc.scalar.activation(h_rows[:, t, :], tanh_banks[:, t, :], COPY, scale=sm_rows[:, t : t + 1])
+                nc.scalar.activation(h_rows[q][:, t, :], tanh_banks[q][:, t, :], COPY, scale=sm_rows[:, t : t + 1])
+
+        def weave_h(q):
+            h_woven[q] = keep.tile([P, 4 * QUARTER], BF16, name=f"h_woven{q}", tag=f"h_woven{q}", align_bytes=64)
             nc.scalar.copy(
-                h_woven[:].rearrange("p (c i t) -> p c t i", i=4, t=4),
-                h_rows[:].rearrange("p t (c i) -> p c t i", i=4),
+                h_woven[q][:].rearrange("p (c i t) -> p c t i", i=4, t=4),
+                h_rows[q][:].rearrange("p t (c i) -> p c t i", i=4),
             )
-            h_codes.append(keep.tile([P, QUARTER], U32, name=f"h_codes{q}", align_bytes=64))
-            h_scales.append(keep.tile([P, QUARTER], U8, name=f"h_scales{q}", align_bytes=64))
-            nc.vector.quantize_mx(h_codes[q][:].bitcast(FP8X4), h_scales[q][:], h_woven[:])
+            h_codes[q] = keep.tile([P, QUARTER], U32, name=f"h_codes{q}", align_bytes=64)
+            h_scales[q] = keep.tile([P, QUARTER], U8, name=f"h_scales{q}", align_bytes=64)
+            nc.vector.quantize_mx(h_codes[q][:].bitcast(FP8X4), h_scales[q][:], h_woven[q][:])
 
-        def message(q):
-            if q < 3:
-                pair = psum.tile([P, 2, N], F32, name="y_banks", tag=f"pair{(q + 1) % 2}")
-                y_banks = [pair[:, i, :] for i in range(2)]
-                turned_tags = ("turned0", "turned1")
-            else:
-                y_banks = [psum.tile([P, N], F32, name="y_bank", tag=f"turned{i}")[:] for i in range(2)]
-                turned_tags = ("sum0", "sum1")
-            for i in range(2):
-                second_product(2 * q + i, y_banks[i], turned_tags[i])
+        def second_product(q, tag):
+            y_banks[q] = psum.tile([P, 2, N], F32, name="y_banks", tag=tag)
+            for b in range(2):
+                for i, (w, fmt) in enumerate(((wd4, FP4X4), (wd8, FP8X4))):
+                    nc.tensor.matmul_mx(
+                        y_banks[q][:, b, :],
+                        lhsT=h_codes[q][:, b * P : (b + 1) * P].bitcast(FP8X4),
+                        lhsT_scale=h_scales[q][:, b * P : (b + 1) * P],
+                        rhs=w.bitcast(fmt),
+                        rhs_scale=w_planes[1][:, i * N : (i + 1) * N],
+                        start=(i == 0),
+                        stop=(i == 1),
+                    )
 
-        hidden(0)
-        for q in range(1, 4):
-            hidden(q)
-            message(q - 1)
-        message(3)
+        def weigh(q):
+            for b in range(2):
+                wy_edges[q, b] = ring.tile([P, 4, P], F32, name="wy_edges")
+                nc.scalar.activation(
+                    wy_edges[q, b][:].rearrange("p t m -> p m t"),
+                    y_banks[q][:, b, :].rearrange("p (m t) -> p m t", t=4),
+                    COPY,
+                    scale=wgo_cols[:, 2 * q + b : 2 * q + b + 1],
+                )
 
-        pages.append(keep.tile([P, T], F32, name="page3", tag="last_page", align_bytes=64))
-        nc.vector.memset(pages[HEAD_PAGES][:].bitcast(I32), 0)
+        def turn_wy(q, tag):
+            wy_banks[q] = psum.tile([P, 2, 4, P], F32, name="wy_banks", tag=tag)
+            for b in range(2):
+                for t in range(4):
+                    nc.tensor.transpose(wy_banks[q][:, b, t, :], wy_edges[q, b][:, t, :], ident[:])
+
+        def copy_wy(q):
+            for b in range(2):
+                j0 = q * QUARTER + b * P
+                nc.scalar.copy(wy[:, :, j0 : j0 + P], wy_banks[q][:, b, :, :])
 
         picked_gates = {}
 
-        def pick_gates(j0, n, rows, tag):
-            picked = keep.tile([P, len(rows), n], F32, name=f"g{j0}_{rows[0]}", tag=tag, align_bytes=64)
-            for k, t in enumerate(rows):
-                nc.vector.tensor_copy(picked[:, k, :], gates[t][:].indirect(offsets(0, j0, n)))
+        def pick_gates(tag, jobs):
+            picked = keep.tile([P, sum(n for t, j0, n in jobs)], F32, name=f"g_{tag}", tag=tag, align_bytes=64)
+            col = 0
+            for t, j0, n in jobs:
+                nc.vector.tensor_copy(picked[:, col : col + n], gates[t].indirect(offsets(0, j0, n)))
                 for c0 in range(0, n, QUARTER):
-                    picked_gates[j0 + c0, t] = picked[:, k, c0:n]
+                    picked_gates[j0 + c0, t] = picked[:, col + c0 : col + n]
+                col = col + n
 
         out_rows = out_0.rearrange("(p t) c -> t p c", t=4)
         n_pieces = T // PIECE
         rounded = [keep.tile([P, 2, PIECE, 2], BF16, name=f"rounded{c}") for c in range(n_pieces)]
 
         def place(j0, n, t):
-            h, c0 = divmod(j0, HALF)
             nc.vector.tensor_tensor(
-                pages[t][:].indirect(offsets(1, j0, n)), wy[h][:, t, c0 : c0 + n], picked_gates[j0, t][:, 0:n], MULT
+                pages[t][:].indirect(offsets(1, j0, n)), wy[:, t, j0 : j0 + n], picked_gates[j0, t][:, 0:n], MULT
             )
             if j0 + n == J:
                 nc.sync.dma_start(out_rows[t], pages[t][:])
                 for c in range(n_pieces):
                     nc.scalar.copy(rounded[c][:, t // 2, :, t % 2], pages[t][:, c * PIECE : (c + 1) * PIECE])
 
-        pick_gates(0, HALF, (0, 1), "g_low_rows")
-        pick_gates(0, QUARTER, (2, 3), "g_high_rows")
-        pick_gates(QUARTER, QUARTER, (2, 3), "h_woven3")
-        pick_gates(HALF, HALF, (0, 1, 2, 3), "g_second_half")
-        for q in range(2):
-            for t in range(4):
-                place(q * QUARTER, QUARTER, t)
+        first_product(0)
+        tanh_rows(0)
+        turn_tanh(0)
+        first_product(1)
+        pick_gates("gates_row0", [(0, 0, J)])
+        scale_rows(0)
+        weave_h(0)
+        pick_gates("h_woven0", [(1, 0, J)])
+        wgo_bank = psum.tile([P, 2, N], F32, name="wgo_bank", tag="second1")
+        nc.tensor.transpose(wgo_bank[:, 0, 0:P], wgo_rows[:], ident[:])
+        wgo_cols = keep.tile([P, J // P], F32, name="wgo_cols")
+        nc.scalar.copy(wgo_cols[:], wgo_bank[:, 0, 0 : J // P])
+        for q in range(1, 4):
+            tanh_rows(q)
+            turn_tanh(q)
+            if q < 3:
+                first_product(q + 1)
+            if q > 1:
+                copy_wy(q - 2)
+                for t in range(3):
+                    place((q - 2) * QUARTER, QUARTER, t)
+            second_product(q - 1, "second0")
+            scale_rows(q)
+            weigh(q - 1)
+            turn_wy(q - 1, "second0")
+            weave_h(q)
+            if q == 1:
+                pick_gates("h_woven1", [(2, 0, J), (3, 0, J)])
+        pages.append(keep.tile([P, T], F32, name="page3", tag="h_woven2", align_bytes=64))
+        nc.gpsimd.memset(pages[3][:].bitcast(I32), 0)
+        copy_wy(2)
+        second_product(3, "second1")
+        weigh(3)
+        turn_wy(3, "second1")
+        copy_wy(3)
         for q in (2, 3):
-            place(q * QUARTER, QUARTER, 0)
-        for t in range(1, 4):
-            place(HALF, HALF, t)
+            for t in range(3):
+                place(q * QUARTER, QUARTER, t)
+        place(0, J, 3)
 
         out_plane = keep.tile([P, T], U8, name="out_plane", align_bytes=64)
         out_words = out_1[0].rearrange("p t i -> p (t i)").bitcast(I32)

@@ -42,17 +42,14 @@ def tile_list_msg_tanh_res_gateP_kernel(
         lists = [keep.tile([P, J // 16], U16, name=f"list{l}") for l in range(2)]
         tab_w = keep.tile([P, T], I32, name="tab_w", tag="gates3", align_bytes=64)
         tab_s = keep.tile([P, T], U8, name="tab_s", tag="gates2", align_bytes=64)
-        w_planes = [keep.tile([P, n * R], U8, name=f"w_planes{i}", align_bytes=64) for i, n in enumerate((4, 2))]
-        pass1_planes = [keep.tile([P, 2 * HALF], U8, name=f"pass1_planes{h}", align_bytes=64) for h in range(2)]
+        planes = keep.tile([P, 6 * R + 2 * J], U8, name="planes", align_bytes=64)
+        w_planes = [planes[:, 0 : 4 * R], planes[:, 4 * R : 6 * R]]
+        pass1_planes = [planes[:, 6 * R + 2 * HALF * h : 6 * R + 2 * HALF * (h + 1)] for h in range(2)]
 
         nc.vector.memset(tab_s[:].bitcast(I32), 0)
-        nc.vector.memset(w_planes[0][:].bitcast(I32), 0)
-        nc.vector.memset(pass1_planes[0][:].bitcast(I32), 0)
-        pages = [keep.tile([P, T], F32, name=f"page{t}") for t in range(3)]
-        for t in range(3):
-            nc.vector.memset(pages[t][:].bitcast(I32), 0)
-        nc.vector.memset(pass1_planes[1][:].bitcast(I32), 0)
-        nc.vector.memset(w_planes[1][:].bitcast(I32), 0)
+        nc.vector.memset(planes[:].bitcast(I32), 0)
+        pages = [keep.tile([P, T], F32, name=f"page{t}") for t in range(1)]
+        nc.vector.memset(pages[0][:].bitcast(I32), 0)
 
         def stage_scales(queue, staged, sources):
             words = staged.bitcast(I32)
@@ -66,10 +63,10 @@ def tile_list_msg_tanh_res_gateP_kernel(
                 )
                 col = col + width
 
-        def spread_scales(queue, planes, staged):
+        def spread_scales(queue, spread, staged):
             for quad in range(4):
                 queue.dma_start(
-                    planes[:].bitcast(I32)[32 * quad : 32 * quad + 4, :],
+                    spread.bitcast(I32)[32 * quad : 32 * quad + 4, :],
                     staged.bitcast(I32)[4 * quad : 4 * quad + 4, :],
                 )
 
@@ -92,6 +89,8 @@ def tile_list_msg_tanh_res_gateP_kernel(
         sm_rows = keep.tile([P, 4], F32, name="sm_rows")
         nc.sync.dma_start(sm_rows[:], sm.rearrange("(p t) -> p t", t=4))
         spread_scales(nc.scalar, w_planes[0], w_staged)
+        wgo_rows = keep.tile([P, P], F32, name="wgo_rows")
+        nc.sync.dma_start(wgo_rows[:], wgo[0 : P * P // J, :].rearrange("r (b p) -> (r b) p", p=P))
 
         def offsets(l, j0, n):
             return lists[l][:, j0 // 16 : (j0 + n) // 16]
@@ -105,7 +104,7 @@ def tile_list_msg_tanh_res_gateP_kernel(
                     pass0_planes[h][:, l * HALF : (l + 1) * HALF], tab_s[:].indirect(offsets(l, h * HALF, HALF))
                 )
             queue.dma_start(
-                pass1_planes[h][:].bitcast(I32)[0 : P - 16, :], pass0_planes[h][:].bitcast(I32)[16:P, :]
+                pass1_planes[h].bitcast(I32)[0 : P - 16, :], pass0_planes[h][:].bitcast(I32)[16:P, :]
             )
 
         def pick_words(j0, n, picked):
@@ -124,7 +123,7 @@ def tile_list_msg_tanh_res_gateP_kernel(
         def place_tile(shape, dtype, name, offset):
             return placed.tile(shape, dtype, name=name, offset=offset, align_bytes=64)
 
-        for q, starts in enumerate(((1024, 11200), (64, 10240))):
+        for q, starts in enumerate(((1024, 11200 + 8192), (64, 10240 + 8192))):
             pick_words(q * QUARTER, QUARTER, [place_tile([P, QUARTER], U32, f"picked{q}_{l}", starts[l])[:] for l in range(2)])
 
         wd = place_tile([P, 8 * N], U8, "wd", 1984)
@@ -132,10 +131,8 @@ def tile_list_msg_tanh_res_gateP_kernel(
         stage_scales(nc.sync, wd_staged, (wd4_scales, wd8_scales))
         nc.sync.dma_start(wd4.bitcast(I32), wd4_words[0].bitcast(I32))
         nc.sync.dma_start(wd8.bitcast(I32), wd8_words[0].rearrange("p n i -> p (n i)").bitcast(I32))
-        wgo_rows = place_tile([P, P], F32, "wgo_rows", 1088)
-        nc.sync.dma_start(wgo_rows[:], wgo[0 : P * P // J, :].rearrange("r (b p) -> (r b) p", p=P))
         gT_rows = gT.rearrange("(p t) c -> t p c", t=4)
-        gates01 = place_tile([P, 2, T], F32, "gates01", 10752)
+        gates01 = place_tile([P, 2, T], F32, "gates01", 10752 + 8192)
         gates = [gates01[:, 0, :], gates01[:, 1, :]]
         for t in range(2):
             nc.sync.dma_start(gates[t], gT_rows[t])
@@ -143,7 +140,7 @@ def tile_list_msg_tanh_res_gateP_kernel(
 
         pass0_planes.append(place_tile([P, 2 * HALF], U8, "pass0_planes1", 0))
         pick_scales(1, nc.sync)
-        picked_half = place_tile([P, 2 * HALF], U32, "picked_half", 6208)
+        picked_half = place_tile([P, 2 * HALF], U32, "picked_half", 6208 + 8192)
         pick_words(HALF, HALF, [picked_half[:, l * HALF : (l + 1) * HALF] for l in range(2)])
         for t in (2, 3):
             gates.append(keep.tile([P, T], F32, name=f"gates{t}", tag=f"gates{t}", align_bytes=64)[:])
@@ -157,17 +154,17 @@ def tile_list_msg_tanh_res_gateP_kernel(
         def first_product(q):
             words, n, c0 = parted[q]
             h, j0 = divmod(q * QUARTER, HALF)
-            a_banks[q] = psum.tile([P, 2, R], F32, name="a_banks", tag=f"first{q % 2}")
-            steps = [(l, a) for a in range(2) for l in range(2)]
+            steps = [(l, a) for a in (1, 0) for l in range(2)]
             for b in range(2):
+                a_banks[q, b] = psum.tile([P, R], F32, name="a_bank", tag=f"bank{2 * (q % 2) + b}")
                 for i, (l, a) in enumerate(steps):
                     col = (2 * l + a) * n + c0 + b * P
-                    planes = (pass0_planes, pass1_planes)[a][h]
+                    edge_planes = (pass0_planes, pass1_planes)[a][h]
                     pcol = l * HALF + j0 + b * P
                     nc.tensor.matmul_mx(
-                        a_banks[q][:, b, :],
+                        a_banks[q, b][:],
                         lhsT=words[:, 2 * col : 2 * (col + P)].bitcast(FP4X4),
-                        lhsT_scale=planes[:, pcol : pcol + P],
+                        lhsT_scale=edge_planes[:, pcol : pcol + P],
                         rhs=w_words[:, 2 * (2 * l + a) * R : 2 * (2 * l + a + 1) * R].bitcast(FP4X4),
                         rhs_scale=w_planes[0][:, (2 * l + a) * R : (2 * l + a + 1) * R],
                         start=(i == 0),
@@ -178,24 +175,29 @@ def tile_list_msg_tanh_res_gateP_kernel(
             for b in range(2):
                 tanh_a[q, b] = ring.tile([P, 4, P], F32, name="tanh_a")
                 nc.scalar.activation(
-                    tanh_a[q, b][:].rearrange("p t m -> p m t"),
-                    a_banks[q][:, b, :].rearrange("p (m t) -> p m t", t=4),
+                    tanh_a[q, b][:],
+                    a_banks[q, b][:].rearrange("p (m t) -> p t m", t=4),
                     TANH,
                 )
 
         def turn_tanh(q):
-            tanh_banks[q] = psum.tile([P, 4, QUARTER], F32, name="tanh_banks", tag=f"first{q % 2}")
-            for t in range(4):
-                for b in range(2):
-                    nc.tensor.transpose(tanh_banks[q][:, t, b * P : (b + 1) * P], tanh_a[q, b][:, t, :], ident[:])
+            for u in range(2):
+                bank = psum.tile([P, 2, QUARTER], F32, name="tanh_bank", tag=f"bank{2 * (q % 2) + u}")
+                for e in range(2):
+                    tanh_banks[q, 2 * u + e] = bank[:, e, :]
+                    for b in range(2):
+                        nc.tensor.transpose(bank[:, e, b * P : (b + 1) * P], tanh_a[q, b][:, 2 * u + e, :], ident[:])
 
         def scale_rows(q):
             h_rows[q] = ring.tile([P, 4, QUARTER], BF16, name="h_rows")
             for t in range(4):
-                nc.scalar.activation(h_rows[q][:, t, :], tanh_banks[q][:, t, :], COPY, scale=sm_rows[:, t : t + 1])
+                nc.scalar.activation(h_rows[q][:, t, :], tanh_banks[q, t], COPY, scale=sm_rows[:, t : t + 1])
 
         def weave_h(q):
-            h_woven[q] = keep.tile([P, 4 * QUARTER], BF16, name=f"h_woven{q}", tag=f"h_woven{q}", align_bytes=64)
+            if q < 3:
+                h_woven[q] = keep.tile([P, 4 * QUARTER], BF16, name=f"h_woven{q}", tag=f"h_woven{q}", align_bytes=64)
+            else:
+                h_woven[q] = place_tile([P, 4 * QUARTER], BF16, "h_woven3", 35328 + 8128)
             nc.scalar.copy(
                 h_woven[q][:].rearrange("p (c i t) -> p c t i", i=4, t=4),
                 h_rows[q][:].rearrange("p t (c i) -> p c t i", i=4),
@@ -204,12 +206,12 @@ def tile_list_msg_tanh_res_gateP_kernel(
             h_scales[q] = keep.tile([P, QUARTER], U8, name=f"h_scales{q}", align_bytes=64)
             nc.vector.quantize_mx(h_codes[q][:].bitcast(FP8X4), h_scales[q][:], h_woven[q][:])
 
-        def second_product(q, tag):
-            y_banks[q] = psum.tile([P, 2, N], F32, name="y_banks", tag=tag)
+        def second_product(q, first_bank):
             for b in range(2):
+                y_banks[q, b] = psum.tile([P, N], F32, name="y_bank", tag=f"bank{first_bank + b}")
                 for i, (w, fmt) in enumerate(((wd4, FP4X4), (wd8, FP8X4))):
                     nc.tensor.matmul_mx(
-                        y_banks[q][:, b, :],
+                        y_banks[q, b][:],
                         lhsT=h_codes[q][:, b * P : (b + 1) * P].bitcast(FP8X4),
                         lhsT_scale=h_scales[q][:, b * P : (b + 1) * P],
                         rhs=w.bitcast(fmt),
@@ -222,22 +224,22 @@ def tile_list_msg_tanh_res_gateP_kernel(
             for b in range(2):
                 wy_edges[q, b] = ring.tile([P, 4, P], F32, name="wy_edges")
                 nc.scalar.activation(
-                    wy_edges[q, b][:].rearrange("p t m -> p m t"),
-                    y_banks[q][:, b, :].rearrange("p (m t) -> p m t", t=4),
+                    wy_edges[q, b][:],
+                    y_banks[q, b][:].rearrange("p (m t) -> p t m", t=4),
                     COPY,
                     scale=wgo_cols[:, 2 * q + b : 2 * q + b + 1],
                 )
 
-        def turn_wy(q, tag):
-            wy_banks[q] = psum.tile([P, 2, 4, P], F32, name="wy_banks", tag=tag)
+        def turn_wy(q, first_bank):
             for b in range(2):
+                wy_banks[q, b] = psum.tile([P, 4, P], F32, name="wy_bank", tag=f"bank{first_bank + b}")
                 for t in range(4):
-                    nc.tensor.transpose(wy_banks[q][:, b, t, :], wy_edges[q, b][:, t, :], ident[:])
+                    nc.tensor.transpose(wy_banks[q, b][:, t, :], wy_edges[q, b][:, t, :], ident[:])
 
         def copy_wy(q):
             for b in range(2):
                 j0 = q * QUARTER + b * P
-                nc.scalar.copy(wy[:, :, j0 : j0 + P], wy_banks[q][:, b, :, :])
+                nc.scalar.copy(wy[:, :, j0 : j0 + P], wy_banks[q, b][:])
 
         picked_gates = {}
 
@@ -263,18 +265,19 @@ def tile_list_msg_tanh_res_gateP_kernel(
                 for c in range(n_pieces):
                     nc.scalar.copy(rounded[c][:, t // 2, :, t % 2], pages[t][:, c * PIECE : (c + 1) * PIECE])
 
+        wgo_bank = psum.tile([P, N], F32, name="wgo_bank", tag="bank6")
+        nc.tensor.transpose(wgo_bank[:, 0:P], wgo_rows[:], ident[:])
+        wgo_cols = keep.tile([P, J // P], F32, name="wgo_cols")
+        nc.scalar.copy(wgo_cols[:], wgo_bank[:, 0 : J // P])
         first_product(0)
         tanh_rows(0)
         turn_tanh(0)
         first_product(1)
-        pick_gates("gates_row0", [(0, 0, J)])
+        pages.append(place_tile([P, T], F32, "page1", 6272))
+        nc.vector.memset(pages[1][:].bitcast(I32), 0)
         scale_rows(0)
         weave_h(0)
-        pick_gates("h_woven0", [(1, 0, J)])
-        wgo_bank = psum.tile([P, 2, N], F32, name="wgo_bank", tag="second1")
-        nc.tensor.transpose(wgo_bank[:, 0, 0:P], wgo_rows[:], ident[:])
-        wgo_cols = keep.tile([P, J // P], F32, name="wgo_cols")
-        nc.scalar.copy(wgo_cols[:], wgo_bank[:, 0, 0 : J // P])
+        pick_gates("h_woven0", [(0, 0, J), (1, 0, J)])
         for q in range(1, 4):
             tanh_rows(q)
             turn_tanh(q)
@@ -282,25 +285,29 @@ def tile_list_msg_tanh_res_gateP_kernel(
                 first_product(q + 1)
             if q > 1:
                 copy_wy(q - 2)
-                for t in range(3):
+                for t in range(2):
                     place((q - 2) * QUARTER, QUARTER, t)
-            second_product(q - 1, "second0")
+            second_product(q - 1, 4)
             scale_rows(q)
             weigh(q - 1)
-            turn_wy(q - 1, "second0")
+            turn_wy(q - 1, 4)
             weave_h(q)
             if q == 1:
-                pick_gates("h_woven1", [(2, 0, J), (3, 0, J)])
-        pages.append(keep.tile([P, T], F32, name="page3", tag="h_woven2", align_bytes=64))
-        nc.gpsimd.memset(pages[3][:].bitcast(I32), 0)
+                pick_gates("h_woven1", [(2, 0, J)])
+            if q == 2:
+                pick_gates("h_woven2", [(3, 0, J)])
+        for t, start in ((2, 35328), (3, 35328 + 10112)):
+            pages.append(place_tile([P, T], F32, f"page{t}", start))
+            nc.gpsimd.memset(pages[t][:].bitcast(I32), 0)
         copy_wy(2)
-        second_product(3, "second1")
+        second_product(3, 6)
         weigh(3)
-        turn_wy(3, "second1")
+        turn_wy(3, 6)
         copy_wy(3)
         for q in (2, 3):
-            for t in range(3):
+            for t in range(2):
                 place(q * QUARTER, QUARTER, t)
+            place((q - 2) * HALF, HALF, 2)
         place(0, J, 3)
 
         out_plane = keep.tile([P, T], U8, name="out_plane", align_bytes=64)

@@ -22,6 +22,7 @@ P = 128
 HALF = J // 2
 QUARTER = J // 4
 SCALE_ROWS = 16
+Y_BANKS = (4, 4, 6, 4)
 STORE_COLS = 512
 PIECE = 256
 VECTOR_PIECES = 6
@@ -92,6 +93,18 @@ def tile_list_msg_tanh_res_gateP_kernel(
         wgo_rows = keep.tile([P, P], F32, name="wgo_rows")
         nc.sync.dma_start(wgo_rows[:], wgo[0 : P * P // J, :].rearrange("r (b p) -> (r b) p", p=P))
 
+        warm_bank = psum.tile([P, N], F32, name="warm_bank", tag="bank7")
+        for i in range(4):
+            nc.tensor.matmul_mx(
+                warm_bank[:],
+                lhsT=w_words[:, 0 : 2 * P].bitcast(FP4X4),
+                lhsT_scale=w_planes[1][:, 0:P],
+                rhs=w_words[:, 0 : 2 * R].bitcast(FP4X4),
+                rhs_scale=w_planes[1][:, 0:R],
+                start=True,
+                stop=True,
+            )
+
         def offsets(l, j0, n):
             return lists[l][:, j0 // 16 : (j0 + n) // 16]
 
@@ -133,8 +146,8 @@ def tile_list_msg_tanh_res_gateP_kernel(
         nc.sync.dma_start(wd8.bitcast(I32), wd8_words[0].rearrange("p n i -> p (n i)").bitcast(I32))
         gT_rows = gT.rearrange("(p t) c -> t p c", t=4)
         gates01 = place_tile([P, 2, T], F32, "gates01", 10752 + 8192)
-        gates = [gates01[:, 0, :], gates01[:, 1, :]]
-        for t in range(2):
+        gates = {0: gates01[:, 0, :], 2: gates01[:, 1, :]}
+        for t in (0, 2):
             nc.sync.dma_start(gates[t], gT_rows[t])
         spread_scales(nc.sync, w_planes[1], wd_staged)
 
@@ -142,8 +155,8 @@ def tile_list_msg_tanh_res_gateP_kernel(
         pick_scales(1, nc.sync)
         picked_half = place_tile([P, 2 * HALF], U32, "picked_half", 6208 + 8192)
         pick_words(HALF, HALF, [picked_half[:, l * HALF : (l + 1) * HALF] for l in range(2)])
-        for t in (2, 3):
-            gates.append(keep.tile([P, T], F32, name=f"gates{t}", tag=f"gates{t}", align_bytes=64)[:])
+        for t, tag in ((3, "gates2"), (1, "gates3")):
+            gates[t] = keep.tile([P, T], F32, name=f"gates{t}", tag=tag, align_bytes=64)[:]
             nc.sync.dma_start(gates[t], gT_rows[t])
 
         wy = keep.tile([P, 4, J], F32, name="wy")
@@ -154,7 +167,7 @@ def tile_list_msg_tanh_res_gateP_kernel(
         def first_product(q):
             words, n, c0 = parted[q]
             h, j0 = divmod(q * QUARTER, HALF)
-            steps = [(l, a) for a in (1, 0) for l in range(2)]
+            steps = [(l, a) for a in ((0, 1) if q == 0 else (1, 0)) for l in range(2)]
             for b in range(2):
                 a_banks[q, b] = psum.tile([P, R], F32, name="a_bank", tag=f"bank{2 * (q % 2) + b}")
                 for i, (l, a) in enumerate(steps):
@@ -273,11 +286,10 @@ def tile_list_msg_tanh_res_gateP_kernel(
         tanh_rows(0)
         turn_tanh(0)
         first_product(1)
-        pages.append(place_tile([P, T], F32, "page1", 6272))
-        nc.vector.memset(pages[1][:].bitcast(I32), 0)
+        pick_gates("gates_row0", [(0, 0, J)])
         scale_rows(0)
         weave_h(0)
-        pick_gates("h_woven0", [(0, 0, J), (1, 0, J)])
+        pick_gates("h_woven0", [(2, 0, J)])
         for q in range(1, 4):
             tanh_rows(q)
             turn_tanh(q)
@@ -285,29 +297,32 @@ def tile_list_msg_tanh_res_gateP_kernel(
                 first_product(q + 1)
             if q > 1:
                 copy_wy(q - 2)
-                for t in range(2):
+                for t in range(q - 1):
                     place((q - 2) * QUARTER, QUARTER, t)
-            second_product(q - 1, 4)
+            second_product(q - 1, Y_BANKS[q - 1])
             scale_rows(q)
             weigh(q - 1)
-            turn_wy(q - 1, 4)
+            turn_wy(q - 1, Y_BANKS[q - 1])
             weave_h(q)
             if q == 1:
-                pick_gates("h_woven1", [(2, 0, J)])
+                pick_gates("h_woven1", [(3, 0, J)])
+                pages.append(keep.tile([P, T], F32, name="page1", tag="gates2", align_bytes=64))
+                nc.gpsimd.memset(pages[1][:].bitcast(I32), 0)
             if q == 2:
-                pick_gates("h_woven2", [(3, 0, J)])
+                pick_gates("h_woven2", [(1, 0, J)])
+                place(0, QUARTER, 1)
         for t, start in ((2, 35328), (3, 35328 + 10112)):
             pages.append(place_tile([P, T], F32, f"page{t}", start))
             nc.gpsimd.memset(pages[t][:].bitcast(I32), 0)
         copy_wy(2)
-        second_product(3, 6)
+        second_product(3, Y_BANKS[3])
         weigh(3)
-        turn_wy(3, 6)
+        turn_wy(3, Y_BANKS[3])
         copy_wy(3)
         for q in (2, 3):
             for t in range(2):
                 place(q * QUARTER, QUARTER, t)
-            place((q - 2) * HALF, HALF, 2)
+            place(*((0, QUARTER), (QUARTER, 3 * QUARTER))[q - 2], 2)
         place(0, J, 3)
 
         out_plane = keep.tile([P, T], U8, name="out_plane", align_bytes=64)

@@ -79,8 +79,8 @@ def tile_list_msg_tanh_res_gateP_kernel(
         for r in range(4):
             nc.sync.dma_start(tab_s[:].bitcast(I32)[r:P:16, :], tab_s_rows[r])
         nc.sync.dma_start(lists[1][:], offs2)
-        nc.sync.dma_start(tab_w[:], tab_words[0].rearrange("p t b -> p (t b)").bitcast(I32))
         stage_scales(nc.sync, w_staged, (ws_scales, wt_scales))
+        nc.sync.dma_start(tab_w[:], tab_words[0].rearrange("p t b -> p (t b)").bitcast(I32))
         w_words = keep.tile([P, 8 * R], U8, name="w_words", align_bytes=64)
         for l, words in enumerate((ws_words, wt_words)):
             nc.sync.dma_start(
@@ -202,15 +202,12 @@ def tile_list_msg_tanh_res_gateP_kernel(
                         nc.tensor.transpose(bank[:, e, b * P : (b + 1) * P], tanh_a[q, b][:, 2 * u + e, :], ident[:])
 
         def scale_rows(q):
-            h_rows[q] = ring.tile([P, 4, QUARTER], BF16, name="h_rows")
+            h_rows[q] = keep.tile([P, 4, QUARTER], BF16, name=f"h_rows{q}", tag=f"h_rows{q}", align_bytes=64)
             for t in range(4):
                 nc.scalar.activation(h_rows[q][:, t, :], tanh_banks[q, t], COPY, scale=sm_rows[:, t : t + 1])
 
         def weave_h(q):
-            if q < 3:
-                h_woven[q] = keep.tile([P, 4 * QUARTER], BF16, name=f"h_woven{q}", tag=f"h_woven{q}", align_bytes=64)
-            else:
-                h_woven[q] = place_tile([P, 4 * QUARTER], BF16, "h_woven3", 35328 + 8128)
+            h_woven[q] = keep.tile([P, 4 * QUARTER], BF16, name=f"h_woven{q}", tag=f"h_woven{q}", align_bytes=64)
             nc.scalar.copy(
                 h_woven[q][:].rearrange("p (c i t) -> p c t i", i=4, t=4),
                 h_rows[q][:].rearrange("p t (c i) -> p c t i", i=4),
@@ -289,7 +286,7 @@ def tile_list_msg_tanh_res_gateP_kernel(
         pick_gates("gates_row0", [(0, 0, J)])
         scale_rows(0)
         weave_h(0)
-        pick_gates("h_woven0", [(2, 0, J)])
+        pick_gates("h_rows0", [(2, 0, J)])
         for q in range(1, 4):
             tanh_rows(q)
             turn_tanh(q)
@@ -305,15 +302,15 @@ def tile_list_msg_tanh_res_gateP_kernel(
             turn_wy(q - 1, Y_BANKS[q - 1])
             weave_h(q)
             if q == 1:
-                pick_gates("h_woven1", [(3, 0, J)])
+                pick_gates("h_rows1", [(3, 0, J)])
                 pages.append(keep.tile([P, T], F32, name="page1", tag="gates2", align_bytes=64))
-                nc.gpsimd.memset(pages[1][:].bitcast(I32), 0)
+                nc.vector.memset(pages[1][:].bitcast(I32), 0)
             if q == 2:
-                pick_gates("h_woven2", [(1, 0, J)])
+                pick_gates("h_rows2", [(1, 0, J)])
                 place(0, QUARTER, 1)
-        for t, start in ((2, 35328), (3, 35328 + 10112)):
-            pages.append(place_tile([P, T], F32, f"page{t}", start))
-            nc.gpsimd.memset(pages[t][:].bitcast(I32), 0)
+        pages.append(keep.tile([P, T], F32, name="page2", tag="h_woven3", align_bytes=64))
+        nc.gpsimd.memset(pages[2][:].bitcast(I32), 0)
+        pages.append(pages[0])
         copy_wy(2)
         second_product(3, Y_BANKS[3])
         weigh(3)

@@ -93,18 +93,6 @@ def tile_list_msg_tanh_res_gateP_kernel(
         wgo_rows = keep.tile([P, P], F32, name="wgo_rows")
         nc.sync.dma_start(wgo_rows[:], wgo[0 : P * P // J, :].rearrange("r (b p) -> (r b) p", p=P))
 
-        warm_bank = psum.tile([P, N], F32, name="warm_bank", tag="bank7")
-        for i in range(4):
-            nc.tensor.matmul_mx(
-                warm_bank[:],
-                lhsT=w_words[:, 0 : 2 * P].bitcast(FP4X4),
-                lhsT_scale=w_planes[1][:, 0:P],
-                rhs=w_words[:, 0 : 2 * R].bitcast(FP4X4),
-                rhs_scale=w_planes[1][:, 0:R],
-                start=True,
-                stop=True,
-            )
-
         def offsets(l, j0, n):
             return lists[l][:, j0 // 16 : (j0 + n) // 16]
 

@@ -22,10 +22,22 @@ P = 128
 HALF = J // 2
 QUARTER = J // 4
 SCALE_ROWS = 16
-Y_BANKS = (4, 4, 6, 4)
 STORE_COLS = 512
 PIECE = 256
 VECTOR_PIECES = 6
+Y_BANKS = (4, 4, 6, 4)
+
+UNIT = 64
+WORDS = 4 * QUARTER
+AT_WORDS00 = WORDS
+AT_WORDS10 = UNIT
+AT_PLANES1 = 0
+AT_SM = AT_WORDS10 + WORDS
+AT_WD = AT_WORDS00 + WORDS - UNIT
+AT_WORDS_HALF = AT_WD + 8 * N
+AT_WORDS11 = AT_WORDS_HALF + 4 * WORDS - UNIT
+AT_WORDS01 = AT_WORDS11 + WORDS - UNIT
+AT_GATES = AT_WORDS11 + UNIT
 
 
 def tile_list_msg_tanh_res_gateP_kernel(
@@ -40,25 +52,28 @@ def tile_list_msg_tanh_res_gateP_kernel(
         ring = ctx.enter_context(tc.tile_pool(name="ring", bufs=4))
         psum = ctx.enter_context(tc.psum_pool(name="psum", bufs=1))
 
+        def place_tile(shape, dtype, name, offset):
+            return placed.tile(shape, dtype, name=name, offset=offset, align_bytes=UNIT)
+
         lists = [keep.tile([P, J // 16], U16, name=f"list{l}") for l in range(2)]
-        tab_w = keep.tile([P, T], I32, name="tab_w", tag="gates3", align_bytes=64)
-        tab_s = keep.tile([P, T], U8, name="tab_s", tag="gates2", align_bytes=64)
+        tab_w = keep.tile([P, T], I32, name="tab_w", tag="tab_w", align_bytes=64)
+        tab_s = keep.tile([P, T], U8, name="tab_s", tag="tab_s", align_bytes=64)
         planes = keep.tile([P, 6 * R + 2 * J], U8, name="planes", align_bytes=64)
-        w_planes = [planes[:, 0 : 4 * R], planes[:, 4 * R : 6 * R]]
+        w_planes, wd_planes = planes[:, 0 : 4 * R], planes[:, 4 * R : 6 * R]
         pass1_planes = [planes[:, 6 * R + 2 * HALF * h : 6 * R + 2 * HALF * (h + 1)] for h in range(2)]
 
         nc.vector.memset(tab_s[:].bitcast(I32), 0)
         nc.vector.memset(planes[:].bitcast(I32), 0)
-        pages = [keep.tile([P, T], F32, name=f"page{t}") for t in range(1)]
+        pages = [keep.tile([P, T], F32, name="page0")]
         nc.vector.memset(pages[0][:].bitcast(I32), 0)
 
-        def stage_scales(queue, staged, sources):
+        def stage_scales(staged, sources):
             words = staged.bitcast(I32)
             col = 0
             for scales in sources:
                 passes = scales.shape[0]
                 width = passes * R // 4
-                queue.dma_start(
+                nc.sync.dma_start(
                     words[0:SCALE_ROWS, col : col + width].rearrange("q (a n) -> q a n", a=passes),
                     scales.bitcast(I32).rearrange("a q n -> q a n"),
                 )
@@ -71,42 +86,39 @@ def tile_list_msg_tanh_res_gateP_kernel(
                     staged.bitcast(I32)[4 * quad : 4 * quad + 4, :],
                 )
 
-        w_staged = keep.tile([SCALE_ROWS, 4 * R], U8, name="w_staged", align_bytes=64)[:]
         ident = keep.tile([P, P], F32, name="ident")
         make_identity(nc, ident[:])
+
         nc.sync.dma_start(lists[0][:], offs)
         tab_s_rows = tab_scales.bitcast(I32).rearrange("a (q r) t -> r q a t", r=4)
         for r in range(4):
             nc.sync.dma_start(tab_s[:].bitcast(I32)[r:P:16, :], tab_s_rows[r])
         nc.sync.dma_start(lists[1][:], offs2)
-        stage_scales(nc.sync, w_staged, (ws_scales, wt_scales))
+        w_staged = [keep.tile([SCALE_ROWS, 2 * R], U8, name=f"w_staged{l}", align_bytes=64)[:] for l in range(2)]
+        w_words = [keep.tile([P, 4 * R], U8, name=f"w_words{l}", align_bytes=64) for l in range(2)]
+        stage_scales(w_staged[0], (ws_scales,))
         nc.sync.dma_start(tab_w[:], tab_words[0].rearrange("p t b -> p (t b)").bitcast(I32))
-        w_words = keep.tile([P, 8 * R], U8, name="w_words", align_bytes=64)
+        stage_scales(w_staged[1], (wt_scales,))
         for l, words in enumerate((ws_words, wt_words)):
             nc.sync.dma_start(
-                w_words[:, 4 * l * R : 4 * (l + 1) * R].bitcast(I32).rearrange("p (a n) -> p a n", a=2),
+                w_words[l][:].bitcast(I32).rearrange("p (a n) -> p a n", a=2),
                 words.bitcast(I32).rearrange("a p n -> p a n"),
             )
-        sm_rows = keep.tile([P, 4], F32, name="sm_rows")
-        nc.sync.dma_start(sm_rows[:], sm.rearrange("(p t) -> p t", t=4))
-        spread_scales(nc.scalar, w_planes[0], w_staged)
+            spread_scales(nc.scalar, w_planes[:, 2 * l * R : 2 * (l + 1) * R], w_staged[l])
         wgo_rows = keep.tile([P, P], F32, name="wgo_rows")
         nc.sync.dma_start(wgo_rows[:], wgo[0 : P * P // J, :].rearrange("r (b p) -> (r b) p", p=P))
 
         def offsets(l, j0, n):
             return lists[l][:, j0 // 16 : (j0 + n) // 16]
 
-        pass0_planes = [keep.tile([P, 2 * HALF], U8, name="pass0_planes0", align_bytes=64)]
+        pass0_planes = []
         parted = {}
 
-        def pick_scales(h, queue):
+        def pick_scales(h, picked):
             for l in range(2):
-                nc.vector.tensor_copy(
-                    pass0_planes[h][:, l * HALF : (l + 1) * HALF], tab_s[:].indirect(offsets(l, h * HALF, HALF))
-                )
-            queue.dma_start(
-                pass1_planes[h].bitcast(I32)[0 : P - 16, :], pass0_planes[h][:].bitcast(I32)[16:P, :]
-            )
+                nc.vector.tensor_copy(picked[:, l * HALF : (l + 1) * HALF], tab_s[:].indirect(offsets(l, h * HALF, HALF)))
+            nc.sync.dma_start(pass1_planes[h].bitcast(I32)[0 : P - 16, :], picked[:].bitcast(I32)[16:P, :])
+            pass0_planes.append(picked)
 
         def pick_words(j0, n, picked):
             for l in range(2):
@@ -120,36 +132,35 @@ def tile_list_msg_tanh_res_gateP_kernel(
             for c0 in range(0, n, QUARTER):
                 parted[(j0 + c0) // QUARTER] = (words, n, c0)
 
-        pick_scales(0, nc.sync)
-        def place_tile(shape, dtype, name, offset):
-            return placed.tile(shape, dtype, name=name, offset=offset, align_bytes=64)
+        pick_scales(0, keep.tile([P, 2 * HALF], U8, name="pass0_planes0", align_bytes=64))
+        for q, starts in enumerate(((AT_WORDS00, AT_WORDS01), (AT_WORDS10, AT_WORDS11))):
+            picked = [place_tile([P, QUARTER], U32, f"picked{q}_{l}", starts[l])[:] for l in range(2)]
+            pick_words(q * QUARTER, QUARTER, picked)
 
-        for q, starts in enumerate(((1024, 11200 + 8192), (64, 10240 + 8192))):
-            pick_words(q * QUARTER, QUARTER, [place_tile([P, QUARTER], U32, f"picked{q}_{l}", starts[l])[:] for l in range(2)])
-
-        wd = place_tile([P, 8 * N], U8, "wd", 1984)
+        wd = place_tile([P, 8 * N], U8, "wd", AT_WD)
         wd4, wd8, wd_staged = wd[:, 0 : 2 * N], wd[:, 2 * N : 6 * N], wd[:, 6 * N : 8 * N]
-        stage_scales(nc.sync, wd_staged, (wd4_scales, wd8_scales))
+        sm_rows = place_tile([P, 4], F32, "sm_rows", AT_SM)
+        nc.sync.dma_start(sm_rows[:], sm.rearrange("(p t) -> p t", t=4))
+        stage_scales(wd_staged, (wd4_scales, wd8_scales))
         nc.sync.dma_start(wd4.bitcast(I32), wd4_words[0].bitcast(I32))
         nc.sync.dma_start(wd8.bitcast(I32), wd8_words[0].rearrange("p n i -> p (n i)").bitcast(I32))
         gT_rows = gT.rearrange("(p t) c -> t p c", t=4)
-        gates01 = place_tile([P, 2, T], F32, "gates01", 10752 + 8192)
-        gates = {0: gates01[:, 0, :], 2: gates01[:, 1, :]}
+        first_gates = place_tile([P, 2, T], F32, "first_gates", AT_GATES)
+        gates = {0: first_gates[:, 0, :], 2: first_gates[:, 1, :]}
         for t in (0, 2):
             nc.sync.dma_start(gates[t], gT_rows[t])
-        spread_scales(nc.sync, w_planes[1], wd_staged)
+        spread_scales(nc.sync, wd_planes, wd_staged)
 
-        pass0_planes.append(place_tile([P, 2 * HALF], U8, "pass0_planes1", 0))
-        pick_scales(1, nc.sync)
-        picked_half = place_tile([P, 2 * HALF], U32, "picked_half", 6208 + 8192)
+        pick_scales(1, place_tile([P, 2 * HALF], U8, "pass0_planes1", AT_PLANES1))
+        picked_half = place_tile([P, 2 * HALF], U32, "picked_half", AT_WORDS_HALF)
         pick_words(HALF, HALF, [picked_half[:, l * HALF : (l + 1) * HALF] for l in range(2)])
-        for t, tag in ((3, "gates2"), (1, "gates3")):
+        for t, tag in ((3, "tab_s"), (1, "tab_w")):
             gates[t] = keep.tile([P, T], F32, name=f"gates{t}", tag=tag, align_bytes=64)[:]
             nc.sync.dma_start(gates[t], gT_rows[t])
 
         wy = keep.tile([P, 4, J], F32, name="wy")
-        h_codes, h_scales, h_woven = {}, {}, {}
-        a_banks, tanh_a, tanh_banks, h_rows = {}, {}, {}, {}
+        a_banks, tanh_a, tanh_banks = {}, {}, {}
+        h_rows, h_codes, h_scales = {}, {}, {}
         y_banks, wy_edges, wy_banks = {}, {}, {}
 
         def first_product(q):
@@ -159,15 +170,14 @@ def tile_list_msg_tanh_res_gateP_kernel(
             for b in range(2):
                 a_banks[q, b] = psum.tile([P, R], F32, name="a_bank", tag=f"bank{2 * (q % 2) + b}")
                 for i, (l, a) in enumerate(steps):
-                    col = (2 * l + a) * n + c0 + b * P
-                    edge_planes = (pass0_planes, pass1_planes)[a][h]
-                    pcol = l * HALF + j0 + b * P
+                    word_col = (2 * l + a) * n + c0 + b * P
+                    plane_col = l * HALF + j0 + b * P
                     nc.tensor.matmul_mx(
                         a_banks[q, b][:],
-                        lhsT=words[:, 2 * col : 2 * (col + P)].bitcast(FP4X4),
-                        lhsT_scale=edge_planes[:, pcol : pcol + P],
-                        rhs=w_words[:, 2 * (2 * l + a) * R : 2 * (2 * l + a + 1) * R].bitcast(FP4X4),
-                        rhs_scale=w_planes[0][:, (2 * l + a) * R : (2 * l + a + 1) * R],
+                        lhsT=words[:, 2 * word_col : 2 * (word_col + P)].bitcast(FP4X4),
+                        lhsT_scale=(pass0_planes, pass1_planes)[a][h][:, plane_col : plane_col + P],
+                        rhs=w_words[l][:, 2 * a * R : 2 * (a + 1) * R].bitcast(FP4X4),
+                        rhs_scale=w_planes[:, (2 * l + a) * R : (2 * l + a + 1) * R],
                         start=(i == 0),
                         stop=(i == len(steps) - 1),
                     )
@@ -175,13 +185,7 @@ def tile_list_msg_tanh_res_gateP_kernel(
         def tanh_rows(q):
             for b in range(2):
                 tanh_a[q, b] = ring.tile([P, 4, P], F32, name="tanh_a")
-                nc.scalar.activation(
-                    tanh_a[q, b][:],
-                    a_banks[q, b][:].rearrange("p (m t) -> p t m", t=4),
-                    TANH,
-                )
-
-        def turn_tanh(q):
+                nc.scalar.activation(tanh_a[q, b][:], a_banks[q, b][:].rearrange("p (m t) -> p t m", t=4), TANH)
             for u in range(2):
                 bank = psum.tile([P, 2, QUARTER], F32, name="tanh_bank", tag=f"bank{2 * (q % 2) + u}")
                 for e in range(2):
@@ -194,26 +198,26 @@ def tile_list_msg_tanh_res_gateP_kernel(
             for t in range(4):
                 nc.scalar.activation(h_rows[q][:, t, :], tanh_banks[q, t], COPY, scale=sm_rows[:, t : t + 1])
 
-        def weave_h(q):
-            h_woven[q] = keep.tile([P, 4 * QUARTER], BF16, name=f"h_woven{q}", tag=f"h_woven{q}", align_bytes=64)
+        def quantise_h(q):
+            h_woven = keep.tile([P, 4 * QUARTER], BF16, name=f"h_woven{q}", tag=f"h_woven{q}", align_bytes=64)
             nc.scalar.copy(
-                h_woven[q][:].rearrange("p (c i t) -> p c t i", i=4, t=4),
+                h_woven[:].rearrange("p (c i t) -> p c t i", i=4, t=4),
                 h_rows[q][:].rearrange("p t (c i) -> p c t i", i=4),
             )
             h_codes[q] = keep.tile([P, QUARTER], U32, name=f"h_codes{q}", align_bytes=64)
             h_scales[q] = keep.tile([P, QUARTER], U8, name=f"h_scales{q}", align_bytes=64)
-            nc.vector.quantize_mx(h_codes[q][:].bitcast(FP8X4), h_scales[q][:], h_woven[q][:])
+            nc.vector.quantize_mx(h_codes[q][:].bitcast(FP8X4), h_scales[q][:], h_woven[:])
 
-        def second_product(q, first_bank):
+        def second_product(q):
             for b in range(2):
-                y_banks[q, b] = psum.tile([P, N], F32, name="y_bank", tag=f"bank{first_bank + b}")
+                y_banks[q, b] = psum.tile([P, N], F32, name="y_bank", tag=f"bank{Y_BANKS[q] + b}")
                 for i, (w, fmt) in enumerate(((wd4, FP4X4), (wd8, FP8X4))):
                     nc.tensor.matmul_mx(
                         y_banks[q, b][:],
                         lhsT=h_codes[q][:, b * P : (b + 1) * P].bitcast(FP8X4),
                         lhsT_scale=h_scales[q][:, b * P : (b + 1) * P],
                         rhs=w.bitcast(fmt),
-                        rhs_scale=w_planes[1][:, i * N : (i + 1) * N],
+                        rhs_scale=wd_planes[:, i * N : (i + 1) * N],
                         start=(i == 0),
                         stop=(i == 1),
                     )
@@ -227,10 +231,8 @@ def tile_list_msg_tanh_res_gateP_kernel(
                     COPY,
                     scale=wgo_cols[:, 2 * q + b : 2 * q + b + 1],
                 )
-
-        def turn_wy(q, first_bank):
             for b in range(2):
-                wy_banks[q, b] = psum.tile([P, 4, P], F32, name="wy_bank", tag=f"bank{first_bank + b}")
+                wy_banks[q, b] = psum.tile([P, 4, P], F32, name="wy_bank", tag=f"bank{Y_BANKS[q] + b}")
                 for t in range(4):
                     nc.tensor.transpose(wy_banks[q, b][:, t, :], wy_edges[q, b][:, t, :], ident[:])
 
@@ -241,74 +243,78 @@ def tile_list_msg_tanh_res_gateP_kernel(
 
         picked_gates = {}
 
-        def pick_gates(tag, jobs):
-            picked = keep.tile([P, sum(n for t, j0, n in jobs)], F32, name=f"g_{tag}", tag=tag, align_bytes=64)
-            col = 0
-            for t, j0, n in jobs:
-                nc.vector.tensor_copy(picked[:, col : col + n], gates[t].indirect(offsets(0, j0, n)))
-                for c0 in range(0, n, QUARTER):
-                    picked_gates[j0 + c0, t] = picked[:, col + c0 : col + n]
-                col = col + n
+        def pick_gates(t, tag):
+            picked_gates[t] = keep.tile([P, J], F32, name=f"picked_gates{t}", tag=tag, align_bytes=64)
+            nc.vector.tensor_copy(picked_gates[t][:], gates[t].indirect(offsets(0, 0, J)))
 
         out_rows = out_0.rearrange("(p t) c -> t p c", t=4)
         n_pieces = T // PIECE
         rounded = [keep.tile([P, 2, PIECE, 2], BF16, name=f"rounded{c}") for c in range(n_pieces)]
 
-        def place(j0, n, t):
+        def place(t, q0, quarters):
+            j0, n = q0 * QUARTER, quarters * QUARTER
             nc.vector.tensor_tensor(
-                pages[t][:].indirect(offsets(1, j0, n)), wy[:, t, j0 : j0 + n], picked_gates[j0, t][:, 0:n], MULT
+                pages[t][:].indirect(offsets(1, j0, n)), wy[:, t, j0 : j0 + n], picked_gates[t][:, j0 : j0 + n], MULT
             )
             if j0 + n == J:
                 nc.sync.dma_start(out_rows[t], pages[t][:])
                 for c in range(n_pieces):
                     nc.scalar.copy(rounded[c][:, t // 2, :, t % 2], pages[t][:, c * PIECE : (c + 1) * PIECE])
 
-        wgo_bank = psum.tile([P, N], F32, name="wgo_bank", tag="bank6")
+        wgo_bank = psum.tile([P, N], F32, name="wgo_bank", tag=f"bank{Y_BANKS[2]}")
         nc.tensor.transpose(wgo_bank[:, 0:P], wgo_rows[:], ident[:])
         wgo_cols = keep.tile([P, J // P], F32, name="wgo_cols")
         nc.scalar.copy(wgo_cols[:], wgo_bank[:, 0 : J // P])
-        first_product(0)
-        tanh_rows(0)
-        turn_tanh(0)
-        first_product(1)
-        pick_gates("gates_row0", [(0, 0, J)])
-        scale_rows(0)
-        weave_h(0)
-        pick_gates("h_rows0", [(2, 0, J)])
-        for q in range(1, 4):
-            tanh_rows(q)
-            turn_tanh(q)
-            if q < 3:
-                first_product(q + 1)
-            if q > 1:
-                copy_wy(q - 2)
-                for t in range(q - 1):
-                    place((q - 2) * QUARTER, QUARTER, t)
-            second_product(q - 1, Y_BANKS[q - 1])
+
+        def hidden_and_message(q):
+            second_product(q - 1)
             scale_rows(q)
             weigh(q - 1)
-            turn_wy(q - 1, Y_BANKS[q - 1])
-            weave_h(q)
-            if q == 1:
-                pick_gates("h_rows1", [(3, 0, J)])
-                pages.append(keep.tile([P, T], F32, name="page1", tag="gates2", align_bytes=64))
-                nc.vector.memset(pages[1][:].bitcast(I32), 0)
-            if q == 2:
-                pick_gates("h_rows2", [(1, 0, J)])
-                place(0, QUARTER, 1)
+            quantise_h(q)
+
+        first_product(0)
+        tanh_rows(0)
+        first_product(1)
+        pick_gates(0, "picked_gates0")
+        scale_rows(0)
+        quantise_h(0)
+        pick_gates(2, "h_rows0")
+
+        tanh_rows(1)
+        first_product(2)
+        hidden_and_message(1)
+        pick_gates(3, "h_rows1")
+        pages.append(keep.tile([P, T], F32, name="page1", tag="tab_s", align_bytes=64))
+        nc.vector.memset(pages[1][:].bitcast(I32), 0)
+
+        tanh_rows(2)
+        first_product(3)
+        copy_wy(0)
+        place(0, 0, 1)
+        hidden_and_message(2)
+        pick_gates(1, "h_rows2")
+        place(1, 0, 1)
+
+        tanh_rows(3)
+        copy_wy(1)
+        for t in range(2):
+            place(t, 1, 1)
+        hidden_and_message(3)
         pages.append(keep.tile([P, T], F32, name="page2", tag="h_woven3", align_bytes=64))
         nc.gpsimd.memset(pages[2][:].bitcast(I32), 0)
         pages.append(pages[0])
+
         copy_wy(2)
-        second_product(3, Y_BANKS[3])
+        second_product(3)
         weigh(3)
-        turn_wy(3, Y_BANKS[3])
         copy_wy(3)
-        for q in (2, 3):
-            for t in range(2):
-                place(q * QUARTER, QUARTER, t)
-            place(*((0, QUARTER), (QUARTER, 3 * QUARTER))[q - 2], 2)
-        place(0, J, 3)
+        for t in range(2):
+            place(t, 2, 1)
+        place(2, 0, 1)
+        for t in range(2):
+            place(t, 3, 1)
+        place(2, 1, 3)
+        place(3, 0, 4)
 
         out_plane = keep.tile([P, T], U8, name="out_plane", align_bytes=64)
         out_words = out_1[0].rearrange("p t i -> p (t i)").bitcast(I32)

@@ -25,19 +25,26 @@ SCALE_ROWS = 16
 STORE_COLS = 512
 PIECE = 256
 VECTOR_PIECES = 6
-Y_BANKS = (4, 4, 6, 4)
+Y_BANKS = ((4, 5), (4, 0), (4, 0), (4, 0))
+WY_BANKS = ((4, 5), (4, 0), (6, 7), (4, 0))
 
 UNIT = 64
 WORDS = 4 * QUARTER
-AT_WORDS00 = WORDS
 AT_WORDS10 = UNIT
+AT_WORDS00 = WORDS
 AT_PLANES1 = 0
 AT_SM = AT_WORDS10 + WORDS
+AT_WGO = AT_SM + UNIT
 AT_WD = AT_WORDS00 + WORDS - UNIT
 AT_WORDS_HALF = AT_WD + 8 * N
 AT_WORDS11 = AT_WORDS_HALF + 4 * WORDS - UNIT
 AT_WORDS01 = AT_WORDS11 + WORDS - UNIT
-AT_GATES = AT_WORDS11 + UNIT
+AT_GATES2 = AT_WORDS01 + WORDS - UNIT
+AT_GATES3 = AT_GATES2 + 4 * T
+AT_TABLE_SCALES = AT_GATES3 + 4 * T - UNIT
+AT_LATE_GATES = AT_TABLE_SCALES + T - UNIT
+AT_CODES = {1: AT_GATES3, 2: AT_LATE_GATES}
+AT_PAGE2 = AT_LATE_GATES + 4 * T
 
 
 def tile_list_msg_tanh_res_gateP_kernel(
@@ -56,16 +63,17 @@ def tile_list_msg_tanh_res_gateP_kernel(
             return placed.tile(shape, dtype, name=name, offset=offset, align_bytes=UNIT)
 
         lists = [keep.tile([P, J // 16], U16, name=f"list{l}") for l in range(2)]
-        tab_w = keep.tile([P, T], I32, name="tab_w", tag="tab_w", align_bytes=64)
-        tab_s = keep.tile([P, T], U8, name="tab_s", tag="tab_s", align_bytes=64)
+        tab_w = keep.tile([P, T], I32, name="tab_w", align_bytes=64)
+        tab_s = place_tile([P, T], U8, "tab_s", AT_TABLE_SCALES)
         planes = keep.tile([P, 6 * R + 2 * J], U8, name="planes", align_bytes=64)
         w_planes, wd_planes = planes[:, 0 : 4 * R], planes[:, 4 * R : 6 * R]
         pass1_planes = [planes[:, 6 * R + 2 * HALF * h : 6 * R + 2 * HALF * (h + 1)] for h in range(2)]
 
         nc.vector.memset(tab_s[:].bitcast(I32), 0)
         nc.vector.memset(planes[:].bitcast(I32), 0)
-        pages = [keep.tile([P, T], F32, name="page0")]
-        nc.vector.memset(pages[0][:].bitcast(I32), 0)
+        pages = [keep.tile([P, T], F32, name=f"page{t}") for t in range(2)]
+        for t in range(2):
+            nc.vector.memset(pages[t][:].bitcast(I32), 0)
 
         def stage_scales(staged, sources):
             words = staged.bitcast(I32)
@@ -94,19 +102,16 @@ def tile_list_msg_tanh_res_gateP_kernel(
         for r in range(4):
             nc.sync.dma_start(tab_s[:].bitcast(I32)[r:P:16, :], tab_s_rows[r])
         nc.sync.dma_start(lists[1][:], offs2)
-        w_staged = [keep.tile([SCALE_ROWS, 2 * R], U8, name=f"w_staged{l}", align_bytes=64)[:] for l in range(2)]
+        w_staged = keep.tile([SCALE_ROWS, 4 * R], U8, name="w_staged", align_bytes=64)[:]
         w_words = [keep.tile([P, 4 * R], U8, name=f"w_words{l}", align_bytes=64) for l in range(2)]
-        stage_scales(w_staged[0], (ws_scales,))
+        stage_scales(w_staged, (ws_scales, wt_scales))
         nc.sync.dma_start(tab_w[:], tab_words[0].rearrange("p t b -> p (t b)").bitcast(I32))
-        stage_scales(w_staged[1], (wt_scales,))
         for l, words in enumerate((ws_words, wt_words)):
             nc.sync.dma_start(
                 w_words[l][:].bitcast(I32).rearrange("p (a n) -> p a n", a=2),
                 words.bitcast(I32).rearrange("a p n -> p a n"),
             )
-            spread_scales(nc.scalar, w_planes[:, 2 * l * R : 2 * (l + 1) * R], w_staged[l])
-        wgo_rows = keep.tile([P, P], F32, name="wgo_rows")
-        nc.sync.dma_start(wgo_rows[:], wgo[0 : P * P // J, :].rearrange("r (b p) -> (r b) p", p=P))
+        spread_scales(nc.scalar, w_planes, w_staged)
 
         def offsets(l, j0, n):
             return lists[l][:, j0 // 16 : (j0 + n) // 16]
@@ -132,31 +137,36 @@ def tile_list_msg_tanh_res_gateP_kernel(
             for c0 in range(0, n, QUARTER):
                 parted[(j0 + c0) // QUARTER] = (words, n, c0)
 
-        pick_scales(0, keep.tile([P, 2 * HALF], U8, name="pass0_planes0", align_bytes=64))
-        for q, starts in enumerate(((AT_WORDS00, AT_WORDS01), (AT_WORDS10, AT_WORDS11))):
+        def pick_quarter(q, starts):
             picked = [place_tile([P, QUARTER], U32, f"picked{q}_{l}", starts[l])[:] for l in range(2)]
             pick_words(q * QUARTER, QUARTER, picked)
 
-        wd = place_tile([P, 8 * N], U8, "wd", AT_WD)
-        wd4, wd8, wd_staged = wd[:, 0 : 2 * N], wd[:, 2 * N : 6 * N], wd[:, 6 * N : 8 * N]
+        pick_scales(0, keep.tile([P, 2 * HALF], U8, name="pass0_planes0", align_bytes=64))
+        pick_quarter(0, (AT_WORDS00, AT_WORDS01))
+
+        late = place_tile([P, 8 * N], U8, "late", AT_WD)
+        wd4, wd8, wd_staged = late[:, 0 : 2 * N], late[:, 2 * N : 6 * N], late[:, 6 * N : 8 * N]
+        stage_scales(wd_staged, (wd4_scales, wd8_scales))
         sm_rows = place_tile([P, 4], F32, "sm_rows", AT_SM)
         nc.sync.dma_start(sm_rows[:], sm.rearrange("(p t) -> p t", t=4))
-        stage_scales(wd_staged, (wd4_scales, wd8_scales))
+        wgo_rows = place_tile([P, P], F32, "wgo_rows", AT_WGO)
+        nc.sync.dma_start(wgo_rows[:], wgo[0 : P * P // J, :].rearrange("r (b p) -> (r b) p", p=P))
+        gT_rows = gT.rearrange("(p t) c -> p t c", t=4)
+        gates2 = place_tile([P, T], F32, "gates2", AT_GATES2)
+        nc.sync.dma_start(gates2[:], gT_rows[:, 2, :])
         nc.sync.dma_start(wd4.bitcast(I32), wd4_words[0].bitcast(I32))
         nc.sync.dma_start(wd8.bitcast(I32), wd8_words[0].rearrange("p n i -> p (n i)").bitcast(I32))
-        gT_rows = gT.rearrange("(p t) c -> t p c", t=4)
-        first_gates = place_tile([P, 2, T], F32, "first_gates", AT_GATES)
-        gates = {0: first_gates[:, 0, :], 2: first_gates[:, 1, :]}
-        for t in (0, 2):
-            nc.sync.dma_start(gates[t], gT_rows[t])
         spread_scales(nc.sync, wd_planes, wd_staged)
 
+        pick_quarter(1, (AT_WORDS10, AT_WORDS11))
         pick_scales(1, place_tile([P, 2 * HALF], U8, "pass0_planes1", AT_PLANES1))
+        gates3 = place_tile([P, T], F32, "gates3", AT_GATES3)
+        nc.sync.dma_start(gates3[:], gT_rows[:, 3, :])
+        late_gates = place_tile([P, 2, T], F32, "late_gates", AT_LATE_GATES)
+        nc.sync.dma_start(late_gates[:], gT_rows[:, 0:2, :])
+        gates = [late_gates[:, 0, :], late_gates[:, 1, :], gates2[:], gates3[:]]
         picked_half = place_tile([P, 2 * HALF], U32, "picked_half", AT_WORDS_HALF)
         pick_words(HALF, HALF, [picked_half[:, l * HALF : (l + 1) * HALF] for l in range(2)])
-        for t, tag in ((3, "tab_s"), (1, "tab_w")):
-            gates[t] = keep.tile([P, T], F32, name=f"gates{t}", tag=tag, align_bytes=64)[:]
-            nc.sync.dma_start(gates[t], gT_rows[t])
 
         wy = keep.tile([P, 4, J], F32, name="wy")
         a_banks, tanh_a, tanh_banks = {}, {}, {}
@@ -182,10 +192,11 @@ def tile_list_msg_tanh_res_gateP_kernel(
                         stop=(i == len(steps) - 1),
                     )
 
-        def tanh_rows(q):
-            for b in range(2):
-                tanh_a[q, b] = ring.tile([P, 4, P], F32, name="tanh_a")
-                nc.scalar.activation(tanh_a[q, b][:], a_banks[q, b][:].rearrange("p (m t) -> p t m", t=4), TANH)
+        def tanh_rows(q, b):
+            tanh_a[q, b] = ring.tile([P, 4, P], F32, name="tanh_a")
+            nc.scalar.activation(tanh_a[q, b][:], a_banks[q, b][:].rearrange("p (m t) -> p t m", t=4), TANH)
+
+        def turn_tanh(q):
             for u in range(2):
                 bank = psum.tile([P, 2, QUARTER], F32, name="tanh_bank", tag=f"bank{2 * (q % 2) + u}")
                 for e in range(2):
@@ -204,13 +215,16 @@ def tile_list_msg_tanh_res_gateP_kernel(
                 h_woven[:].rearrange("p (c i t) -> p c t i", i=4, t=4),
                 h_rows[q][:].rearrange("p t (c i) -> p c t i", i=4),
             )
-            h_codes[q] = keep.tile([P, QUARTER], U32, name=f"h_codes{q}", align_bytes=64)
+            if q in AT_CODES:
+                h_codes[q] = place_tile([P, QUARTER], U32, f"h_codes{q}", AT_CODES[q])
+            else:
+                h_codes[q] = keep.tile([P, QUARTER], U32, name=f"h_codes{q}", align_bytes=64)
             h_scales[q] = keep.tile([P, QUARTER], U8, name=f"h_scales{q}", align_bytes=64)
             nc.vector.quantize_mx(h_codes[q][:].bitcast(FP8X4), h_scales[q][:], h_woven[:])
 
         def second_product(q):
             for b in range(2):
-                y_banks[q, b] = psum.tile([P, N], F32, name="y_bank", tag=f"bank{Y_BANKS[q] + b}")
+                y_banks[q, b] = psum.tile([P, N], F32, name="y_bank", tag=f"bank{Y_BANKS[q][b]}")
                 for i, (w, fmt) in enumerate(((wd4, FP4X4), (wd8, FP8X4))):
                     nc.tensor.matmul_mx(
                         y_banks[q, b][:],
@@ -222,30 +236,34 @@ def tile_list_msg_tanh_res_gateP_kernel(
                         stop=(i == 1),
                     )
 
-        def weigh(q):
-            for b in range(2):
-                wy_edges[q, b] = ring.tile([P, 4, P], F32, name="wy_edges")
-                nc.scalar.activation(
-                    wy_edges[q, b][:],
-                    y_banks[q, b][:].rearrange("p (m t) -> p t m", t=4),
-                    COPY,
-                    scale=wgo_cols[:, 2 * q + b : 2 * q + b + 1],
-                )
-            for b in range(2):
-                wy_banks[q, b] = psum.tile([P, 4, P], F32, name="wy_bank", tag=f"bank{Y_BANKS[q] + b}")
-                for t in range(4):
-                    nc.tensor.transpose(wy_banks[q, b][:, t, :], wy_edges[q, b][:, t, :], ident[:])
+        def weigh(q, b):
+            wy_edges[q, b] = ring.tile([P, 4, P], F32, name="wy_edges")
+            nc.scalar.activation(
+                wy_edges[q, b][:],
+                y_banks[q, b][:].rearrange("p (m t) -> p t m", t=4),
+                COPY,
+                scale=wgo_cols[:, 2 * q + b : 2 * q + b + 1],
+            )
 
-        def copy_wy(q):
-            for b in range(2):
-                j0 = q * QUARTER + b * P
-                nc.scalar.copy(wy[:, :, j0 : j0 + P], wy_banks[q, b][:])
+        def turn_wy(q):
+            for u in range(2):
+                wy_banks[q, u] = psum.tile([P, 2, QUARTER], F32, name="wy_bank", tag=f"bank{WY_BANKS[q][u]}")
+                for e in range(2):
+                    for b in range(2):
+                        nc.tensor.transpose(
+                            wy_banks[q, u][:, e, b * P : (b + 1) * P], wy_edges[q, b][:, 2 * u + e, :], ident[:]
+                        )
+
+        def copy_wy(q, u):
+            nc.scalar.copy(wy[:, 2 * u : 2 * u + 2, q * QUARTER : (q + 1) * QUARTER], wy_banks[q, u][:])
 
         picked_gates = {}
 
-        def pick_gates(t, tag):
-            picked_gates[t] = keep.tile([P, J], F32, name=f"picked_gates{t}", tag=tag, align_bytes=64)
-            nc.vector.tensor_copy(picked_gates[t][:], gates[t].indirect(offsets(0, 0, J)))
+        def pick_gates(rows, tag):
+            picked = keep.tile([P, len(rows), J], F32, name=f"picked_gates{rows[0]}", tag=tag, align_bytes=64)
+            for i, t in enumerate(rows):
+                picked_gates[t] = picked[:, i, :]
+                nc.vector.tensor_copy(picked_gates[t], gates[t].indirect(offsets(0, 0, J)))
 
         out_rows = out_0.rearrange("(p t) c -> t p c", t=4)
         n_pieces = T // PIECE
@@ -261,59 +279,77 @@ def tile_list_msg_tanh_res_gateP_kernel(
                 for c in range(n_pieces):
                     nc.scalar.copy(rounded[c][:, t // 2, :, t % 2], pages[t][:, c * PIECE : (c + 1) * PIECE])
 
-        wgo_bank = psum.tile([P, N], F32, name="wgo_bank", tag=f"bank{Y_BANKS[2]}")
+        first_product(0)
+        tanh_rows(0, 0)
+        tanh_rows(0, 1)
+        turn_tanh(0)
+        first_product(1)
+        pick_gates((2,), "picked_gates2")
+        tanh_rows(1, 0)
+        scale_rows(0)
+        tanh_rows(1, 1)
+        turn_tanh(1)
+        quantise_h(0)
+        pick_gates((3,), "h_rows0")
+        scale_rows(1)
+
+        wgo_bank = psum.tile([P, N], F32, name="wgo_bank", tag="bank6")
         nc.tensor.transpose(wgo_bank[:, 0:P], wgo_rows[:], ident[:])
         wgo_cols = keep.tile([P, J // P], F32, name="wgo_cols")
         nc.scalar.copy(wgo_cols[:], wgo_bank[:, 0 : J // P])
 
-        def hidden_and_message(q):
-            second_product(q - 1)
-            scale_rows(q)
-            weigh(q - 1)
-            quantise_h(q)
-
-        first_product(0)
-        tanh_rows(0)
-        first_product(1)
-        pick_gates(0, "picked_gates0")
-        scale_rows(0)
-        quantise_h(0)
-        pick_gates(2, "h_rows0")
-
-        tanh_rows(1)
         first_product(2)
-        hidden_and_message(1)
-        pick_gates(3, "h_rows1")
-        pages.append(keep.tile([P, T], F32, name="page1", tag="tab_s", align_bytes=64))
-        nc.vector.memset(pages[1][:].bitcast(I32), 0)
-
-        tanh_rows(2)
-        first_product(3)
-        copy_wy(0)
-        place(0, 0, 1)
-        hidden_and_message(2)
-        pick_gates(1, "h_rows2")
-        place(1, 0, 1)
-
-        tanh_rows(3)
-        copy_wy(1)
-        for t in range(2):
-            place(t, 1, 1)
-        hidden_and_message(3)
-        pages.append(keep.tile([P, T], F32, name="page2", tag="h_woven3", align_bytes=64))
+        tanh_rows(2, 0)
+        quantise_h(1)
+        pick_gates((0, 1), "h_rows1")
+        pages.append(place_tile([P, T], F32, "page2", AT_PAGE2))
         nc.gpsimd.memset(pages[2][:].bitcast(I32), 0)
         pages.append(pages[0])
-
-        copy_wy(2)
-        second_product(3)
-        weigh(3)
-        copy_wy(3)
-        for t in range(2):
-            place(t, 2, 1)
+        tanh_rows(2, 1)
+        turn_tanh(2)
+        second_product(0)
+        weigh(0, 0)
+        weigh(0, 1)
+        turn_wy(0)
+        first_product(3)
+        tanh_rows(3, 0)
+        copy_wy(0, 0)
+        place(0, 0, 1)
+        place(1, 0, 1)
+        scale_rows(2)
+        tanh_rows(3, 1)
+        turn_tanh(3)
+        quantise_h(2)
+        copy_wy(0, 1)
         place(2, 0, 1)
-        for t in range(2):
-            place(t, 3, 1)
-        place(2, 1, 3)
+        second_product(1)
+        weigh(1, 0)
+        scale_rows(3)
+        weigh(1, 1)
+        turn_wy(1)
+        quantise_h(3)
+        copy_wy(1, 0)
+        copy_wy(1, 1)
+        place(0, 1, 1)
+        place(1, 1, 1)
+        place(2, 1, 1)
+        second_product(2)
+        weigh(2, 0)
+        weigh(2, 1)
+        turn_wy(2)
+        second_product(3)
+        weigh(3, 0)
+        weigh(3, 1)
+        turn_wy(3)
+        copy_wy(2, 0)
+        place(0, 2, 1)
+        place(1, 2, 1)
+        copy_wy(3, 0)
+        copy_wy(2, 1)
+        copy_wy(3, 1)
+        place(0, 3, 1)
+        place(1, 3, 1)
+        place(2, 2, 2)
         place(3, 0, 4)
 
         out_plane = keep.tile([P, T], U8, name="out_plane", align_bytes=64)

@@ -43,6 +43,8 @@ AT_GATES2 = AT_WORDS01 + WORDS - UNIT
 AT_GATES3 = AT_GATES2 + 4 * T
 AT_TABLE_SCALES = AT_GATES3 + 4 * T - UNIT
 AT_LATE_GATES = AT_TABLE_SCALES + T - UNIT
+AT_WD_PLANES = AT_WORDS11 + UNIT
+AT_PASS1_PLANES = AT_TABLE_SCALES + UNIT
 AT_CODES = {1: AT_GATES3, 2: AT_LATE_GATES}
 AT_PAGE2 = AT_LATE_GATES + 4 * T
 
@@ -65,9 +67,9 @@ def tile_list_msg_tanh_res_gateP_kernel(
         lists = [keep.tile([P, J // 16], U16, name=f"list{l}") for l in range(2)]
         tab_w = keep.tile([P, T], I32, name="tab_w", align_bytes=64)
         tab_s = place_tile([P, T], U8, "tab_s", AT_TABLE_SCALES)
-        planes = keep.tile([P, 6 * R + 2 * J], U8, name="planes", align_bytes=64)
-        w_planes, wd_planes = planes[:, 0 : 4 * R], planes[:, 4 * R : 6 * R]
-        pass1_planes = [planes[:, 6 * R + 2 * HALF * h : 6 * R + 2 * HALF * (h + 1)] for h in range(2)]
+        planes = keep.tile([P, 4 * R + J], U8, name="planes", align_bytes=64)
+        w_planes = planes[:, 0 : 4 * R]
+        pass1_planes = [planes[:, 4 * R :]]
 
         nc.vector.memset(tab_s[:].bitcast(I32), 0)
         nc.vector.memset(planes[:].bitcast(I32), 0)
@@ -156,9 +158,11 @@ def tile_list_msg_tanh_res_gateP_kernel(
         nc.sync.dma_start(gates2[:], gT_rows[:, 2, :])
         nc.sync.dma_start(wd4.bitcast(I32), wd4_words[0].bitcast(I32))
         nc.sync.dma_start(wd8.bitcast(I32), wd8_words[0].rearrange("p n i -> p (n i)").bitcast(I32))
-        spread_scales(nc.sync, wd_planes, wd_staged)
 
         pick_quarter(1, (AT_WORDS10, AT_WORDS11))
+        wd_planes = place_tile([P, 2 * N], U8, "wd_planes", AT_WD_PLANES)[:]
+        spread_scales(nc.sync, wd_planes, wd_staged)
+        pass1_planes.append(place_tile([P, J], U8, "pass1_planes1", AT_PASS1_PLANES)[:])
         pick_scales(1, place_tile([P, 2 * HALF], U8, "pass0_planes1", AT_PLANES1))
         gates3 = place_tile([P, T], F32, "gates3", AT_GATES3)
         nc.sync.dma_start(gates3[:], gT_rows[:, 3, :])
@@ -204,17 +208,23 @@ def tile_list_msg_tanh_res_gateP_kernel(
                     for b in range(2):
                         nc.tensor.transpose(bank[:, e, b * P : (b + 1) * P], tanh_a[q, b][:, 2 * u + e, :], ident[:])
 
-        def scale_rows(q):
+        def scale_rows(q, parts=1):
             h_rows[q] = keep.tile([P, 4, QUARTER], BF16, name=f"h_rows{q}", tag=f"h_rows{q}", align_bytes=64)
-            for t in range(4):
-                nc.scalar.activation(h_rows[q][:, t, :], tanh_banks[q, t], COPY, scale=sm_rows[:, t : t + 1])
+            n = QUARTER // parts
+            for j0 in range(0, QUARTER, n):
+                for t in range(4):
+                    nc.scalar.activation(
+                        h_rows[q][:, t, j0 : j0 + n], tanh_banks[q, t][:, j0 : j0 + n], COPY, scale=sm_rows[:, t : t + 1]
+                    )
 
-        def quantise_h(q):
+        def quantise_h(q, parts=1):
             h_woven = keep.tile([P, 4 * QUARTER], BF16, name=f"h_woven{q}", tag=f"h_woven{q}", align_bytes=64)
-            nc.scalar.copy(
-                h_woven[:].rearrange("p (c i t) -> p c t i", i=4, t=4),
-                h_rows[q][:].rearrange("p t (c i) -> p c t i", i=4),
-            )
+            n = QUARTER // parts
+            for j0 in range(0, QUARTER, n):
+                nc.scalar.copy(
+                    h_woven[:, 4 * j0 : 4 * (j0 + n)].rearrange("p (c i t) -> p c t i", i=4, t=4),
+                    h_rows[q][:, :, j0 : j0 + n].rearrange("p t (c i) -> p c t i", i=4),
+                )
             if q in AT_CODES:
                 h_codes[q] = place_tile([P, QUARTER], U32, f"h_codes{q}", AT_CODES[q])
             else:
@@ -324,10 +334,10 @@ def tile_list_msg_tanh_res_gateP_kernel(
         place(2, 0, 1)
         second_product(1)
         weigh(1, 0)
-        scale_rows(3)
+        scale_rows(3, 2)
         weigh(1, 1)
         turn_wy(1)
-        quantise_h(3)
+        quantise_h(3, 2)
         copy_wy(1, 0)
         copy_wy(1, 1)
         place(0, 1, 1)
@@ -352,7 +362,7 @@ def tile_list_msg_tanh_res_gateP_kernel(
         place(2, 2, 2)
         place(3, 0, 4)
 
-        out_plane = keep.tile([P, T], U8, name="out_plane", align_bytes=64)
+        out_plane = keep.tile([P, STORE_COLS], U8, name="out_plane", align_bytes=64)
         out_words = out_1[0].rearrange("p t i -> p (t i)").bitcast(I32)
         out_codes = [
             keep.tile([P, STORE_COLS], I32, name=f"out_codes{s}", align_bytes=64) for s in range(T // STORE_COLS)
@@ -369,7 +379,7 @@ def tile_list_msg_tanh_res_gateP_kernel(
         def quantise(c):
             s, c0 = divmod(c * PIECE, STORE_COLS)
             nc.vector.quantize_mx(
-                out_codes[s][:, c0 : c0 + PIECE].bitcast(FP8X4), out_plane[:, c * PIECE : (c + 1) * PIECE], woven[c][:]
+                out_codes[s][:, c0 : c0 + PIECE].bitcast(FP8X4), out_plane[4 * s :, c0 : c0 + PIECE], woven[c][:]
             )
             if c0 + PIECE == STORE_COLS:
                 nc.sync.dma_start(out_words[:, s * STORE_COLS : (s + 1) * STORE_COLS], out_codes[s][:])
@@ -379,8 +389,8 @@ def tile_list_msg_tanh_res_gateP_kernel(
             weave(c)
             quantise(c - 1)
         quantise(n_pieces - 1)
-        out_scales = out_2[0].bitcast(I32)
+        out_scales = out_2[0].bitcast(I32).rearrange("q (s c) -> s q c", s=4)
         for quad in range(4):
             (nc.sync, nc.scalar)[quad % 2].dma_start(
-                out_scales[4 * quad : 4 * quad + 4, :], out_plane[:].bitcast(I32)[32 * quad : 32 * quad + 4, :]
+                out_scales[:, 4 * quad : 4 * quad + 4, :], out_plane[:].bitcast(I32)[32 * quad : 32 * quad + 16, :]
             )

@@ -24,6 +24,7 @@ QUARTER = J // 4
 SCALE_ROWS = 16
 STORE_COLS = 512
 PIECE = 256
+DIRECT_PIECES = 1
 VECTOR_PIECES = 6
 Y_BANKS = ((4, 5), (4, 0), (4, 0), (4, 0))
 WY_BANKS = ((4, 5), (4, 0), (6, 7), (4, 0))
@@ -72,7 +73,6 @@ def tile_list_msg_tanh_res_gateP_kernel(
         pass1_planes = [planes[:, 4 * R :]]
 
         nc.vector.memset(tab_s[:].bitcast(I32), 0)
-        nc.vector.memset(planes[:].bitcast(I32), 0)
         pages = [keep.tile([P, T], F32, name=f"page{t}") for t in range(2)]
         for t in range(2):
             nc.vector.memset(pages[t][:].bitcast(I32), 0)
@@ -278,6 +278,15 @@ def tile_list_msg_tanh_res_gateP_kernel(
         out_rows = out_0.rearrange("(p t) c -> t p c", t=4)
         n_pieces = T // PIECE
         rounded = [keep.tile([P, 2, PIECE, 2], BF16, name=f"rounded{c}") for c in range(n_pieces)]
+        woven = [keep.tile([P, 4 * PIECE], BF16, name=f"woven{c}", align_bytes=64) for c in range(n_pieces)]
+
+        def weave(c):
+            on_vector = DIRECT_PIECES <= c < VECTOR_PIECES
+            copy, word = (nc.vector.tensor_copy, I32) if on_vector else (nc.scalar.copy, U32)
+            copy(
+                woven[c][:].bitcast(word).rearrange("p (j u) -> p j u", u=2),
+                rounded[c][:].rearrange("p u j e -> p u (j e)").bitcast(word).rearrange("p u j -> p j u"),
+            )
 
         def place(t, q0, quarters):
             j0, n = q0 * QUARTER, quarters * QUARTER
@@ -286,8 +295,15 @@ def tile_list_msg_tanh_res_gateP_kernel(
             )
             if j0 + n == J:
                 nc.sync.dma_start(out_rows[t], pages[t][:])
-                for c in range(n_pieces):
-                    nc.scalar.copy(rounded[c][:, t // 2, :, t % 2], pages[t][:, c * PIECE : (c + 1) * PIECE])
+                for c in range(DIRECT_PIECES if t == 3 else 0, n_pieces):
+                    piece = pages[t][:, c * PIECE : (c + 1) * PIECE]
+                    if t == 2 and c < DIRECT_PIECES:
+                        nc.scalar.copy(rounded[c][:, 1, :, :], piece.unsqueeze(2).to_broadcast([P, PIECE, 2]))
+                    else:
+                        nc.scalar.copy(rounded[c][:, t // 2, :, t % 2], piece)
+                    if t == 2 and c == DIRECT_PIECES:
+                        for early in range(DIRECT_PIECES):
+                            weave(early)
 
         first_product(0)
         tanh_rows(0, 0)
@@ -367,14 +383,14 @@ def tile_list_msg_tanh_res_gateP_kernel(
         out_codes = [
             keep.tile([P, STORE_COLS], I32, name=f"out_codes{s}", align_bytes=64) for s in range(T // STORE_COLS)
         ]
-        woven = [keep.tile([P, 4 * PIECE], BF16, name=f"woven{c}", align_bytes=64) for c in range(n_pieces)]
 
-        def weave(c):
-            copy, word = (nc.vector.tensor_copy, I32) if c < VECTOR_PIECES else (nc.scalar.copy, U32)
-            copy(
-                woven[c][:].bitcast(word).rearrange("p (j u) -> p j u", u=2),
-                rounded[c][:].rearrange("p u j e -> p u (j e)").bitcast(word).rearrange("p u j -> p j u"),
-            )
+        def finish(c):
+            if c < DIRECT_PIECES:
+                nc.vector.tensor_copy(
+                    woven[c][:].rearrange("p (j t) -> p j t", t=4)[:, :, 3], pages[3][:, c * PIECE : (c + 1) * PIECE]
+                )
+            else:
+                weave(c)
 
         def quantise(c):
             s, c0 = divmod(c * PIECE, STORE_COLS)
@@ -384,9 +400,9 @@ def tile_list_msg_tanh_res_gateP_kernel(
             if c0 + PIECE == STORE_COLS:
                 nc.sync.dma_start(out_words[:, s * STORE_COLS : (s + 1) * STORE_COLS], out_codes[s][:])
 
-        weave(0)
+        finish(0)
         for c in range(1, n_pieces):
-            weave(c)
+            finish(c)
             quantise(c - 1)
         quantise(n_pieces - 1)
         out_scales = out_2[0].bitcast(I32).rearrange("q (s c) -> s q c", s=4)

@@ -31,21 +31,19 @@ WY_BANKS = ((4, 5), (4, 0), (6, 7), (4, 0))
 
 UNIT = 64
 WORDS = 4 * QUARTER
-AT_WORDS10 = UNIT
-AT_WORDS00 = WORDS
-AT_PLANES1 = 0
-AT_SM = AT_WORDS10 + WORDS
+AT_WORDS_HALF = 0
+AT_WORDS10 = AT_WORDS_HALF + 4 * WORDS - UNIT
+AT_LAST_SCALES = AT_WORDS10 + UNIT
+AT_WORDS00 = AT_WORDS10 + WORDS - UNIT
+AT_SM = AT_WORDS00 + UNIT
 AT_WGO = AT_SM + UNIT
 AT_WD = AT_WORDS00 + WORDS - UNIT
-AT_WORDS_HALF = AT_WD + 8 * N
-AT_WORDS11 = AT_WORDS_HALF + 4 * WORDS - UNIT
+AT_GATES3 = AT_WD + 8 * N
+AT_WORDS11 = AT_GATES3 + 4 * T - UNIT
 AT_WORDS01 = AT_WORDS11 + WORDS - UNIT
 AT_GATES2 = AT_WORDS01 + WORDS - UNIT
-AT_GATES3 = AT_GATES2 + 4 * T
-AT_TABLE_SCALES = AT_GATES3 + 4 * T - UNIT
+AT_TABLE_SCALES = AT_GATES2 + 4 * T
 AT_LATE_GATES = AT_TABLE_SCALES + T - UNIT
-AT_WD_PLANES = AT_WORDS11 + UNIT
-AT_PASS1_PLANES = AT_TABLE_SCALES + UNIT
 AT_CODES = {1: AT_GATES3, 2: AT_LATE_GATES}
 AT_PAGE2 = AT_LATE_GATES + 4 * T
 
@@ -68,9 +66,8 @@ def tile_list_msg_tanh_res_gateP_kernel(
         lists = [keep.tile([P, J // 16], U16, name=f"list{l}") for l in range(2)]
         tab_w = keep.tile([P, T], I32, name="tab_w", align_bytes=64)
         tab_s = place_tile([P, T], U8, "tab_s", AT_TABLE_SCALES)
-        planes = keep.tile([P, 4 * R + J], U8, name="planes", align_bytes=64)
-        w_planes = planes[:, 0 : 4 * R]
-        pass1_planes = [planes[:, 4 * R :]]
+        w_planes = keep.tile([P, 4 * R], U8, name="w_planes", align_bytes=64)[:]
+        wd_planes = keep.tile([P, 2 * N], U8, name="wd_planes", align_bytes=64)[:]
 
         nc.vector.memset(tab_s[:].bitcast(I32), 0)
         pages = [keep.tile([P, T], F32, name=f"page{t}") for t in range(2)]
@@ -118,33 +115,34 @@ def tile_list_msg_tanh_res_gateP_kernel(
         def offsets(l, j0, n):
             return lists[l][:, j0 // 16 : (j0 + n) // 16]
 
-        pass0_planes = []
+        tab_planes = {}
         parted = {}
 
-        def pick_scales(h, picked):
-            for l in range(2):
-                nc.vector.tensor_copy(picked[:, l * HALF : (l + 1) * HALF], tab_s[:].indirect(offsets(l, h * HALF, HALF)))
-            nc.sync.dma_start(pass1_planes[h].bitcast(I32)[0 : P - 16, :], picked[:].bitcast(I32)[16:P, :])
-            pass0_planes.append(picked)
-
-        def pick_words(j0, n, picked):
-            for l in range(2):
-                nc.vector.tensor_copy(picked[l], tab_w[:].bitcast(U32).indirect(offsets(l, j0, n)))
-            words = keep.tile([P, 2 * 2 * 2 * n], U8, name=f"parted{j0}", align_bytes=64)
-            for l in range(2):
-                nc.vector.tensor_copy(
-                    words[:].bitcast(U16)[:, 2 * l * n : 2 * (l + 1) * n].rearrange("p (a j) -> p a j", a=2),
-                    picked[l].bitcast(U16).rearrange("p (j a) -> p a j", a=2),
-                )
+        def pick_scales(l, j0, picked):
+            n = picked.shape[1]
+            nc.vector.tensor_copy(picked, tab_s[:].indirect(offsets(l, j0, n)))
+            moved = keep.tile([P, n], U8, name=f"moved{l}_{j0}", align_bytes=64)[:]
+            nc.sync.dma_start(moved.bitcast(I32)[0 : P - 16, :], picked.bitcast(I32)[16:P, :])
             for c0 in range(0, n, QUARTER):
-                parted[(j0 + c0) // QUARTER] = (words, n, c0)
+                tab_planes[l, (j0 + c0) // QUARTER] = (picked[:, c0 : c0 + QUARTER], moved[:, c0 : c0 + QUARTER])
 
-        def pick_quarter(q, starts):
-            picked = [place_tile([P, QUARTER], U32, f"picked{q}_{l}", starts[l])[:] for l in range(2)]
-            pick_words(q * QUARTER, QUARTER, picked)
+        def pick_words(l, j0, picked):
+            nc.vector.tensor_copy(picked, tab_w[:].bitcast(U32).indirect(offsets(l, j0, picked.shape[1])))
 
-        pick_scales(0, keep.tile([P, 2 * HALF], U8, name="pass0_planes0", align_bytes=64))
-        pick_quarter(0, (AT_WORDS00, AT_WORDS01))
+        def part_words(l, j0, picked):
+            n = picked.shape[1]
+            words = keep.tile([P, 2, 2 * n], U8, name=f"parted{l}_{j0}", align_bytes=64)
+            nc.vector.tensor_copy(words[:].bitcast(U16), picked.bitcast(U16).rearrange("p (j a) -> p a j", a=2))
+            for c0 in range(0, n, QUARTER):
+                parted[l, (j0 + c0) // QUARTER] = [words[:, a, 2 * c0 : 2 * (c0 + QUARTER)] for a in range(2)]
+
+        starts = {(0, 0): AT_WORDS00, (1, 0): AT_WORDS01, (0, 1): AT_WORDS10, (1, 1): AT_WORDS11}
+        picked = {key: place_tile([P, QUARTER], U32, f"picked{key[1]}_{key[0]}", at)[:] for key, at in starts.items()}
+        pick_scales(0, 0, keep.tile([P, J], U8, name="scales0", align_bytes=64)[:])
+        pick_scales(1, 0, keep.tile([P, HALF], U8, name="scales1", align_bytes=64)[:])
+        for step in (pick_words, part_words):
+            for l in range(2):
+                step(l, 0, picked[l, 0])
 
         late = place_tile([P, 8 * N], U8, "late", AT_WD)
         wd4, wd8, wd_staged = late[:, 0 : 2 * N], late[:, 2 * N : 6 * N], late[:, 6 * N : 8 * N]
@@ -159,18 +157,20 @@ def tile_list_msg_tanh_res_gateP_kernel(
         nc.sync.dma_start(wd4.bitcast(I32), wd4_words[0].bitcast(I32))
         nc.sync.dma_start(wd8.bitcast(I32), wd8_words[0].rearrange("p n i -> p (n i)").bitcast(I32))
 
-        pick_quarter(1, (AT_WORDS10, AT_WORDS11))
-        wd_planes = place_tile([P, 2 * N], U8, "wd_planes", AT_WD_PLANES)[:]
+        for step in (pick_words, part_words):
+            for l in range(2):
+                step(l, QUARTER, picked[l, 1])
         spread_scales(nc.sync, wd_planes, wd_staged)
-        pass1_planes.append(place_tile([P, J], U8, "pass1_planes1", AT_PASS1_PLANES)[:])
-        pick_scales(1, place_tile([P, 2 * HALF], U8, "pass0_planes1", AT_PLANES1))
         gates3 = place_tile([P, T], F32, "gates3", AT_GATES3)
         nc.sync.dma_start(gates3[:], gT_rows[:, 3, :])
+        pick_scales(1, HALF, place_tile([P, HALF], U8, "last_scales", AT_LAST_SCALES)[:])
         late_gates = place_tile([P, 2, T], F32, "late_gates", AT_LATE_GATES)
         nc.sync.dma_start(late_gates[:], gT_rows[:, 0:2, :])
         gates = [late_gates[:, 0, :], late_gates[:, 1, :], gates2[:], gates3[:]]
         picked_half = place_tile([P, 2 * HALF], U32, "picked_half", AT_WORDS_HALF)
-        pick_words(HALF, HALF, [picked_half[:, l * HALF : (l + 1) * HALF] for l in range(2)])
+        for step in (pick_words, part_words):
+            for l in range(2):
+                step(l, HALF, picked_half[:, l * HALF : (l + 1) * HALF])
 
         wy = keep.tile([P, 4, J], F32, name="wy")
         a_banks, tanh_a, tanh_banks = {}, {}, {}
@@ -178,18 +178,16 @@ def tile_list_msg_tanh_res_gateP_kernel(
         y_banks, wy_edges, wy_banks = {}, {}, {}
 
         def first_product(q):
-            words, n, c0 = parted[q]
-            h, j0 = divmod(q * QUARTER, HALF)
-            steps = [(l, a) for a in ((0, 1) if q == 0 else (1, 0)) for l in range(2)]
+            steps = [(l, a) for l in range(2) for a in range(2)]
+            if q == 1:
+                steps = steps[::-1]
             for b in range(2):
                 a_banks[q, b] = psum.tile([P, R], F32, name="a_bank", tag=f"bank{2 * (q % 2) + b}")
                 for i, (l, a) in enumerate(steps):
-                    word_col = (2 * l + a) * n + c0 + b * P
-                    plane_col = l * HALF + j0 + b * P
                     nc.tensor.matmul_mx(
                         a_banks[q, b][:],
-                        lhsT=words[:, 2 * word_col : 2 * (word_col + P)].bitcast(FP4X4),
-                        lhsT_scale=(pass0_planes, pass1_planes)[a][h][:, plane_col : plane_col + P],
+                        lhsT=parted[l, q][a][:, 2 * b * P : 2 * (b + 1) * P].bitcast(FP4X4),
+                        lhsT_scale=tab_planes[l, q][a][:, b * P : (b + 1) * P],
                         rhs=w_words[l][:, 2 * a * R : 2 * (a + 1) * R].bitcast(FP4X4),
                         rhs_scale=w_planes[:, (2 * l + a) * R : (2 * l + a + 1) * R],
                         start=(i == 0),
@@ -305,6 +303,17 @@ def tile_list_msg_tanh_res_gateP_kernel(
                         for early in range(DIRECT_PIECES):
                             weave(early)
 
+        warm_bank = psum.tile([P, R], F32, name="warm_bank", tag="bank7")
+        for i in range(3):
+            nc.tensor.matmul_mx(
+                warm_bank[:],
+                lhsT=w_words[0][:, 0 : 2 * P].bitcast(FP4X4),
+                lhsT_scale=w_planes[:, 0:P],
+                rhs=w_words[0][:, 0 : 2 * R].bitcast(FP4X4),
+                rhs_scale=w_planes[:, 0:R],
+                start=(i == 0),
+                stop=(i == 3 - 1),
+            )
         first_product(0)
         tanh_rows(0, 0)
         tanh_rows(0, 1)
@@ -380,9 +389,12 @@ def tile_list_msg_tanh_res_gateP_kernel(
 
         out_plane = keep.tile([P, STORE_COLS], U8, name="out_plane", align_bytes=64)
         out_words = out_1[0].rearrange("p t i -> p (t i)").bitcast(I32)
-        out_codes = [
-            keep.tile([P, STORE_COLS], I32, name=f"out_codes{s}", align_bytes=64) for s in range(T // STORE_COLS)
-        ]
+        stores = ((0, 1), (2, 3), (4, 5), (6,), (7,))
+        out_codes = {}
+        for group in stores:
+            codes = keep.tile([P, len(group) * PIECE], I32, name=f"out_codes{group[0]}", align_bytes=64)
+            for i, c in enumerate(group):
+                out_codes[c] = (codes, i, group)
 
         def finish(c):
             if c < DIRECT_PIECES:
@@ -394,11 +406,12 @@ def tile_list_msg_tanh_res_gateP_kernel(
 
         def quantise(c):
             s, c0 = divmod(c * PIECE, STORE_COLS)
+            codes, i, group = out_codes[c]
             nc.vector.quantize_mx(
-                out_codes[s][:, c0 : c0 + PIECE].bitcast(FP8X4), out_plane[4 * s :, c0 : c0 + PIECE], woven[c][:]
+                codes[:, i * PIECE : (i + 1) * PIECE].bitcast(FP8X4), out_plane[4 * s :, c0 : c0 + PIECE], woven[c][:]
             )
-            if c0 + PIECE == STORE_COLS:
-                nc.sync.dma_start(out_words[:, s * STORE_COLS : (s + 1) * STORE_COLS], out_codes[s][:])
+            if c == group[-1]:
+                nc.sync.dma_start(out_words[:, group[0] * PIECE : (c + 1) * PIECE], codes[:])
 
         finish(0)
         for c in range(1, n_pieces):

@@ -26,8 +26,8 @@ STORE_COLS = 512
 PIECE = 256
 DIRECT_PIECES = 1
 VECTOR_PIECES = 6
-Y_BANKS = ((4, 5), (4, 0), (4, 0), (4, 0))
-WY_BANKS = ((4, 5), (4, 0), (6, 7), (4, 0))
+Y_BANKS = ((4, 5), (4, 0), (0, 4), (6, 7))
+WY_BANKS = ((4, 5), (4, 5), (0, 4), (6, 7))
 
 UNIT = 64
 WORDS = 4 * QUARTER
@@ -69,7 +69,10 @@ def tile_list_msg_tanh_res_gateP_kernel(
         w_planes = keep.tile([P, 4 * R], U8, name="w_planes", align_bytes=64)[:]
         wd_planes = keep.tile([P, 2 * N], U8, name="wd_planes", align_bytes=64)[:]
 
-        nc.vector.memset(tab_s[:].bitcast(I32), 0)
+        nc.gpsimd.memset(tab_s[:].bitcast(I32), 0)
+        ident = keep.tile([P, P], F32, name="ident")
+        nc.vector.memset(ident[:], 0.0)
+        make_identity(nc, ident[:], nomemset=True)
         pages = [keep.tile([P, T], F32, name=f"page{t}") for t in range(2)]
         for t in range(2):
             nc.vector.memset(pages[t][:].bitcast(I32), 0)
@@ -93,8 +96,6 @@ def tile_list_msg_tanh_res_gateP_kernel(
                     staged.bitcast(I32)[4 * quad : 4 * quad + 4, :],
                 )
 
-        ident = keep.tile([P, P], F32, name="ident")
-        make_identity(nc, ident[:])
 
         nc.sync.dma_start(lists[0][:], offs)
         tab_s_rows = tab_scales.bitcast(I32).rearrange("a (q r) t -> r q a t", r=4)
@@ -275,7 +276,7 @@ def tile_list_msg_tanh_res_gateP_kernel(
 
         out_rows = out_0.rearrange("(p t) c -> t p c", t=4)
         n_pieces = T // PIECE
-        rounded = [keep.tile([P, 2, PIECE, 2], BF16, name=f"rounded{c}") for c in range(n_pieces)]
+        rounded = keep.tile([P, 2, T, 2], BF16, name="rounded", align_bytes=64)
         woven = [keep.tile([P, 4 * PIECE], BF16, name=f"woven{c}", align_bytes=64) for c in range(n_pieces)]
 
         def weave(c):
@@ -283,8 +284,22 @@ def tile_list_msg_tanh_res_gateP_kernel(
             copy, word = (nc.vector.tensor_copy, I32) if on_vector else (nc.scalar.copy, U32)
             copy(
                 woven[c][:].bitcast(word).rearrange("p (j u) -> p j u", u=2),
-                rounded[c][:].rearrange("p u j e -> p u (j e)").bitcast(word).rearrange("p u j -> p j u"),
+                rounded[:].rearrange("p u j e -> p u (j e)").bitcast(word)[:, :, c * PIECE : (c + 1) * PIECE]
+                .rearrange("p u j -> p j u"),
             )
+
+        def round_row(t):
+            early = DIRECT_PIECES * PIECE
+            if t < 2:
+                nc.scalar.copy(rounded[:, 0, :, t], pages[t][:])
+            elif t == 2:
+                nc.scalar.copy(rounded[:, 1, 0:early, :], pages[t][:, 0:early].unsqueeze(2).to_broadcast([P, early, 2]))
+                nc.scalar.copy(rounded[:, 1, early:, 0], pages[t][:, early:])
+                for c in range(DIRECT_PIECES):
+                    weave(c)
+            else:
+                for c0 in range(early, T, PIECE):
+                    nc.scalar.copy(rounded[:, 1, c0 : c0 + PIECE, 1], pages[t][:, c0 : c0 + PIECE])
 
         def place(t, q0, quarters):
             j0, n = q0 * QUARTER, quarters * QUARTER
@@ -293,15 +308,7 @@ def tile_list_msg_tanh_res_gateP_kernel(
             )
             if j0 + n == J:
                 nc.sync.dma_start(out_rows[t], pages[t][:])
-                for c in range(DIRECT_PIECES if t == 3 else 0, n_pieces):
-                    piece = pages[t][:, c * PIECE : (c + 1) * PIECE]
-                    if t == 2 and c < DIRECT_PIECES:
-                        nc.scalar.copy(rounded[c][:, 1, :, :], piece.unsqueeze(2).to_broadcast([P, PIECE, 2]))
-                    else:
-                        nc.scalar.copy(rounded[c][:, t // 2, :, t % 2], piece)
-                    if t == 2 and c == DIRECT_PIECES:
-                        for early in range(DIRECT_PIECES):
-                            weave(early)
+                round_row(t)
 
         warm_bank = psum.tile([P, R], F32, name="warm_bank", tag="bank7")
         for i in range(3):
@@ -369,19 +376,19 @@ def tile_list_msg_tanh_res_gateP_kernel(
         place(1, 1, 1)
         place(2, 1, 1)
         second_product(2)
+        second_product(3)
         weigh(2, 0)
         weigh(2, 1)
         turn_wy(2)
-        second_product(3)
         weigh(3, 0)
         weigh(3, 1)
         turn_wy(3)
         copy_wy(2, 0)
-        place(0, 2, 1)
-        place(1, 2, 1)
         copy_wy(3, 0)
         copy_wy(2, 1)
         copy_wy(3, 1)
+        place(0, 2, 1)
+        place(1, 2, 1)
         place(0, 3, 1)
         place(1, 3, 1)
         place(2, 2, 2)

@@ -26,26 +26,31 @@ STORE_COLS = 512
 PIECE = 256
 DIRECT_PIECES = 1
 VECTOR_PIECES = 6
-Y_BANKS = ((4, 5), (4, 0), (0, 4), (6, 7))
-WY_BANKS = ((4, 5), (4, 5), (0, 4), (6, 7))
+WARM_UPS = 3
+A_BANKS = ((0, 1), (2, 3), (3, 4), (5, 3))
+TURN_BANKS = (0, 4, 0, 6)
+Y_BANKS = ((6, 7, 0, 1), (2, 3, 4, 5))
 
 UNIT = 64
 WORDS = 4 * QUARTER
-AT_WORDS_HALF = 0
+GATES = 4 * T
+AT_PAGE2 = 0
+AT_WORDS_HALF = AT_PAGE2 + GATES - UNIT
 AT_WORDS10 = AT_WORDS_HALF + 4 * WORDS - UNIT
 AT_LAST_SCALES = AT_WORDS10 + UNIT
 AT_WORDS00 = AT_WORDS10 + WORDS - UNIT
-AT_SM = AT_WORDS00 + UNIT
-AT_WGO = AT_SM + UNIT
-AT_WD = AT_WORDS00 + WORDS - UNIT
-AT_GATES3 = AT_WD + 8 * N
-AT_WORDS11 = AT_GATES3 + 4 * T - UNIT
+AT_GATES2 = AT_WORDS00 + WORDS - UNIT
+AT_GATES3 = AT_GATES2 + GATES
+AT_CODES0 = AT_GATES3
+AT_WORDS11 = AT_GATES3 + GATES - UNIT
 AT_WORDS01 = AT_WORDS11 + WORDS - UNIT
-AT_GATES2 = AT_WORDS01 + WORDS - UNIT
-AT_TABLE_SCALES = AT_GATES2 + 4 * T
-AT_LATE_GATES = AT_TABLE_SCALES + T - UNIT
-AT_CODES = {1: AT_GATES3, 2: AT_LATE_GATES}
-AT_PAGE2 = AT_LATE_GATES + 4 * T
+AT_GATES1 = AT_WORDS01 + WORDS - UNIT
+AT_TABLE_SCALES = AT_GATES1 + GATES
+AT_TABLE_WORDS = AT_TABLE_SCALES + T
+AT_WGO = AT_TABLE_WORDS + GATES
+AT_STAGED = AT_WGO + 4 * J - UNIT
+AT_SM = AT_STAGED + UNIT
+AT_WD = AT_SM + UNIT
 
 
 def tile_list_msg_tanh_res_gateP_kernel(
@@ -64,54 +69,47 @@ def tile_list_msg_tanh_res_gateP_kernel(
             return placed.tile(shape, dtype, name=name, offset=offset, align_bytes=UNIT)
 
         lists = [keep.tile([P, J // 16], U16, name=f"list{l}") for l in range(2)]
-        tab_w = keep.tile([P, T], I32, name="tab_w", align_bytes=64)
+        tab_w = place_tile([P, T], I32, "tab_w", AT_TABLE_WORDS)
         tab_s = place_tile([P, T], U8, "tab_s", AT_TABLE_SCALES)
         w_planes = keep.tile([P, 4 * R], U8, name="w_planes", align_bytes=64)[:]
-        wd_planes = keep.tile([P, 2 * N], U8, name="wd_planes", align_bytes=64)[:]
 
         nc.gpsimd.memset(tab_s[:].bitcast(I32), 0)
         ident = keep.tile([P, P], F32, name="ident")
         nc.vector.memset(ident[:], 0.0)
         make_identity(nc, ident[:], nomemset=True)
+        wd_rows = keep.tile([P, N], U8, name="wd_rows", align_bytes=64)
+        nc.vector.memset(wd_rows[:].bitcast(I32), 0)
         pages = [keep.tile([P, T], F32, name=f"page{t}") for t in range(2)]
         for t in range(2):
             nc.vector.memset(pages[t][:].bitcast(I32), 0)
-
-        def stage_scales(staged, sources):
-            words = staged.bitcast(I32)
-            col = 0
-            for scales in sources:
-                passes = scales.shape[0]
-                width = passes * R // 4
-                nc.sync.dma_start(
-                    words[0:SCALE_ROWS, col : col + width].rearrange("q (a n) -> q a n", a=passes),
-                    scales.bitcast(I32).rearrange("a q n -> q a n"),
-                )
-                col = col + width
-
-        def spread_scales(queue, spread, staged):
-            for quad in range(4):
-                queue.dma_start(
-                    spread.bitcast(I32)[32 * quad : 32 * quad + 4, :],
-                    staged.bitcast(I32)[4 * quad : 4 * quad + 4, :],
-                )
-
 
         nc.sync.dma_start(lists[0][:], offs)
         tab_s_rows = tab_scales.bitcast(I32).rearrange("a (q r) t -> r q a t", r=4)
         for r in range(4):
             nc.sync.dma_start(tab_s[:].bitcast(I32)[r:P:16, :], tab_s_rows[r])
         nc.sync.dma_start(lists[1][:], offs2)
-        w_staged = keep.tile([SCALE_ROWS, 4 * R], U8, name="w_staged", align_bytes=64)[:]
+        w_staged = place_tile([SCALE_ROWS, 4 * R], U8, "w_staged", AT_STAGED)[:]
         w_words = [keep.tile([P, 4 * R], U8, name=f"w_words{l}", align_bytes=64) for l in range(2)]
-        stage_scales(w_staged, (ws_scales, wt_scales))
+        for l, scales in enumerate((ws_scales, wt_scales)):
+            nc.sync.dma_start(
+                w_staged.bitcast(I32)[:, l * R // 2 : (l + 1) * R // 2].rearrange("q (a n) -> q a n", a=2),
+                scales.bitcast(I32).rearrange("a q n -> q a n"),
+            )
         nc.sync.dma_start(tab_w[:], tab_words[0].rearrange("p t b -> p (t b)").bitcast(I32))
         for l, words in enumerate((ws_words, wt_words)):
             nc.sync.dma_start(
                 w_words[l][:].bitcast(I32).rearrange("p (a n) -> p a n", a=2),
                 words.bitcast(I32).rearrange("a p n -> p a n"),
             )
-        spread_scales(nc.scalar, w_planes, w_staged)
+        for i, scales in enumerate((wd4_scales, wd8_scales)):
+            rows = scales[0].bitcast(I32).rearrange("(q r) n -> r q n", r=4)
+            for r in range(4):
+                nc.sync.dma_start(wd_rows[:].bitcast(I32)[4 * i + r : P : 32, :], rows[r])
+        for quad in range(4):
+            nc.scalar.dma_start(
+                w_planes.bitcast(I32)[32 * quad : 32 * quad + 4, :],
+                w_staged.bitcast(I32)[4 * quad : 4 * quad + 4, :],
+            )
 
         def offsets(l, j0, n):
             return lists[l][:, j0 // 16 : (j0 + n) // 16]
@@ -119,13 +117,16 @@ def tile_list_msg_tanh_res_gateP_kernel(
         tab_planes = {}
         parted = {}
 
-        def pick_scales(l, j0, picked):
-            n = picked.shape[1]
-            nc.vector.tensor_copy(picked, tab_s[:].indirect(offsets(l, j0, n)))
+        def pick_scales(l, j0, picked_s):
+            n = picked_s.shape[1]
+            nc.vector.tensor_copy(picked_s, tab_s[:].indirect(offsets(l, j0, n)))
             moved = keep.tile([P, n], U8, name=f"moved{l}_{j0}", align_bytes=64)[:]
-            nc.sync.dma_start(moved.bitcast(I32)[0 : P - 16, :], picked.bitcast(I32)[16:P, :])
-            for c0 in range(0, n, QUARTER):
-                tab_planes[l, (j0 + c0) // QUARTER] = (picked[:, c0 : c0 + QUARTER], moved[:, c0 : c0 + QUARTER])
+            nc.sync.dma_start(moved.bitcast(I32)[0 : P - 16, :], picked_s.bitcast(I32)[16:P, :])
+            for c0 in range(0, n, P):
+                tab_planes[l, (j0 + c0) // P] = (picked_s[:, c0 : c0 + P], moved[:, c0 : c0 + P])
+
+        pick_scales(0, 0, keep.tile([P, J], U8, name="scales0", align_bytes=64)[:])
+        pick_scales(1, 0, keep.tile([P, HALF], U8, name="scales1", align_bytes=64)[:])
 
         def pick_words(l, j0, picked):
             nc.vector.tensor_copy(picked, tab_w[:].bitcast(U32).indirect(offsets(l, j0, picked.shape[1])))
@@ -139,56 +140,55 @@ def tile_list_msg_tanh_res_gateP_kernel(
 
         starts = {(0, 0): AT_WORDS00, (1, 0): AT_WORDS01, (0, 1): AT_WORDS10, (1, 1): AT_WORDS11}
         picked = {key: place_tile([P, QUARTER], U32, f"picked{key[1]}_{key[0]}", at)[:] for key, at in starts.items()}
-        pick_scales(0, 0, keep.tile([P, J], U8, name="scales0", align_bytes=64)[:])
-        pick_scales(1, 0, keep.tile([P, HALF], U8, name="scales1", align_bytes=64)[:])
+
+        gT_rows = gT.rearrange("(p t) c -> p t c", t=4)
+        gates = {}
+
+        def load_gates(t, at):
+            gates[t] = place_tile([P, T], F32, f"gates{t}", at)
+            nc.sync.dma_start(gates[t][:], gT_rows[:, t, :])
+
+        wd = place_tile([P, 6 * N], U8, "wd", AT_WD)
+        wd4, wd8 = wd[:, 0 : 2 * N], wd[:, 2 * N : 6 * N]
+        nc.sync.dma_start(wd4.bitcast(I32), wd4_words[0].bitcast(I32))
+        nc.sync.dma_start(wd8.bitcast(I32), wd8_words[0].rearrange("p n i -> p (n i)").bitcast(I32))
+        sm_rows = place_tile([P, 4], F32, "sm_rows", AT_SM)
+        nc.sync.dma_start(sm_rows[:], sm.rearrange("(p t) -> p t", t=4))
+        wgo_rows = place_tile([P, J], F32, "wgo_rows", AT_WGO)
+        nc.sync.dma_start(wgo_rows[:], wgo)
         for step in (pick_words, part_words):
             for l in range(2):
                 step(l, 0, picked[l, 0])
-
-        late = place_tile([P, 8 * N], U8, "late", AT_WD)
-        wd4, wd8, wd_staged = late[:, 0 : 2 * N], late[:, 2 * N : 6 * N], late[:, 6 * N : 8 * N]
-        stage_scales(wd_staged, (wd4_scales, wd8_scales))
-        sm_rows = place_tile([P, 4], F32, "sm_rows", AT_SM)
-        nc.sync.dma_start(sm_rows[:], sm.rearrange("(p t) -> p t", t=4))
-        wgo_rows = place_tile([P, P], F32, "wgo_rows", AT_WGO)
-        nc.sync.dma_start(wgo_rows[:], wgo[0 : P * P // J, :].rearrange("r (b p) -> (r b) p", p=P))
-        gT_rows = gT.rearrange("(p t) c -> p t c", t=4)
-        gates2 = place_tile([P, T], F32, "gates2", AT_GATES2)
-        nc.sync.dma_start(gates2[:], gT_rows[:, 2, :])
-        nc.sync.dma_start(wd4.bitcast(I32), wd4_words[0].bitcast(I32))
-        nc.sync.dma_start(wd8.bitcast(I32), wd8_words[0].rearrange("p n i -> p (n i)").bitcast(I32))
-
+        load_gates(2, AT_GATES2)
+        load_gates(1, AT_GATES1)
         for step in (pick_words, part_words):
             for l in range(2):
                 step(l, QUARTER, picked[l, 1])
-        spread_scales(nc.sync, wd_planes, wd_staged)
-        gates3 = place_tile([P, T], F32, "gates3", AT_GATES3)
-        nc.sync.dma_start(gates3[:], gT_rows[:, 3, :])
+        load_gates(3, AT_GATES3)
         pick_scales(1, HALF, place_tile([P, HALF], U8, "last_scales", AT_LAST_SCALES)[:])
-        late_gates = place_tile([P, 2, T], F32, "late_gates", AT_LATE_GATES)
-        nc.sync.dma_start(late_gates[:], gT_rows[:, 0:2, :])
-        gates = [late_gates[:, 0, :], late_gates[:, 1, :], gates2[:], gates3[:]]
         picked_half = place_tile([P, 2 * HALF], U32, "picked_half", AT_WORDS_HALF)
         for step in (pick_words, part_words):
             for l in range(2):
                 step(l, HALF, picked_half[:, l * HALF : (l + 1) * HALF])
+        load_gates(0, AT_TABLE_WORDS)
+        pages.append(place_tile([P, T], F32, "page2", AT_PAGE2))
+        nc.gpsimd.memset(pages[2][:].bitcast(I32), 0)
+        pages.append(pages[0])
 
-        wy = keep.tile([P, 4, J], F32, name="wy")
-        a_banks, tanh_a, tanh_banks = {}, {}, {}
-        h_rows, h_codes, h_scales = {}, {}, {}
-        y_banks, wy_edges, wy_banks = {}, {}, {}
+        a_banks, tanh_a, tanh_banks, h_rows = {}, {}, {}, {}
+        h_woven, h_codes, h_scales, y_banks, y_rows = {}, {}, {}, {}, {}
 
         def first_product(q):
             steps = [(l, a) for l in range(2) for a in range(2)]
             if q == 1:
                 steps = steps[::-1]
             for b in range(2):
-                a_banks[q, b] = psum.tile([P, R], F32, name="a_bank", tag=f"bank{2 * (q % 2) + b}")
+                a_banks[q, b] = psum.tile([P, R], F32, name="a_bank", tag=f"bank{A_BANKS[q][b]}")
                 for i, (l, a) in enumerate(steps):
                     nc.tensor.matmul_mx(
                         a_banks[q, b][:],
                         lhsT=parted[l, q][a][:, 2 * b * P : 2 * (b + 1) * P].bitcast(FP4X4),
-                        lhsT_scale=tab_planes[l, q][a][:, b * P : (b + 1) * P],
+                        lhsT_scale=tab_planes[l, 2 * q + b][a],
                         rhs=w_words[l][:, 2 * a * R : 2 * (a + 1) * R].bitcast(FP4X4),
                         rhs_scale=w_planes[:, (2 * l + a) * R : (2 * l + a + 1) * R],
                         start=(i == 0),
@@ -201,78 +201,78 @@ def tile_list_msg_tanh_res_gateP_kernel(
 
         def turn_tanh(q):
             for u in range(2):
-                bank = psum.tile([P, 2, QUARTER], F32, name="tanh_bank", tag=f"bank{2 * (q % 2) + u}")
+                bank = psum.tile([P, 2, QUARTER], F32, name="tanh_bank", tag=f"bank{TURN_BANKS[q] + u}")
                 for e in range(2):
                     tanh_banks[q, 2 * u + e] = bank[:, e, :]
                     for b in range(2):
                         nc.tensor.transpose(bank[:, e, b * P : (b + 1) * P], tanh_a[q, b][:, 2 * u + e, :], ident[:])
 
-        def scale_rows(q, parts=1):
+        def scale_rows(q):
             h_rows[q] = keep.tile([P, 4, QUARTER], BF16, name=f"h_rows{q}", tag=f"h_rows{q}", align_bytes=64)
-            n = QUARTER // parts
-            for j0 in range(0, QUARTER, n):
-                for t in range(4):
-                    nc.scalar.activation(
-                        h_rows[q][:, t, j0 : j0 + n], tanh_banks[q, t][:, j0 : j0 + n], COPY, scale=sm_rows[:, t : t + 1]
-                    )
+            for t in range(4):
+                nc.scalar.activation(h_rows[q][:, t, :], tanh_banks[q, t], COPY, scale=sm_rows[:, t : t + 1])
 
-        def quantise_h(q, parts=1):
-            h_woven = keep.tile([P, 4 * QUARTER], BF16, name=f"h_woven{q}", tag=f"h_woven{q}", align_bytes=64)
-            n = QUARTER // parts
-            for j0 in range(0, QUARTER, n):
-                nc.scalar.copy(
-                    h_woven[:, 4 * j0 : 4 * (j0 + n)].rearrange("p (c i t) -> p c t i", i=4, t=4),
-                    h_rows[q][:, :, j0 : j0 + n].rearrange("p t (c i) -> p c t i", i=4),
-                )
-            if q in AT_CODES:
-                h_codes[q] = place_tile([P, QUARTER], U32, f"h_codes{q}", AT_CODES[q])
-            else:
-                h_codes[q] = keep.tile([P, QUARTER], U32, name=f"h_codes{q}", align_bytes=64)
-            h_scales[q] = keep.tile([P, QUARTER], U8, name=f"h_scales{q}", align_bytes=64)
-            nc.vector.quantize_mx(h_codes[q][:].bitcast(FP8X4), h_scales[q][:], h_woven[:])
-
-        def second_product(q):
-            for b in range(2):
-                y_banks[q, b] = psum.tile([P, N], F32, name="y_bank", tag=f"bank{Y_BANKS[q][b]}")
-                for i, (w, fmt) in enumerate(((wd4, FP4X4), (wd8, FP8X4))):
-                    nc.tensor.matmul_mx(
-                        y_banks[q, b][:],
-                        lhsT=h_codes[q][:, b * P : (b + 1) * P].bitcast(FP8X4),
-                        lhsT_scale=h_scales[q][:, b * P : (b + 1) * P],
-                        rhs=w.bitcast(fmt),
-                        rhs_scale=wd_planes[:, i * N : (i + 1) * N],
-                        start=(i == 0),
-                        stop=(i == 1),
-                    )
-
-        def weigh(q, b):
-            wy_edges[q, b] = ring.tile([P, 4, P], F32, name="wy_edges")
-            nc.scalar.activation(
-                wy_edges[q, b][:],
-                y_banks[q, b][:].rearrange("p (m t) -> p t m", t=4),
-                COPY,
-                scale=wgo_cols[:, 2 * q + b : 2 * q + b + 1],
+        def weave_h(q):
+            if q % 2 == 0:
+                h_woven[q // 2] = keep.tile([P, 4 * HALF], BF16, name=f"h_woven{q // 2}", align_bytes=64)
+            c0 = 4 * QUARTER * (q % 2)
+            nc.scalar.copy(
+                h_woven[q // 2][:, c0 : c0 + 4 * QUARTER].rearrange("p (c i t) -> p c t i", i=4, t=4),
+                h_rows[q][:].rearrange("p t (c i) -> p c t i", i=4),
             )
 
-        def turn_wy(q):
-            for u in range(2):
-                wy_banks[q, u] = psum.tile([P, 2, QUARTER], F32, name="wy_bank", tag=f"bank{WY_BANKS[q][u]}")
-                for e in range(2):
-                    for b in range(2):
-                        nc.tensor.transpose(
-                            wy_banks[q, u][:, e, b * P : (b + 1) * P], wy_edges[q, b][:, 2 * u + e, :], ident[:]
-                        )
+        def quantise_h(half, codes):
+            h_codes[half] = codes
+            h_scales[half] = keep.tile([P, HALF], U8, name=f"h_scales{half}", align_bytes=64)
+            nc.vector.quantize_mx(codes[:].bitcast(FP8X4), h_scales[half][:], h_woven[half][:])
 
-        def copy_wy(q, u):
-            nc.scalar.copy(wy[:, 2 * u : 2 * u + 2, q * QUARTER : (q + 1) * QUARTER], wy_banks[q, u][:])
+        dealt4 = keep.tile([P, 2 * N], U8, name="dealt4", align_bytes=64)
+        dealt8 = keep.tile([P, N], U32, name="dealt8", align_bytes=64)
+        dealt_s = keep.tile([P, N], U8, name="dealt_s", align_bytes=64)
+
+        def deal_words():
+            nc.scalar.copy(
+                dealt4[:].bitcast(U16).rearrange("p (t m) -> p t m", t=4), wd4.bitcast(U16).rearrange("p (m t) -> p t m", t=4)
+            )
+            nc.scalar.copy(
+                dealt8[:].rearrange("p (t m) -> p t m", t=4), wd8.bitcast(U32).rearrange("p (m t) -> p t m", t=4)
+            )
+
+        def deal_scales():
+            nc.vector.tensor_copy(
+                dealt_s[:].rearrange("p (t m) -> p t m", t=4), wd_rows[:].rearrange("p (m t) -> p t m", t=4)
+            )
+
+        def second_product(t, half):
+            y_banks[t, half] = psum.tile([P, HALF], F32, name="y_bank", tag=f"bank{Y_BANKS[half][t]}")
+            cols = slice(t * P, (t + 1) * P)
+            nc.tensor.matmul_mx(
+                y_banks[t, half][:],
+                lhsT=dealt4[:, 2 * t * P : 2 * (t + 1) * P].bitcast(FP4X4),
+                lhsT_scale=dealt_s[:, cols],
+                rhs=h_codes[half][:].bitcast(FP8X4),
+                rhs_scale=h_scales[half][:],
+                start=True,
+                stop=False,
+            )
+            nc.tensor.matmul_mx(
+                y_banks[t, half][:],
+                lhsT=dealt8[:, cols].bitcast(FP8X4),
+                lhsT_scale=dealt_s[4:, cols],
+                rhs=h_codes[half][:].bitcast(FP8X4),
+                rhs_scale=h_scales[half][:],
+                start=False,
+                stop=True,
+            )
+
+        def copy_y(t, half):
+            nc.scalar.copy(y_rows[t, half], y_banks[t, half][:])
 
         picked_gates = {}
 
-        def pick_gates(rows, tag):
-            picked = keep.tile([P, len(rows), J], F32, name=f"picked_gates{rows[0]}", tag=tag, align_bytes=64)
-            for i, t in enumerate(rows):
-                picked_gates[t] = picked[:, i, :]
-                nc.vector.tensor_copy(picked_gates[t], gates[t].indirect(offsets(0, 0, J)))
+        def pick_gates(t, picked_t):
+            picked_gates[t] = picked_t
+            nc.vector.tensor_tensor(picked_t[:], gates[t][:].indirect(lists[0][:]), wgo_rows[:], MULT)
 
         out_rows = out_0.rearrange("(p t) c -> t p c", t=4)
         n_pieces = T // PIECE
@@ -301,17 +301,16 @@ def tile_list_msg_tanh_res_gateP_kernel(
                 for c0 in range(early, T, PIECE):
                     nc.scalar.copy(rounded[:, 1, c0 : c0 + PIECE, 1], pages[t][:, c0 : c0 + PIECE])
 
-        def place(t, q0, quarters):
-            j0, n = q0 * QUARTER, quarters * QUARTER
+        def place(t, j0, n):
             nc.vector.tensor_tensor(
-                pages[t][:].indirect(offsets(1, j0, n)), wy[:, t, j0 : j0 + n], picked_gates[t][:, j0 : j0 + n], MULT
+                pages[t][:].indirect(offsets(1, j0, n)), y_rows[t, j0 // HALF] if n == HALF else y_last[:], picked_gates[t][:, j0 : j0 + n], MULT
             )
             if j0 + n == J:
                 nc.sync.dma_start(out_rows[t], pages[t][:])
                 round_row(t)
 
         warm_bank = psum.tile([P, R], F32, name="warm_bank", tag="bank7")
-        for i in range(3):
+        for i in range(WARM_UPS):
             nc.tensor.matmul_mx(
                 warm_bank[:],
                 lhsT=w_words[0][:, 0 : 2 * P].bitcast(FP4X4),
@@ -319,80 +318,64 @@ def tile_list_msg_tanh_res_gateP_kernel(
                 rhs=w_words[0][:, 0 : 2 * R].bitcast(FP4X4),
                 rhs_scale=w_planes[:, 0:R],
                 start=(i == 0),
-                stop=(i == 3 - 1),
+                stop=(i == WARM_UPS - 1),
             )
+        deal_scales()
+        deal_words()
         first_product(0)
         tanh_rows(0, 0)
         tanh_rows(0, 1)
         turn_tanh(0)
         first_product(1)
-        pick_gates((2,), "picked_gates2")
         tanh_rows(1, 0)
         scale_rows(0)
         tanh_rows(1, 1)
         turn_tanh(1)
-        quantise_h(0)
-        pick_gates((3,), "h_rows0")
+        weave_h(0)
         scale_rows(1)
-
-        wgo_bank = psum.tile([P, N], F32, name="wgo_bank", tag="bank6")
-        nc.tensor.transpose(wgo_bank[:, 0:P], wgo_rows[:], ident[:])
-        wgo_cols = keep.tile([P, J // P], F32, name="wgo_cols")
-        nc.scalar.copy(wgo_cols[:], wgo_bank[:, 0 : J // P])
-
         first_product(2)
         tanh_rows(2, 0)
-        quantise_h(1)
-        pick_gates((0, 1), "h_rows1")
-        pages.append(place_tile([P, T], F32, "page2", AT_PAGE2))
-        nc.gpsimd.memset(pages[2][:].bitcast(I32), 0)
-        pages.append(pages[0])
+        weave_h(1)
         tanh_rows(2, 1)
         turn_tanh(2)
-        second_product(0)
-        weigh(0, 0)
-        weigh(0, 1)
-        turn_wy(0)
+        for t in (2, 1, 3):
+            pick_gates(t, keep.tile([P, J], F32, name=f"picked_gates{t}"))
+        quantise_h(0, place_tile([P, HALF], U32, "h_codes0", AT_CODES0))
+        pick_gates(0, keep.tile([P, J], F32, name="picked_gates0"))
         first_product(3)
         tanh_rows(3, 0)
-        copy_wy(0, 0)
-        place(0, 0, 1)
-        place(1, 0, 1)
         scale_rows(2)
         tanh_rows(3, 1)
+        weave_h(2)
+        for t in range(2):
+            second_product(t, 0)
+        y_rows[0, 0] = keep.tile([P, HALF], F32, name="y_row00", tag="y_row00", align_bytes=64)[:]
+        y_rows[1, 0] = place_tile([P, HALF], F32, "y_row10", AT_TABLE_WORDS)[:]
+        copy_y(0, 0)
+        place(0, 0, HALF)
+        copy_y(1, 0)
+        place(1, 0, HALF)
         turn_tanh(3)
-        quantise_h(2)
-        copy_wy(0, 1)
-        place(2, 0, 1)
-        second_product(1)
-        weigh(1, 0)
-        scale_rows(3, 2)
-        weigh(1, 1)
-        turn_wy(1)
-        quantise_h(3, 2)
-        copy_wy(1, 0)
-        copy_wy(1, 1)
-        place(0, 1, 1)
-        place(1, 1, 1)
-        place(2, 1, 1)
-        second_product(2)
-        second_product(3)
-        weigh(2, 0)
-        weigh(2, 1)
-        turn_wy(2)
-        weigh(3, 0)
-        weigh(3, 1)
-        turn_wy(3)
-        copy_wy(2, 0)
-        copy_wy(3, 0)
-        copy_wy(2, 1)
-        copy_wy(3, 1)
-        place(0, 2, 1)
-        place(1, 2, 1)
-        place(0, 3, 1)
-        place(1, 3, 1)
-        place(2, 2, 2)
-        place(3, 0, 4)
+        for t in range(2, 4):
+            second_product(t, 0)
+        scale_rows(3)
+        weave_h(3)
+        quantise_h(1, keep.tile([P, HALF], U32, name="h_codes1", tag="y_row00", align_bytes=64))
+        y_rows[2, 0] = keep.tile([P, HALF], F32, name="y_row20", tag="h_rows3", align_bytes=64)[:]
+        for t in range(3):
+            y_rows[t, 1] = keep.tile([P, HALF], F32, name=f"y_row{t}1")[:]
+        y_last = keep.tile([P, J], F32, name="y_last")
+        for half in range(2):
+            y_rows[3, half] = y_last[:, half * HALF : (half + 1) * HALF]
+        copy_y(2, 0)
+        place(2, 0, HALF)
+        copy_y(3, 0)
+        for t in range(4):
+            second_product(t, 1)
+            copy_y(t, 1)
+        for t in range(3):
+            place(t, HALF, HALF)
+        place(3, 0, J)
 
         out_plane = keep.tile([P, STORE_COLS], U8, name="out_plane", align_bytes=64)
         out_words = out_1[0].rearrange("p t i -> p (t i)").bitcast(I32)

@@ -40,17 +40,19 @@ AT_WORDS10 = AT_WORDS_HALF + 4 * WORDS - UNIT
 AT_LAST_SCALES = AT_WORDS10 + UNIT
 AT_WORDS00 = AT_WORDS10 + WORDS - UNIT
 AT_GATES2 = AT_WORDS00 + WORDS - UNIT
-AT_GATES3 = AT_GATES2 + GATES
-AT_CODES0 = AT_GATES3
-AT_WORDS11 = AT_GATES3 + GATES - UNIT
+AT_WORDS11 = AT_GATES2 + GATES
 AT_WORDS01 = AT_WORDS11 + WORDS - UNIT
-AT_GATES1 = AT_WORDS01 + WORDS - UNIT
-AT_TABLE_SCALES = AT_GATES1 + GATES
-AT_TABLE_WORDS = AT_TABLE_SCALES + T
+AT_GATES3 = AT_WORDS01 + WORDS
+AT_CODES0 = AT_GATES3
+AT_TABLE_SCALES = AT_GATES3 + GATES - UNIT
+AT_DEALT = AT_TABLE_SCALES + UNIT
+AT_GATES1 = AT_TABLE_SCALES + T - UNIT
+AT_TABLE_WORDS = AT_GATES1 + GATES
 AT_WGO = AT_TABLE_WORDS + GATES
 AT_STAGED = AT_WGO + 4 * J - UNIT
 AT_SM = AT_STAGED + UNIT
-AT_WD = AT_SM + UNIT
+AT_WD_STAGED = AT_SM + UNIT
+AT_WD = AT_WD_STAGED + 2 * N
 
 
 def tile_list_msg_tanh_res_gateP_kernel(
@@ -77,8 +79,8 @@ def tile_list_msg_tanh_res_gateP_kernel(
         ident = keep.tile([P, P], F32, name="ident")
         nc.vector.memset(ident[:], 0.0)
         make_identity(nc, ident[:], nomemset=True)
-        wd_rows = keep.tile([P, N], U8, name="wd_rows", align_bytes=64)
-        nc.vector.memset(wd_rows[:].bitcast(I32), 0)
+        wd_planes = keep.tile([P, 2 * N], U8, name="wd_planes", align_bytes=64)[:]
+        nc.vector.memset(wd_planes.bitcast(I32), 0)
         pages = [keep.tile([P, T], F32, name=f"page{t}") for t in range(2)]
         for t in range(2):
             nc.vector.memset(pages[t][:].bitcast(I32), 0)
@@ -101,10 +103,6 @@ def tile_list_msg_tanh_res_gateP_kernel(
                 w_words[l][:].bitcast(I32).rearrange("p (a n) -> p a n", a=2),
                 words.bitcast(I32).rearrange("a p n -> p a n"),
             )
-        for i, scales in enumerate((wd4_scales, wd8_scales)):
-            rows = scales[0].bitcast(I32).rearrange("(q r) n -> r q n", r=4)
-            for r in range(4):
-                nc.sync.dma_start(wd_rows[:].bitcast(I32)[4 * i + r : P : 32, :], rows[r])
         for quad in range(4):
             nc.scalar.dma_start(
                 w_planes.bitcast(I32)[32 * quad : 32 * quad + 4, :],
@@ -154,18 +152,25 @@ def tile_list_msg_tanh_res_gateP_kernel(
         nc.sync.dma_start(wd8.bitcast(I32), wd8_words[0].rearrange("p n i -> p (n i)").bitcast(I32))
         sm_rows = place_tile([P, 4], F32, "sm_rows", AT_SM)
         nc.sync.dma_start(sm_rows[:], sm.rearrange("(p t) -> p t", t=4))
+        wd_staged = place_tile([SCALE_ROWS, 2 * N], U8, "wd_staged", AT_WD_STAGED)[:]
+        for i, scales in enumerate((wd4_scales, wd8_scales)):
+            nc.sync.dma_start(wd_staged.bitcast(I32)[:, i * N // 4 : (i + 1) * N // 4], scales[0].bitcast(I32))
+        for quad in range(4):
+            nc.sync.dma_start(
+                wd_planes.bitcast(I32)[32 * quad : 32 * quad + 4, :], wd_staged.bitcast(I32)[4 * quad : 4 * quad + 4, :]
+            )
         wgo_rows = place_tile([P, J], F32, "wgo_rows", AT_WGO)
         nc.sync.dma_start(wgo_rows[:], wgo)
         for step in (pick_words, part_words):
             for l in range(2):
                 step(l, 0, picked[l, 0])
         load_gates(2, AT_GATES2)
-        load_gates(1, AT_GATES1)
         for step in (pick_words, part_words):
             for l in range(2):
                 step(l, QUARTER, picked[l, 1])
-        load_gates(3, AT_GATES3)
         pick_scales(1, HALF, place_tile([P, HALF], U8, "last_scales", AT_LAST_SCALES)[:])
+        load_gates(1, AT_GATES1)
+        load_gates(3, AT_GATES3)
         picked_half = place_tile([P, 2 * HALF], U32, "picked_half", AT_WORDS_HALF)
         for step in (pick_words, part_words):
             for l in range(2):
@@ -228,7 +233,7 @@ def tile_list_msg_tanh_res_gateP_kernel(
 
         dealt4 = keep.tile([P, 2 * N], U8, name="dealt4", align_bytes=64)
         dealt8 = keep.tile([P, N], U32, name="dealt8", align_bytes=64)
-        dealt_s = keep.tile([P, N], U8, name="dealt_s", align_bytes=64)
+        dealt_s = place_tile([P, 2, N], U8, "dealt_s", AT_DEALT)
 
         def deal_words():
             nc.scalar.copy(
@@ -240,7 +245,8 @@ def tile_list_msg_tanh_res_gateP_kernel(
 
         def deal_scales():
             nc.vector.tensor_copy(
-                dealt_s[:].rearrange("p (t m) -> p t m", t=4), wd_rows[:].rearrange("p (m t) -> p t m", t=4)
+                dealt_s[:].rearrange("p i (t m) -> p i t m", t=4),
+                wd_planes.rearrange("p (i m t) -> p i t m", i=2, t=4),
             )
 
         def second_product(t, half):
@@ -249,7 +255,7 @@ def tile_list_msg_tanh_res_gateP_kernel(
             nc.tensor.matmul_mx(
                 y_banks[t, half][:],
                 lhsT=dealt4[:, 2 * t * P : 2 * (t + 1) * P].bitcast(FP4X4),
-                lhsT_scale=dealt_s[:, cols],
+                lhsT_scale=dealt_s[:, 0, cols],
                 rhs=h_codes[half][:].bitcast(FP8X4),
                 rhs_scale=h_scales[half][:],
                 start=True,
@@ -258,7 +264,7 @@ def tile_list_msg_tanh_res_gateP_kernel(
             nc.tensor.matmul_mx(
                 y_banks[t, half][:],
                 lhsT=dealt8[:, cols].bitcast(FP8X4),
-                lhsT_scale=dealt_s[4:, cols],
+                lhsT_scale=dealt_s[:, 1, cols],
                 rhs=h_codes[half][:].bitcast(FP8X4),
                 rhs_scale=h_scales[half][:],
                 start=False,

@@ -51,8 +51,6 @@ AT_TABLE_WORDS = AT_GATES1 + GATES
 AT_WGO = AT_TABLE_WORDS + GATES
 AT_STAGED = AT_WGO + 4 * J - UNIT
 AT_SM = AT_STAGED + UNIT
-AT_WD_STAGED = AT_SM + UNIT
-AT_WD = AT_WD_STAGED + 2 * N
 
 
 def tile_list_msg_tanh_res_gateP_kernel(
@@ -76,16 +74,20 @@ def tile_list_msg_tanh_res_gateP_kernel(
         w_planes = keep.tile([P, 4 * R], U8, name="w_planes", align_bytes=64)[:]
 
         nc.gpsimd.memset(tab_s[:].bitcast(I32), 0)
+        wd_staged = keep.tile([P, 2 * N], U8, name="wd_staged", align_bytes=64)[:]
+        nc.vector.memset(wd_staged.bitcast(I32), 0)
         ident = keep.tile([P, P], F32, name="ident")
         nc.vector.memset(ident[:], 0.0)
         make_identity(nc, ident[:], nomemset=True)
-        wd_planes = keep.tile([P, 2 * N], U8, name="wd_planes", align_bytes=64)[:]
-        nc.vector.memset(wd_planes.bitcast(I32), 0)
         pages = [keep.tile([P, T], F32, name=f"page{t}") for t in range(2)]
         for t in range(2):
             nc.vector.memset(pages[t][:].bitcast(I32), 0)
 
         nc.sync.dma_start(lists[0][:], offs)
+        for i, scales in enumerate((wd4_scales, wd8_scales)):
+            nc.sync.dma_start(
+                wd_staged.bitcast(I32)[0:SCALE_ROWS, i * N // 4 : (i + 1) * N // 4], scales[0].bitcast(I32)
+            )
         tab_s_rows = tab_scales.bitcast(I32).rearrange("a (q r) t -> r q a t", r=4)
         for r in range(4):
             nc.sync.dma_start(tab_s[:].bitcast(I32)[r:P:16, :], tab_s_rows[r])
@@ -103,11 +105,20 @@ def tile_list_msg_tanh_res_gateP_kernel(
                 w_words[l][:].bitcast(I32).rearrange("p (a n) -> p a n", a=2),
                 words.bitcast(I32).rearrange("a p n -> p a n"),
             )
+        wd = keep.tile([P, 6 * N], U8, name="wd", align_bytes=64)
+        wd4, wd8 = wd[:, 0 : 2 * N], wd[:, 2 * N : 6 * N]
+        nc.sync.dma_start(wd4.bitcast(I32), wd4_words[0].bitcast(I32))
+        nc.sync.dma_start(wd8.bitcast(I32), wd8_words[0].rearrange("p n i -> p (n i)").bitcast(I32))
         for quad in range(4):
             nc.scalar.dma_start(
                 w_planes.bitcast(I32)[32 * quad : 32 * quad + 4, :],
                 w_staged.bitcast(I32)[4 * quad : 4 * quad + 4, :],
             )
+
+        dealt_rows = keep.tile([P, 2 * N], U8, name="dealt_rows", align_bytes=64)[:]
+        nc.vector.tensor_copy(
+            dealt_rows.rearrange("p (i t m) -> p i t m", i=2, t=4), wd_staged.rearrange("p (i m t) -> p i t m", i=2, t=4)
+        )
 
         def offsets(l, j0, n):
             return lists[l][:, j0 // 16 : (j0 + n) // 16]
@@ -146,19 +157,8 @@ def tile_list_msg_tanh_res_gateP_kernel(
             gates[t] = place_tile([P, T], F32, f"gates{t}", at)
             nc.sync.dma_start(gates[t][:], gT_rows[:, t, :])
 
-        wd = place_tile([P, 6 * N], U8, "wd", AT_WD)
-        wd4, wd8 = wd[:, 0 : 2 * N], wd[:, 2 * N : 6 * N]
-        nc.sync.dma_start(wd4.bitcast(I32), wd4_words[0].bitcast(I32))
-        nc.sync.dma_start(wd8.bitcast(I32), wd8_words[0].rearrange("p n i -> p (n i)").bitcast(I32))
         sm_rows = place_tile([P, 4], F32, "sm_rows", AT_SM)
         nc.sync.dma_start(sm_rows[:], sm.rearrange("(p t) -> p t", t=4))
-        wd_staged = place_tile([SCALE_ROWS, 2 * N], U8, "wd_staged", AT_WD_STAGED)[:]
-        for i, scales in enumerate((wd4_scales, wd8_scales)):
-            nc.sync.dma_start(wd_staged.bitcast(I32)[:, i * N // 4 : (i + 1) * N // 4], scales[0].bitcast(I32))
-        for quad in range(4):
-            nc.sync.dma_start(
-                wd_planes.bitcast(I32)[32 * quad : 32 * quad + 4, :], wd_staged.bitcast(I32)[4 * quad : 4 * quad + 4, :]
-            )
         wgo_rows = place_tile([P, J], F32, "wgo_rows", AT_WGO)
         nc.sync.dma_start(wgo_rows[:], wgo)
         for step in (pick_words, part_words):
@@ -171,6 +171,12 @@ def tile_list_msg_tanh_res_gateP_kernel(
         pick_scales(1, HALF, place_tile([P, HALF], U8, "last_scales", AT_LAST_SCALES)[:])
         load_gates(1, AT_GATES1)
         load_gates(3, AT_GATES3)
+        dealt_s = place_tile([P, 2, N], U8, "dealt_s", AT_DEALT)
+        for quad in range(4):
+            nc.sync.dma_start(
+                dealt_s[:].rearrange("p i n -> p (i n)").bitcast(I32)[32 * quad : 32 * quad + 4, :],
+                dealt_rows.bitcast(I32)[4 * quad : 4 * quad + 4, :],
+            )
         picked_half = place_tile([P, 2 * HALF], U32, "picked_half", AT_WORDS_HALF)
         for step in (pick_words, part_words):
             for l in range(2):
@@ -233,7 +239,6 @@ def tile_list_msg_tanh_res_gateP_kernel(
 
         dealt4 = keep.tile([P, 2 * N], U8, name="dealt4", align_bytes=64)
         dealt8 = keep.tile([P, N], U32, name="dealt8", align_bytes=64)
-        dealt_s = place_tile([P, 2, N], U8, "dealt_s", AT_DEALT)
 
         def deal_words():
             nc.scalar.copy(
@@ -241,12 +246,6 @@ def tile_list_msg_tanh_res_gateP_kernel(
             )
             nc.scalar.copy(
                 dealt8[:].rearrange("p (t m) -> p t m", t=4), wd8.bitcast(U32).rearrange("p (m t) -> p t m", t=4)
-            )
-
-        def deal_scales():
-            nc.vector.tensor_copy(
-                dealt_s[:].rearrange("p i (t m) -> p i t m", t=4),
-                wd_planes.rearrange("p (i m t) -> p i t m", i=2, t=4),
             )
 
         def second_product(t, half):
@@ -276,9 +275,13 @@ def tile_list_msg_tanh_res_gateP_kernel(
 
         picked_gates = {}
 
-        def pick_gates(t, picked_t):
+        def pick_gates(t, picked_t, parts=1):
             picked_gates[t] = picked_t
-            nc.vector.tensor_tensor(picked_t[:], gates[t][:].indirect(lists[0][:]), wgo_rows[:], MULT)
+            n = J // parts
+            for j0 in range(0, J, n):
+                nc.vector.tensor_tensor(
+                    picked_t[:, j0 : j0 + n], gates[t][:].indirect(offsets(0, j0, n)), wgo_rows[:, j0 : j0 + n], MULT
+                )
 
         out_rows = out_0.rearrange("(p t) c -> t p c", t=4)
         n_pieces = T // PIECE
@@ -326,7 +329,6 @@ def tile_list_msg_tanh_res_gateP_kernel(
                 start=(i == 0),
                 stop=(i == WARM_UPS - 1),
             )
-        deal_scales()
         deal_words()
         first_product(0)
         tanh_rows(0, 0)
@@ -347,7 +349,7 @@ def tile_list_msg_tanh_res_gateP_kernel(
         for t in (2, 1, 3):
             pick_gates(t, keep.tile([P, J], F32, name=f"picked_gates{t}"))
         quantise_h(0, place_tile([P, HALF], U32, "h_codes0", AT_CODES0))
-        pick_gates(0, keep.tile([P, J], F32, name="picked_gates0"))
+        pick_gates(0, keep.tile([P, J], F32, name="picked_gates0"), 2)
         first_product(3)
         tanh_rows(3, 0)
         scale_rows(2)

@@ -34,12 +34,13 @@ Y_BANKS = ((6, 7, 0, 1), (2, 3, 4, 5))
 UNIT = 64
 WORDS = 4 * QUARTER
 GATES = 4 * T
-AT_PAGE2 = 0
-AT_WORDS_HALF = AT_PAGE2 + GATES - UNIT
+AT_PAGE1 = 0
+AT_WORDS_HALF = AT_PAGE1 + GATES - UNIT
 AT_WORDS10 = AT_WORDS_HALF + 4 * WORDS - UNIT
 AT_LAST_SCALES = AT_WORDS10 + UNIT
 AT_WORDS00 = AT_WORDS10 + WORDS - UNIT
 AT_GATES2 = AT_WORDS00 + WORDS - UNIT
+AT_PAGE2 = AT_GATES2
 AT_WORDS11 = AT_GATES2 + GATES
 AT_WORDS01 = AT_WORDS11 + WORDS - UNIT
 AT_GATES3 = AT_WORDS01 + WORDS
@@ -79,9 +80,8 @@ def tile_list_msg_tanh_res_gateP_kernel(
         ident = keep.tile([P, P], F32, name="ident")
         nc.vector.memset(ident[:], 0.0)
         make_identity(nc, ident[:], nomemset=True)
-        pages = [keep.tile([P, T], F32, name=f"page{t}") for t in range(2)]
-        for t in range(2):
-            nc.vector.memset(pages[t][:].bitcast(I32), 0)
+        pages = [keep.tile([P, T], F32, name="page0")]
+        nc.vector.memset(pages[0][:].bitcast(I32), 0)
 
         nc.sync.dma_start(lists[0][:], offs)
         for i, scales in enumerate((wd4_scales, wd8_scales)):
@@ -119,6 +119,18 @@ def tile_list_msg_tanh_res_gateP_kernel(
         nc.vector.tensor_copy(
             dealt_rows.rearrange("p (i t m) -> p i t m", i=2, t=4), wd_staged.rearrange("p (i m t) -> p i t m", i=2, t=4)
         )
+
+        warm_bank = psum.tile([P, R], F32, name="warm_bank", tag="bank7")
+        for i in range(WARM_UPS):
+            nc.tensor.matmul_mx(
+                warm_bank[:],
+                lhsT=tab_w[:].bitcast(U8)[:, 0 : 2 * P].bitcast(FP4X4),
+                lhsT_scale=tab_s[:, 0:P],
+                rhs=tab_w[:].bitcast(U8)[:, 0 : 2 * R].bitcast(FP4X4),
+                rhs_scale=tab_s[:, 0:R],
+                start=(i == 0),
+                stop=(i == WARM_UPS - 1),
+            )
 
         def offsets(l, j0, n):
             return lists[l][:, j0 // 16 : (j0 + n) // 16]
@@ -182,9 +194,12 @@ def tile_list_msg_tanh_res_gateP_kernel(
             for l in range(2):
                 step(l, HALF, picked_half[:, l * HALF : (l + 1) * HALF])
         load_gates(0, AT_TABLE_WORDS)
-        pages.append(place_tile([P, T], F32, "page2", AT_PAGE2))
-        nc.gpsimd.memset(pages[2][:].bitcast(I32), 0)
-        pages.append(pages[0])
+
+        def clear_page(t, at):
+            pages.append(place_tile([P, T], F32, f"page{t}", at))
+            nc.gpsimd.memset(pages[t][:].bitcast(I32), 0)
+
+        clear_page(1, AT_PAGE1)
 
         a_banks, tanh_a, tanh_banks, h_rows = {}, {}, {}, {}
         h_woven, h_codes, h_scales, y_banks, y_rows = {}, {}, {}, {}, {}
@@ -224,8 +239,10 @@ def tile_list_msg_tanh_res_gateP_kernel(
                 nc.scalar.activation(h_rows[q][:, t, :], tanh_banks[q, t], COPY, scale=sm_rows[:, t : t + 1])
 
         def weave_h(q):
-            if q % 2 == 0:
-                h_woven[q // 2] = keep.tile([P, 4 * HALF], BF16, name=f"h_woven{q // 2}", align_bytes=64)
+            if q == 0:
+                h_woven[0] = keep.tile([P, 4 * HALF], BF16, name="h_woven0", align_bytes=64)
+            if q == 2:
+                h_woven[1] = place_tile([P, 4 * HALF], BF16, "h_woven1", AT_TABLE_WORDS + 4 * HALF)
             c0 = 4 * QUARTER * (q % 2)
             nc.scalar.copy(
                 h_woven[q // 2][:, c0 : c0 + 4 * QUARTER].rearrange("p (c i t) -> p c t i", i=4, t=4),
@@ -318,17 +335,6 @@ def tile_list_msg_tanh_res_gateP_kernel(
                 nc.sync.dma_start(out_rows[t], pages[t][:])
                 round_row(t)
 
-        warm_bank = psum.tile([P, R], F32, name="warm_bank", tag="bank7")
-        for i in range(WARM_UPS):
-            nc.tensor.matmul_mx(
-                warm_bank[:],
-                lhsT=w_words[0][:, 0 : 2 * P].bitcast(FP4X4),
-                lhsT_scale=w_planes[:, 0:P],
-                rhs=w_words[0][:, 0 : 2 * R].bitcast(FP4X4),
-                rhs_scale=w_planes[:, 0:R],
-                start=(i == 0),
-                stop=(i == WARM_UPS - 1),
-            )
         deal_words()
         first_product(0)
         tanh_rows(0, 0)
@@ -348,13 +354,14 @@ def tile_list_msg_tanh_res_gateP_kernel(
         turn_tanh(2)
         for t in (2, 1, 3):
             pick_gates(t, keep.tile([P, J], F32, name=f"picked_gates{t}"))
+        clear_page(2, AT_PAGE2)
+        pages.append(pages[0])
         quantise_h(0, place_tile([P, HALF], U32, "h_codes0", AT_CODES0))
         pick_gates(0, keep.tile([P, J], F32, name="picked_gates0"), 2)
         first_product(3)
         tanh_rows(3, 0)
         scale_rows(2)
         tanh_rows(3, 1)
-        weave_h(2)
         for t in range(2):
             second_product(t, 0)
         y_rows[0, 0] = keep.tile([P, HALF], F32, name="y_row00", tag="y_row00", align_bytes=64)[:]
@@ -364,6 +371,7 @@ def tile_list_msg_tanh_res_gateP_kernel(
         copy_y(1, 0)
         place(1, 0, HALF)
         turn_tanh(3)
+        weave_h(2)
         for t in range(2, 4):
             second_product(t, 0)
         scale_rows(3)

@@ -37,18 +37,17 @@ GATES = 4 * T
 AT_PAGE1 = 0
 AT_WORDS_HALF = AT_PAGE1 + GATES - UNIT
 AT_WORDS10 = AT_WORDS_HALF + 4 * WORDS - UNIT
-AT_LAST_SCALES = AT_WORDS10 + UNIT
 AT_WORDS00 = AT_WORDS10 + WORDS - UNIT
 AT_GATES2 = AT_WORDS00 + WORDS - UNIT
 AT_PAGE2 = AT_GATES2
-AT_WORDS11 = AT_GATES2 + GATES
-AT_WORDS01 = AT_WORDS11 + WORDS - UNIT
-AT_GATES3 = AT_WORDS01 + WORDS
+AT_GATES3 = AT_GATES2 + GATES
 AT_CODES0 = AT_GATES3
-AT_TABLE_SCALES = AT_GATES3 + GATES - UNIT
-AT_DEALT = AT_TABLE_SCALES + UNIT
-AT_GATES1 = AT_TABLE_SCALES + T - UNIT
-AT_TABLE_WORDS = AT_GATES1 + GATES
+AT_WORDS11 = AT_GATES3 + GATES - UNIT
+AT_DEALT = AT_WORDS11 + WORDS
+AT_WORDS01 = AT_WORDS11 + WORDS - UNIT
+AT_GATES1 = AT_DEALT + 2 * N
+AT_TABLE_SCALES = AT_GATES1 + GATES - UNIT
+AT_TABLE_WORDS = AT_TABLE_SCALES + T
 AT_WGO = AT_TABLE_WORDS + GATES
 AT_STAGED = AT_WGO + 4 * J - UNIT
 AT_SM = AT_STAGED + UNIT
@@ -147,7 +146,7 @@ def tile_list_msg_tanh_res_gateP_kernel(
                 tab_planes[l, (j0 + c0) // P] = (picked_s[:, c0 : c0 + P], moved[:, c0 : c0 + P])
 
         pick_scales(0, 0, keep.tile([P, J], U8, name="scales0", align_bytes=64)[:])
-        pick_scales(1, 0, keep.tile([P, HALF], U8, name="scales1", align_bytes=64)[:])
+        pick_scales(1, 0, keep.tile([P, J], U8, name="scales1", align_bytes=64)[:])
 
         def pick_words(l, j0, picked):
             nc.vector.tensor_copy(picked, tab_w[:].bitcast(U32).indirect(offsets(l, j0, picked.shape[1])))
@@ -173,6 +172,7 @@ def tile_list_msg_tanh_res_gateP_kernel(
         nc.sync.dma_start(sm_rows[:], sm.rearrange("(p t) -> p t", t=4))
         wgo_rows = place_tile([P, J], F32, "wgo_rows", AT_WGO)
         nc.sync.dma_start(wgo_rows[:], wgo)
+        load_gates(1, AT_GATES1)
         for step in (pick_words, part_words):
             for l in range(2):
                 step(l, 0, picked[l, 0])
@@ -180,8 +180,6 @@ def tile_list_msg_tanh_res_gateP_kernel(
         for step in (pick_words, part_words):
             for l in range(2):
                 step(l, QUARTER, picked[l, 1])
-        pick_scales(1, HALF, place_tile([P, HALF], U8, "last_scales", AT_LAST_SCALES)[:])
-        load_gates(1, AT_GATES1)
         load_gates(3, AT_GATES3)
         dealt_s = place_tile([P, 2, N], U8, "dealt_s", AT_DEALT)
         for quad in range(4):
@@ -352,7 +350,7 @@ def tile_list_msg_tanh_res_gateP_kernel(
         weave_h(1)
         tanh_rows(2, 1)
         turn_tanh(2)
-        for t in (2, 1, 3):
+        for t in (1, 2, 3):
             pick_gates(t, keep.tile([P, J], F32, name=f"picked_gates{t}"))
         clear_page(2, AT_PAGE2)
         pages.append(pages[0])

@@ -73,9 +73,9 @@ def tile_list_msg_tanh_res_gateP_kernel(
         tab_s = place_tile([P, T], U8, "tab_s", AT_TABLE_SCALES)
         w_planes = keep.tile([P, 4 * R], U8, name="w_planes", align_bytes=64)[:]
 
-        nc.gpsimd.memset(tab_s[:].bitcast(I32), 0)
         wd_staged = keep.tile([P, 2 * N], U8, name="wd_staged", align_bytes=64)[:]
         nc.vector.memset(wd_staged.bitcast(I32), 0)
+        nc.vector.memset(tab_s[:].bitcast(I32), 0)
         ident = keep.tile([P, P], F32, name="ident")
         nc.vector.memset(ident[:], 0.0)
         make_identity(nc, ident[:], nomemset=True)

@@ -26,7 +26,6 @@ STORE_COLS = 512
 PIECE = 256
 DIRECT_PIECES = 1
 VECTOR_PIECES = 6
-WARM_UPS = 3
 A_BANKS = ((0, 1), (2, 3), (3, 4), (5, 3))
 TURN_BANKS = (0, 4, 0, 6)
 Y_BANKS = ((6, 7, 0, 1), (2, 3, 4, 5))
@@ -118,18 +117,6 @@ def tile_list_msg_tanh_res_gateP_kernel(
         nc.vector.tensor_copy(
             dealt_rows.rearrange("p (i t m) -> p i t m", i=2, t=4), wd_staged.rearrange("p (i m t) -> p i t m", i=2, t=4)
         )
-
-        warm_bank = psum.tile([P, R], F32, name="warm_bank", tag="bank7")
-        for i in range(WARM_UPS):
-            nc.tensor.matmul_mx(
-                warm_bank[:],
-                lhsT=tab_w[:].bitcast(U8)[:, 0 : 2 * P].bitcast(FP4X4),
-                lhsT_scale=tab_s[:, 0:P],
-                rhs=tab_w[:].bitcast(U8)[:, 0 : 2 * R].bitcast(FP4X4),
-                rhs_scale=tab_s[:, 0:R],
-                start=(i == 0),
-                stop=(i == WARM_UPS - 1),
-            )
 
         def offsets(l, j0, n):
             return lists[l][:, j0 // 16 : (j0 + n) // 16]

@@ -26,6 +26,7 @@ STORE_COLS = 512
 PIECE = 256
 DIRECT_PIECES = 1
 VECTOR_PIECES = 6
+
 A_BANKS = ((0, 1), (2, 3), (3, 4), (5, 3))
 TURN_BANKS = (0, 4, 0, 6)
 Y_BANKS = ((6, 7, 0, 1), (2, 3, 4, 5))
@@ -47,6 +48,9 @@ AT_WORDS01 = AT_WORDS11 + WORDS - UNIT
 AT_GATES1 = AT_DEALT + 2 * N
 AT_TABLE_SCALES = AT_GATES1 + GATES - UNIT
 AT_TABLE_WORDS = AT_TABLE_SCALES + T
+AT_GATES0 = AT_TABLE_WORDS
+AT_Y10 = AT_GATES0
+AT_WOVEN1 = AT_Y10 + 4 * HALF
 AT_WGO = AT_TABLE_WORDS + GATES
 AT_STAGED = AT_WGO + 4 * J - UNIT
 AT_SM = AT_STAGED + UNIT
@@ -115,25 +119,22 @@ def tile_list_msg_tanh_res_gateP_kernel(
 
         dealt_rows = keep.tile([P, 2 * N], U8, name="dealt_rows", align_bytes=64)[:]
         nc.vector.tensor_copy(
-            dealt_rows.rearrange("p (i t m) -> p i t m", i=2, t=4), wd_staged.rearrange("p (i m t) -> p i t m", i=2, t=4)
+            dealt_rows.rearrange("p (i t m) -> p i t m", i=2, t=4),
+            wd_staged.rearrange("p (i m t) -> p i t m", i=2, t=4),
         )
 
         def offsets(l, j0, n):
             return lists[l][:, j0 // 16 : (j0 + n) // 16]
 
-        tab_planes = {}
+        tab_planes = []
         parted = {}
 
-        def pick_scales(l, j0, picked_s):
-            n = picked_s.shape[1]
-            nc.vector.tensor_copy(picked_s, tab_s[:].indirect(offsets(l, j0, n)))
-            moved = keep.tile([P, n], U8, name=f"moved{l}_{j0}", align_bytes=64)[:]
+        for l in range(2):
+            picked_s = keep.tile([P, J], U8, name=f"scales{l}", align_bytes=64)[:]
+            nc.vector.tensor_copy(picked_s, tab_s[:].indirect(offsets(l, 0, J)))
+            moved = keep.tile([P, J], U8, name=f"moved{l}_0", align_bytes=64)[:]
             nc.sync.dma_start(moved.bitcast(I32)[0 : P - 16, :], picked_s.bitcast(I32)[16:P, :])
-            for c0 in range(0, n, P):
-                tab_planes[l, (j0 + c0) // P] = (picked_s[:, c0 : c0 + P], moved[:, c0 : c0 + P])
-
-        pick_scales(0, 0, keep.tile([P, J], U8, name="scales0", align_bytes=64)[:])
-        pick_scales(1, 0, keep.tile([P, J], U8, name="scales1", align_bytes=64)[:])
+            tab_planes.append((picked_s, moved))
 
         def pick_words(l, j0, picked):
             nc.vector.tensor_copy(picked, tab_w[:].bitcast(U32).indirect(offsets(l, j0, picked.shape[1])))
@@ -178,7 +179,7 @@ def tile_list_msg_tanh_res_gateP_kernel(
         for step in (pick_words, part_words):
             for l in range(2):
                 step(l, HALF, picked_half[:, l * HALF : (l + 1) * HALF])
-        load_gates(0, AT_TABLE_WORDS)
+        load_gates(0, AT_GATES0)
 
         def clear_page(t, at):
             pages.append(place_tile([P, T], F32, f"page{t}", at))
@@ -199,7 +200,7 @@ def tile_list_msg_tanh_res_gateP_kernel(
                     nc.tensor.matmul_mx(
                         a_banks[q, b][:],
                         lhsT=parted[l, q][a][:, 2 * b * P : 2 * (b + 1) * P].bitcast(FP4X4),
-                        lhsT_scale=tab_planes[l, 2 * q + b][a],
+                        lhsT_scale=tab_planes[l][a][:, (2 * q + b) * P : (2 * q + b + 1) * P],
                         rhs=w_words[l][:, 2 * a * R : 2 * (a + 1) * R].bitcast(FP4X4),
                         rhs_scale=w_planes[:, (2 * l + a) * R : (2 * l + a + 1) * R],
                         start=(i == 0),
@@ -227,7 +228,7 @@ def tile_list_msg_tanh_res_gateP_kernel(
             if q == 0:
                 h_woven[0] = keep.tile([P, 4 * HALF], BF16, name="h_woven0", align_bytes=64)
             if q == 2:
-                h_woven[1] = place_tile([P, 4 * HALF], BF16, "h_woven1", AT_TABLE_WORDS + 4 * HALF)
+                h_woven[1] = place_tile([P, 4 * HALF], BF16, "h_woven1", AT_WOVEN1)
             c0 = 4 * QUARTER * (q % 2)
             nc.scalar.copy(
                 h_woven[q // 2][:, c0 : c0 + 4 * QUARTER].rearrange("p (c i t) -> p c t i", i=4, t=4),
@@ -244,7 +245,8 @@ def tile_list_msg_tanh_res_gateP_kernel(
 
         def deal_words():
             nc.scalar.copy(
-                dealt4[:].bitcast(U16).rearrange("p (t m) -> p t m", t=4), wd4.bitcast(U16).rearrange("p (m t) -> p t m", t=4)
+                dealt4[:].bitcast(U16).rearrange("p (t m) -> p t m", t=4),
+                wd4.bitcast(U16).rearrange("p (m t) -> p t m", t=4),
             )
             nc.scalar.copy(
                 dealt8[:].rearrange("p (t m) -> p t m", t=4), wd8.bitcast(U32).rearrange("p (m t) -> p t m", t=4)
@@ -312,10 +314,9 @@ def tile_list_msg_tanh_res_gateP_kernel(
                 for c0 in range(early, T, PIECE):
                     nc.scalar.copy(rounded[:, 1, c0 : c0 + PIECE, 1], pages[t][:, c0 : c0 + PIECE])
 
-        def place(t, j0, n):
-            nc.vector.tensor_tensor(
-                pages[t][:].indirect(offsets(1, j0, n)), y_rows[t, j0 // HALF] if n == HALF else y_last[:], picked_gates[t][:, j0 : j0 + n], MULT
-            )
+        def place(t, j0, y):
+            n = y.shape[1]
+            nc.vector.tensor_tensor(pages[t][:].indirect(offsets(1, j0, n)), y, picked_gates[t][:, j0 : j0 + n], MULT)
             if j0 + n == J:
                 nc.sync.dma_start(out_rows[t], pages[t][:])
                 round_row(t)
@@ -337,6 +338,7 @@ def tile_list_msg_tanh_res_gateP_kernel(
         weave_h(1)
         tanh_rows(2, 1)
         turn_tanh(2)
+
         for t in (1, 2, 3):
             pick_gates(t, keep.tile([P, J], F32, name=f"picked_gates{t}"))
         clear_page(2, AT_PAGE2)
@@ -350,11 +352,11 @@ def tile_list_msg_tanh_res_gateP_kernel(
         for t in range(2):
             second_product(t, 0)
         y_rows[0, 0] = keep.tile([P, HALF], F32, name="y_row00", tag="y_row00", align_bytes=64)[:]
-        y_rows[1, 0] = place_tile([P, HALF], F32, "y_row10", AT_TABLE_WORDS)[:]
+        y_rows[1, 0] = place_tile([P, HALF], F32, "y_row10", AT_Y10)[:]
         copy_y(0, 0)
-        place(0, 0, HALF)
+        place(0, 0, y_rows[0, 0])
         copy_y(1, 0)
-        place(1, 0, HALF)
+        place(1, 0, y_rows[1, 0])
         turn_tanh(3)
         weave_h(2)
         for t in range(2, 4):
@@ -369,14 +371,14 @@ def tile_list_msg_tanh_res_gateP_kernel(
         for half in range(2):
             y_rows[3, half] = y_last[:, half * HALF : (half + 1) * HALF]
         copy_y(2, 0)
-        place(2, 0, HALF)
+        place(2, 0, y_rows[2, 0])
         copy_y(3, 0)
         for t in range(4):
             second_product(t, 1)
             copy_y(t, 1)
         for t in range(3):
-            place(t, HALF, HALF)
-        place(3, 0, J)
+            place(t, HALF, y_rows[t, 1])
+        place(3, 0, y_last[:])
 
         out_plane = keep.tile([P, STORE_COLS], U8, name="out_plane", align_bytes=64)
         out_words = out_1[0].rearrange("p t i -> p (t i)").bitcast(I32)
@@ -411,6 +413,6 @@ def tile_list_msg_tanh_res_gateP_kernel(
         quantise(n_pieces - 1)
         out_scales = out_2[0].bitcast(I32).rearrange("q (s c) -> s q c", s=4)
         for quad in range(4):
-            (nc.sync, nc.scalar)[quad % 2].dma_start(
+            nc.sync.dma_start(
                 out_scales[:, 4 * quad : 4 * quad + 4, :], out_plane[:].bitcast(I32)[32 * quad : 32 * quad + 16, :]
             )

from contextlib import ExitStack

import concourse.mybir as mybir
from concourse.masks import make_identity

K, R, N, T, J = 1024, 512, 512, 2048, 1024
FLOPS = 2 * (2 * K * R * J + 2 * R * N * J)

F32 = mybir.dt.float32
BF16 = mybir.dt.bfloat16
I32 = mybir.dt.int32
U32 = mybir.dt.uint32
U16 = mybir.dt.uint16
U8 = mybir.dt.uint8
FP8X4 = mybir.dt.float8_e4m3fn_x4
FP4X4 = mybir.dt.float4_e2m1fn_x4
COPY = mybir.ActivationFunctionType.Copy
TANH = mybir.ActivationFunctionType.Tanh
MULT = mybir.AluOpType.mult

P = 128
HALF = J // 2
QUARTER = J // 4
SCALE_ROWS = 16
STORE_COLS = 512
PIECE = 256
DIRECT_PIECES = 1
VECTOR_PIECES = 6

A_BANKS = ((0, 1), (2, 3), (3, 4), (5, 3))
TURN_BANKS = (0, 4, 0, 6)
Y_BANKS = ((6, 7, 0, 1), (2, 3, 4, 5))

UNIT = 64
WORDS = 4 * QUARTER
GATES = 4 * T
AT_PAGE1 = 0
AT_WORDS_HALF = AT_PAGE1 + GATES - UNIT
AT_WORDS10 = AT_WORDS_HALF + 4 * WORDS - UNIT
AT_WORDS00 = AT_WORDS10 + WORDS - UNIT
AT_GATES2 = AT_WORDS00 + WORDS - UNIT
AT_PAGE2 = AT_GATES2
AT_GATES3 = AT_GATES2 + GATES
AT_CODES0 = AT_GATES3
AT_WORDS11 = AT_GATES3 + GATES - UNIT
AT_DEALT = AT_WORDS11 + WORDS
AT_WORDS01 = AT_WORDS11 + WORDS - UNIT
AT_GATES1 = AT_DEALT + 2 * N
AT_TABLE_SCALES = AT_GATES1 + GATES - UNIT
AT_TABLE_WORDS = AT_TABLE_SCALES + T
AT_GATES0 = AT_TABLE_WORDS
AT_Y10 = AT_GATES0
AT_WOVEN1 = AT_Y10 + 4 * HALF
AT_WGO = AT_TABLE_WORDS + GATES
AT_STAGED = AT_WGO + 4 * J - UNIT
AT_SM = AT_STAGED + UNIT


def tile_list_msg_tanh_res_gateP_kernel(
    tc, tab_words, tab_scales, ws_words, ws_scales, wt_words, wt_scales, sm,
    wd4_words, wd4_scales, wd8_words, wd8_scales, gT, wgo, offs, offs2,
    out_0, out_1, out_2,
):
    nc = tc.nc
    with ExitStack() as ctx:
        keep = ctx.enter_context(tc.tile_pool(name="keep", bufs=1))
        placed = ctx.enter_context(tc.tile_pool(name="placed", bufs=1))
        ring = ctx.enter_context(tc.tile_pool(name="ring", bufs=4))
        psum = ctx.enter_context(tc.psum_pool(name="psum", bufs=1))

        def place_tile(shape, dtype, name, offset):
            return placed.tile(shape, dtype, name=name, offset=offset, align_bytes=UNIT)

        lists = [keep.tile([P, J // 16], U16, name=f"list{l}") for l in range(2)]
        tab_w = place_tile([P, T], I32, "tab_w", AT_TABLE_WORDS)
        tab_s = place_tile([P, T], U8, "tab_s", AT_TABLE_SCALES)
        w_planes = keep.tile([P, 4 * R], U8, name="w_planes", align_bytes=64)[:]

        wd_staged = keep.tile([P, 2 * N], U8, name="wd_staged", align_bytes=64)[:]
        nc.vector.memset(wd_staged.bitcast(I32), 0)
        nc.vector.memset(tab_s[:].bitcast(I32), 0)
        ident = keep.tile([P, P], F32, name="ident")
        nc.vector.memset(ident[:], 0.0)
        make_identity(nc, ident[:], nomemset=True)
        pages = [keep.tile([P, T], F32, name="page0")]
        nc.vector.memset(pages[0][:].bitcast(I32), 0)

        nc.sync.dma_start(lists[0][:], offs)
        for i, scales in enumerate((wd4_scales, wd8_scales)):
            nc.sync.dma_start(
                wd_staged.bitcast(I32)[0:SCALE_ROWS, i * N // 4 : (i + 1) * N // 4], scales[0].bitcast(I32)
            )
        tab_s_rows = tab_scales.bitcast(I32).rearrange("a (q r) t -> r q a t", r=4)
        for r in range(4):
            nc.sync.dma_start(tab_s[:].bitcast(I32)[r:P:16, :], tab_s_rows[r])
        nc.sync.dma_start(lists[1][:], offs2)
        w_staged = place_tile([SCALE_ROWS, 4 * R], U8, "w_staged", AT_STAGED)[:]
        w_words = [keep.tile([P, 4 * R], U8, name=f"w_words{l}", align_bytes=64) for l in range(2)]
        for l, scales in enumerate((ws_scales, wt_scales)):
            nc.sync.dma_start(
                w_staged.bitcast(I32)[:, l * R // 2 : (l + 1) * R // 2].rearrange("q (a n) -> q a n", a=2),
                scales.bitcast(I32).rearrange("a q n -> q a n"),
            )
        nc.sync.dma_start(tab_w[:], tab_words[0].rearrange("p t b -> p (t b)").bitcast(I32))
        for l, words in enumerate((ws_words, wt_words)):
            nc.sync.dma_start(
                w_words[l][:].bitcast(I32).rearrange("p (a n) -> p a n", a=2),
                words.bitcast(I32).rearrange("a p n -> p a n"),
            )
        wd = keep.tile([P, 6 * N], U8, name="wd", align_bytes=64)
        wd4, wd8 = wd[:, 0 : 2 * N], wd[:, 2 * N : 6 * N]
        nc.sync.dma_start(wd4.bitcast(I32), wd4_words[0].bitcast(I32))
        nc.sync.dma_start(wd8.bitcast(I32), wd8_words[0].rearrange("p n i -> p (n i)").bitcast(I32))
        for quad in range(4):
            nc.scalar.dma_start(
                w_planes.bitcast(I32)[32 * quad : 32 * quad + 4, :],
                w_staged.bitcast(I32)[4 * quad : 4 * quad + 4, :],
            )

        dealt_rows = keep.tile([P, 2 * N], U8, name="dealt_rows", align_bytes=64)[:]
        nc.vector.tensor_copy(
            dealt_rows.rearrange("p (i t m) -> p i t m", i=2, t=4),
            wd_staged.rearrange("p (i m t) -> p i t m", i=2, t=4),
        )

        def offsets(l, j0, n):
            return lists[l][:, j0 // 16 : (j0 + n) // 16]

        tab_planes = []
        parted = {}

        for l in range(2):
            picked_s = keep.tile([P, J], U8, name=f"scales{l}", align_bytes=64)[:]
            nc.vector.tensor_copy(picked_s, tab_s[:].indirect(offsets(l, 0, J)))
            moved = keep.tile([P, J], U8, name=f"moved{l}_0", align_bytes=64)[:]
            nc.sync.dma_start(moved.bitcast(I32)[0 : P - 16, :], picked_s.bitcast(I32)[16:P, :])
            tab_planes.append((picked_s, moved))

        def pick_words(l, j0, picked):
            nc.vector.tensor_copy(picked, tab_w[:].bitcast(U32).indirect(offsets(l, j0, picked.shape[1])))

        def part_words(l, j0, picked):
            n = picked.shape[1]
            words = keep.tile([P, 2, 2 * n], U8, name=f"parted{l}_{j0}", align_bytes=64)
            nc.vector.tensor_copy(words[:].bitcast(U16), picked.bitcast(U16).rearrange("p (j a) -> p a j", a=2))
            for c0 in range(0, n, QUARTER):
                parted[l, (j0 + c0) // QUARTER] = [words[:, a, 2 * c0 : 2 * (c0 + QUARTER)] for a in range(2)]

        starts = {(0, 0): AT_WORDS00, (1, 0): AT_WORDS01, (0, 1): AT_WORDS10, (1, 1): AT_WORDS11}
        picked = {key: place_tile([P, QUARTER], U32, f"picked{key[1]}_{key[0]}", at)[:] for key, at in starts.items()}

        gT_rows = gT.rearrange("(p t) c -> p t c", t=4)
        gates = {}

        def load_gates(t, at):
            gates[t] = place_tile([P, T], F32, f"gates{t}", at)
            nc.sync.dma_start(gates[t][:], gT_rows[:, t, :])

        sm_rows = place_tile([P, 4], F32, "sm_rows", AT_SM)
        nc.sync.dma_start(sm_rows[:], sm.rearrange("(p t) -> p t", t=4))
        wgo_rows = place_tile([P, J], F32, "wgo_rows", AT_WGO)
        nc.sync.dma_start(wgo_rows[:], wgo)
        load_gates(1, AT_GATES1)
        for step in (pick_words, part_words):
            for l in range(2):
                step(l, 0, picked[l, 0])
        load_gates(2, AT_GATES2)
        for step in (pick_words, part_words):
            for l in range(2):
                step(l, QUARTER, picked[l, 1])
        load_gates(3, AT_GATES3)
        dealt_s = place_tile([P, 2, N], U8, "dealt_s", AT_DEALT)
        for quad in range(4):
            nc.sync.dma_start(
                dealt_s[:].rearrange("p i n -> p (i n)").bitcast(I32)[32 * quad : 32 * quad + 4, :],
                dealt_rows.bitcast(I32)[4 * quad : 4 * quad + 4, :],
            )
        picked_half = place_tile([P, 2 * HALF], U32, "picked_half", AT_WORDS_HALF)
        for step in (pick_words, part_words):
            for l in range(2):
                step(l, HALF, picked_half[:, l * HALF : (l + 1) * HALF])
        load_gates(0, AT_GATES0)

        def clear_page(t, at):
            pages.append(place_tile([P, T], F32, f"page{t}", at))
            nc.gpsimd.memset(pages[t][:].bitcast(I32), 0)

        clear_page(1, AT_PAGE1)

        a_banks, tanh_a, tanh_banks, h_rows = {}, {}, {}, {}
        h_woven, h_codes, h_scales, y_banks, y_rows = {}, {}, {}, {}, {}

        def first_product(q):
            steps = [(l, a) for l in range(2) for a in range(2)]
            if q == 1:
                steps = steps[::-1]
            for b in range(2):
                a_banks[q, b] = psum.tile([P, R], F32, name="a_bank", tag=f"bank{A_BANKS[q][b]}")
                for i, (l, a) in enumerate(steps):
                    nc.tensor.matmul_mx(
                        a_banks[q, b][:],
                        lhsT=parted[l, q][a][:, 2 * b * P : 2 * (b + 1) * P].bitcast(FP4X4),
                        lhsT_scale=tab_planes[l][a][:, (2 * q + b) * P : (2 * q + b + 1) * P],
                        rhs=w_words[l][:, 2 * a * R : 2 * (a + 1) * R].bitcast(FP4X4),
                        rhs_scale=w_planes[:, (2 * l + a) * R : (2 * l + a + 1) * R],
                        start=(i == 0),
                        stop=(i == len(steps) - 1),
                    )

        def tanh_rows(q, b):
            tanh_a[q, b] = ring.tile([P, 4, P], F32, name="tanh_a")
            nc.scalar.activation(tanh_a[q, b][:], a_banks[q, b][:].rearrange("p (m t) -> p t m", t=4), TANH)

        def turn_tanh(q):
            for u in range(2):
                bank = psum.tile([P, 2, QUARTER], F32, name="tanh_bank", tag=f"bank{TURN_BANKS[q] + u}")
                for e in range(2):
                    tanh_banks[q, 2 * u + e] = bank[:, e, :]
                    for b in range(2):
                        nc.tensor.transpose(bank[:, e, b * P : (b + 1) * P], tanh_a[q, b][:, 2 * u + e, :], ident[:])

        def scale_rows(q):
            h_rows[q] = keep.tile([P, 4, QUARTER], BF16, name=f"h_rows{q}", tag=f"h_rows{q}", align_bytes=64)
            for t in range(4):
                nc.scalar.activation(h_rows[q][:, t, :], tanh_banks[q, t], COPY, scale=sm_rows[:, t : t + 1])

        def weave_h(q):
            if q == 0:
                h_woven[0] = keep.tile([P, 4 * HALF], BF16, name="h_woven0", align_bytes=64)
            if q == 2:
                h_woven[1] = place_tile([P, 4 * HALF], BF16, "h_woven1", AT_WOVEN1)
            c0 = 4 * QUARTER * (q % 2)
            nc.scalar.copy(
                h_woven[q // 2][:, c0 : c0 + 4 * QUARTER].rearrange("p (c i t) -> p c t i", i=4, t=4),
                h_rows[q][:].rearrange("p t (c i) -> p c t i", i=4),
            )

        def quantise_h(half, codes):
            h_codes[half] = codes
            h_scales[half] = keep.tile([P, HALF], U8, name=f"h_scales{half}", align_bytes=64)
            nc.vector.quantize_mx(codes[:].bitcast(FP8X4), h_scales[half][:], h_woven[half][:])

        dealt4 = keep.tile([P, 2 * N], U8, name="dealt4", align_bytes=64)
        dealt8 = keep.tile([P, N], U32, name="dealt8", align_bytes=64)

        def deal_words():
            nc.scalar.copy(
                dealt4[:].bitcast(U16).rearrange("p (t m) -> p t m", t=4),
                wd4.bitcast(U16).rearrange("p (m t) -> p t m", t=4),
            )
            nc.scalar.copy(
                dealt8[:].rearrange("p (t m) -> p t m", t=4), wd8.bitcast(U32).rearrange("p (m t) -> p t m", t=4)
            )

        def second_product(t, half):
            y_banks[t, half] = psum.tile([P, HALF], F32, name="y_bank", tag=f"bank{Y_BANKS[half][t]}")
            cols = slice(t * P, (t + 1) * P)
            nc.tensor.matmul_mx(
                y_banks[t, half][:],
                lhsT=dealt4[:, 2 * t * P : 2 * (t + 1) * P].bitcast(FP4X4),
                lhsT_scale=dealt_s[:, 0, cols],
                rhs=h_codes[half][:].bitcast(FP8X4),
                rhs_scale=h_scales[half][:],
                start=True,
                stop=False,
            )
            nc.tensor.matmul_mx(
                y_banks[t, half][:],
                lhsT=dealt8[:, cols].bitcast(FP8X4),
                lhsT_scale=dealt_s[:, 1, cols],
                rhs=h_codes[half][:].bitcast(FP8X4),
                rhs_scale=h_scales[half][:],
                start=False,
                stop=True,
            )

        def copy_y(t, half):
            nc.scalar.copy(y_rows[t, half], y_banks[t, half][:])

        picked_gates = {}

        def pick_gates(t, picked_t, parts=1):
            picked_gates[t] = picked_t
            n = J // parts
            for j0 in range(0, J, n):
                nc.vector.tensor_tensor(
                    picked_t[:, j0 : j0 + n], gates[t][:].indirect(offsets(0, j0, n)), wgo_rows[:, j0 : j0 + n], MULT
                )

        out_rows = out_0.rearrange("(p t) c -> t p c", t=4)
        n_pieces = T // PIECE
        rounded = keep.tile([P, 2, T, 2], BF16, name="rounded", align_bytes=64)
        woven = [keep.tile([P, 4 * PIECE], BF16, name=f"woven{c}", align_bytes=64) for c in range(n_pieces)]

        def weave(c):
            on_vector = DIRECT_PIECES <= c < VECTOR_PIECES
            copy, word = (nc.vector.tensor_copy, I32) if on_vector else (nc.scalar.copy, U32)
            copy(
                woven[c][:].bitcast(word).rearrange("p (j u) -> p j u", u=2),
                rounded[:].rearrange("p u j e -> p u (j e)").bitcast(word)[:, :, c * PIECE : (c + 1) * PIECE]
                .rearrange("p u j -> p j u"),
            )

        def round_row(t):
            early = DIRECT_PIECES * PIECE
            if t < 2:
                nc.scalar.copy(rounded[:, 0, :, t], pages[t][:])
            elif t == 2:
                nc.scalar.copy(rounded[:, 1, 0:early, :], pages[t][:, 0:early].unsqueeze(2).to_broadcast([P, early, 2]))
                nc.scalar.copy(rounded[:, 1, early:, 0], pages[t][:, early:])
                for c in range(DIRECT_PIECES):
                    weave(c)
            else:
                for c0 in range(early, T, PIECE):
                    nc.scalar.copy(rounded[:, 1, c0 : c0 + PIECE, 1], pages[t][:, c0 : c0 + PIECE])

        def place(t, j0, y):
            n = y.shape[1]
            nc.vector.tensor_tensor(pages[t][:].indirect(offsets(1, j0, n)), y, picked_gates[t][:, j0 : j0 + n], MULT)
            if j0 + n == J:
                nc.sync.dma_start(out_rows[t], pages[t][:])
                round_row(t)

        deal_words()
        first_product(0)
        tanh_rows(0, 0)
        tanh_rows(0, 1)
        turn_tanh(0)
        first_product(1)
        tanh_rows(1, 0)
        scale_rows(0)
        tanh_rows(1, 1)
        turn_tanh(1)
        weave_h(0)
        scale_rows(1)
        first_product(2)
        tanh_rows(2, 0)
        weave_h(1)
        tanh_rows(2, 1)
        turn_tanh(2)

        for t in (1, 2, 3):
            pick_gates(t, keep.tile([P, J], F32, name=f"picked_gates{t}"))
        clear_page(2, AT_PAGE2)
        pages.append(pages[0])
        quantise_h(0, place_tile([P, HALF], U32, "h_codes0", AT_CODES0))
        pick_gates(0, keep.tile([P, J], F32, name="picked_gates0"), 2)
        first_product(3)
        tanh_rows(3, 0)
        scale_rows(2)
        tanh_rows(3, 1)
        for t in range(2):
            second_product(t, 0)
        y_rows[0, 0] = keep.tile([P, HALF], F32, name="y_row00", tag="y_row00", align_bytes=64)[:]
        y_rows[1, 0] = place_tile([P, HALF], F32, "y_row10", AT_Y10)[:]
        copy_y(0, 0)
        place(0, 0, y_rows[0, 0])
        copy_y(1, 0)
        place(1, 0, y_rows[1, 0])
        turn_tanh(3)
        weave_h(2)
        for t in range(2, 4):
            second_product(t, 0)
        scale_rows(3)
        weave_h(3)
        quantise_h(1, keep.tile([P, HALF], U32, name="h_codes1", tag="y_row00", align_bytes=64))
        y_rows[2, 0] = keep.tile([P, HALF], F32, name="y_row20", tag="h_rows3", align_bytes=64)[:]
        for t in range(3):
            y_rows[t, 1] = keep.tile([P, HALF], F32, name=f"y_row{t}1")[:]
        y_last = keep.tile([P, J], F32, name="y_last")
        for half in range(2):
            y_rows[3, half] = y_last[:, half * HALF : (half + 1) * HALF]
        copy_y(2, 0)
        place(2, 0, y_rows[2, 0])
        copy_y(3, 0)
        for t in range(4):
            second_product(t, 1)
            copy_y(t, 1)
        for t in range(3):
            place(t, HALF, y_rows[t, 1])
        place(3, 0, y_last[:])

        out_plane = keep.tile([P, STORE_COLS], U8, name="out_plane", align_bytes=64)
        out_words = out_1[0].rearrange("p t i -> p (t i)").bitcast(I32)
        stores = ((0, 1), (2, 3), (4, 5), (6,), (7,))
        out_codes = {}
        for group in stores:
            codes = keep.tile([P, len(group) * PIECE], I32, name=f"out_codes{group[0]}", align_bytes=64)
            for i, c in enumerate(group):
                out_codes[c] = (codes, i, group)

        def finish(c):
            if c < DIRECT_PIECES:
                nc.vector.tensor_copy(
                    woven[c][:].rearrange("p (j t) -> p j t", t=4)[:, :, 3], pages[3][:, c * PIECE : (c + 1) * PIECE]
                )
            else:
                weave(c)

        def quantise(c):
            s, c0 = divmod(c * PIECE, STORE_COLS)
            codes, i, group = out_codes[c]
            nc.vector.quantize_mx(
                codes[:, i * PIECE : (i + 1) * PIECE].bitcast(FP8X4), out_plane[4 * s :, c0 : c0 + PIECE], woven[c][:]
            )
            if c == group[-1]:
                nc.sync.dma_start(out_words[:, group[0] * PIECE : (c + 1) * PIECE], codes[:])

        finish(0)
        for c in range(1, n_pieces):
            finish(c)
            quantise(c - 1)
        quantise(n_pieces - 1)
        out_scales = out_2[0].bitcast(I32).rearrange("q (s c) -> s q c", s=4)
        for quad in range(4):
            nc.sync.dma_start(
                out_scales[:, 4 * quad : 4 * quad + 4, :], out_plane[:].bitcast(I32)[32 * quad : 32 * quad + 16, :]
            )
